import numpy as np
import ml_dtypes


def mxq(x, axis, fmt="e4m3"):
    dtype, down = {"e4m3": (ml_dtypes.float8_e4m3fn, 7), "e5m2": (ml_dtypes.float8_e5m2, 14)}[fmt]
    v = np.moveaxis(np.asarray(x, np.float32).astype(ml_dtypes.bfloat16).astype(np.float64), axis, -1)
    blocks = v.reshape(v.shape[:-1] + (-1, 32))
    amax = np.abs(blocks).max(-1, keepdims=True)
    byte = np.maximum(np.where(amax > 0, np.frexp(amax)[1] - 1 + 127, 0) - down, 1)
    scale = np.exp2(byte - 127.0)
    codes = (blocks / scale).astype(np.float32).astype(dtype).astype(np.float64)
    return np.moveaxis((codes * scale).reshape(v.shape), -1, axis)


WIDE = False


def mx_kscale(k):
    if not WIDE:
        return np.ones(k)
    levels = np.array([10, -10, 5, -5, 0])
    if k % 512:
        return np.exp2(np.random.permutation(np.resize(levels, k // 32))).repeat(32)
    a = np.empty((k // 512, 16))
    for p in range(k // 512):
        a[p, :8] = np.random.permutation(np.resize(levels, 8))
        for g in range(8):
            far = levels[np.abs(levels - a[p, g]) >= 10]
            a[p, g + 8] = far[np.random.randint(len(far))]
    return np.exp2(a.ravel()).repeat(32)


def f64(x):
    return np.asarray(x).astype(np.float64)


def striped(idx):
    return np.tile(idx.reshape(-1, 16).T, (8, 1)).astype(np.uint16)


def unstriped(offs):
    return offs[:16].T.reshape(-1).astype(np.int64)


E2M1 = np.array([0.0, 0.5, 1.0, 1.5, 2.0, 3.0, 4.0, 6.0, -0.0, -0.5, -1.0, -1.5, -2.0, -3.0, -4.0, -6.0])


def pack_weight(w, fmt):
    k, n = w.shape
    w = f64(np.asarray(w, np.float32).astype(ml_dtypes.bfloat16)).reshape(k // 32, 32, n)
    amax = np.abs(w).max(1)
    if fmt == "e4m3":
        byte = np.frexp(amax)[1] - 1 + 127 - 7
    else:
        mant, ex = np.frexp(amax / 6.0)
        byte = np.where(mant > 0.5, ex, ex - 1) + 127
    byte = np.clip(np.where(amax > 0, byte, 1), 1, 254)
    scaled = (w * np.exp2(127.0 - byte)[:, None, :]).reshape(k, n).astype(np.float32)
    by_word = np.ascontiguousarray(scaled.reshape(k // 512, 128, 4, n).transpose(0, 1, 3, 2))
    if fmt == "e4m3":
        words = by_word.astype(ml_dtypes.float8_e4m3fn).view(np.uint8)
    else:
        c = by_word.astype(ml_dtypes.float4_e2m1fn).view(np.uint8) & 0xF
        words = (c[..., 0::2] | (c[..., 1::2] << 4)).reshape(k // 512, 128, 2 * n)
    return np.ascontiguousarray(words), np.ascontiguousarray(byte.astype(np.uint8).reshape(k // 512, 16, n))


def unpack_weight(words, scales, fmt):
    g, _, n = scales.shape
    words = np.ascontiguousarray(words).reshape(g, 128, n, -1)
    if fmt == "e4m3":
        vals = words.view(ml_dtypes.float8_e4m3fn).astype(np.float64)
    else:
        nib = np.empty((g, 128, n, 4), np.uint8)
        nib[..., 0::2] = words & 0xF
        nib[..., 1::2] = words >> 4
        vals = E2M1[nib]
    vals = vals * np.repeat(np.exp2(scales.astype(np.float64) - 127.0), 8, axis=1)[..., None]
    return vals.transpose(0, 1, 3, 2).reshape(g * 512, n)


def d_silu(v):
    s = 1.0 / (1.0 + np.exp(-np.maximum(v, -700.0)))
    return s * (1.0 + v * (1.0 - s))


K, T, E1, C1, E2, C2, H = 512, 768, 3, 256, 3, 256, 512
N = 512


def by_expert(wq, xq, E, C):
    return np.concatenate([wq[e].T @ xq[:, e * C:(e + 1) * C] for e in range(E)], axis=1)


def setup_inputs():
    n = np.random.standard_normal
    v = mx_kscale(N)
    u = mx_kscale(H)
    slots1, slots2 = np.random.permutation(T), np.random.permutation(T)
    dy = pack_weight(n((N, T)) * v[:, None], "e4m3")
    w2t = [pack_weight(m, "e2m1") for m in n((E2, N, H)) / np.sqrt(N) / v[None, :, None] * u]
    w1t = [pack_weight(m, "e4m3") for m in n((E1, H, K)) / np.sqrt(H) / u[None, :, None]]
    return {
        "dy_words": dy[0],
        "dy_scales": dy[1],
        "w2t_words": np.stack([m[0] for m in w2t]),
        "w2t_scales": np.stack([m[1] for m in w2t]),
        "w1t_words": np.stack([m[0] for m in w1t]),
        "w1t_scales": np.stack([m[1] for m in w1t]),
        "a": (n((H, T))).astype(np.float32),
        "gate1": (np.tile(np.random.uniform(0.2, 1.0, T), (128, 1))).astype(np.float32),
        "gate2": (np.tile(np.random.uniform(0.2, 1.0, T), (128, 1))).astype(np.float32),
        "offs": striped(slots1),
        "offs2": striped(slots2),
    }


def reference(dy_words, dy_scales, w2t_words, w2t_scales, w1t_words, w1t_scales, a, gate1, gate2, offs, offs2):
    w2t = np.stack([unpack_weight(w2t_words[e], w2t_scales[e], "e2m1") for e in range(E2)])
    w1t = np.stack([unpack_weight(w1t_words[e], w1t_scales[e], "e4m3") for e in range(E1)])
    idx, idx2 = unstriped(offs), unstriped(offs2)
    gq = unpack_weight(dy_words, dy_scales, "e4m3")[:, idx2]
    dc = np.zeros((H, T))
    dc[:, idx2] = f64(gate2[:1]) * by_expert(w2t, gq, E2, C2)
    da = f64(gate1[:1]) * dc[:, idx] * d_silu(f64(a))
    out = np.zeros((K, T))
    out[:, idx] = by_expert(w1t, mxq(da, 0, "e4m3"), E1, C1)
    return out

@@ -1,0 +1,204 @@
+from contextlib import ExitStack
+
+import concourse.mybir as mybir
+from concourse.masks import make_identity
+
+F32 = mybir.dt.float32
+BF16 = mybir.dt.bfloat16
+I32 = mybir.dt.int32
+U32 = mybir.dt.uint32
+U16 = mybir.dt.uint16
+U8 = mybir.dt.uint8
+FP8X4 = mybir.dt.float8_e4m3fn_x4
+FP4X4 = mybir.dt.float4_e2m1fn_x4
+ACT = mybir.ActivationFunctionType
+MULT = mybir.AluOpType.mult
+
+P = 128
+PACK = 4
+T = 768
+E = 3
+C = 256
+W = 512
+FLOPS = 2 * 2 * W * W * T
+
+
+def tile_moe_seb_silu_kernel(
+    tc, dy_words, dy_scales, w2t_words, w2t_scales, w1t_words, w1t_scales, a, gate1, gate2, offs, offs2, out
+):
+    nc = tc.nc
+    with ExitStack() as ctx:
+        keep = ctx.enter_context(tc.tile_pool(name="keep", bufs=1))
+        ring = ctx.enter_context(tc.tile_pool(name="ring", bufs=3))
+        psum2 = ctx.enter_context(tc.psum_pool(name="psum2", bufs=2))
+        psum4 = ctx.enter_context(tc.psum_pool(name="psum4", bufs=4))
+
+        list1 = keep.tile([P, T // 16], U16, name="list1")
+        list2 = keep.tile([P, T // 16], U16, name="list2")
+        dy_w = keep.tile([P, T], I32, name="dy_w", align_bytes=64)
+        dy_s = keep.tile([P, T], U8, name="dy_s", align_bytes=64)
+        w2_w = keep.tile([P, E, 2 * W], U8, name="w2_w", align_bytes=64)
+        w2_s = keep.tile([P, E, W], U8, name="w2_s", align_bytes=64)
+        w1_w = keep.tile([P, E, W], I32, name="w1_w", align_bytes=64)
+        w1_s = keep.tile([P, E, W], U8, name="w1_s", align_bytes=64)
+        a_sb = keep.tile([P, PACK, T], F32, name="a_sb")
+        g_sb = keep.tile([P, T], F32, name="g_sb")
+        q_rows = keep.tile([P, P], F32, name="q_rows")
+        q_cols = keep.tile([P, 8], F32, name="q_cols")
+        ident = keep.tile([P, P], F32, name="ident")
+
+        nc.vector.memset(dy_s[:].bitcast(I32), 0)
+        nc.vector.memset(w2_s[:].rearrange("p e w -> p (e w)").bitcast(I32), 0)
+        nc.vector.memset(w1_s[:].rearrange("p e w -> p (e w)").bitcast(I32), 0)
+        make_identity(nc, ident[:])
+
+        def load_planes(plane, scales):
+            for quad in range(4):
+                nc.sync.dma_start(
+                    plane[32 * quad : 32 * quad + 4].bitcast(I32),
+                    scales[:, 0, 4 * quad : 4 * quad + 4, :].rearrange("e r w -> r e w").bitcast(I32),
+                )
+
+        nc.sync.dma_start(list2[:], offs2)
+        nc.sync.dma_start(dy_w[:], dy_words[0].rearrange("p t d -> p (t d)").bitcast(I32))
+        for quad in range(4):
+            nc.sync.dma_start(
+                dy_s[32 * quad : 32 * quad + 4, :].bitcast(I32),
+                dy_scales[0, 4 * quad : 4 * quad + 4, :].bitcast(I32),
+            )
+        nc.sync.dma_start(q_rows[:], gate2.rearrange("p (c n) -> (p c) n", n=P)[0:P, :])
+        nc.sync.dma_start(w2_w[:].bitcast(I32), w2t_words[:, 0].rearrange("e p w -> p e w").bitcast(I32))
+        load_planes(w2_s, w2t_scales)
+        nc.sync.dma_start(a_sb[:], a.rearrange("(p j) w -> p j w", j=PACK))
+        nc.sync.dma_start(g_sb[:], gate1)
+        nc.sync.dma_start(list1[:], offs)
+        nc.sync.dma_start(w1_w[:], w1t_words[:, 0].rearrange("e p k d -> p e (k d)").bitcast(I32))
+        load_planes(w1_s, w1t_scales)
+
+        def part(lst, e0, e1):
+            return lst[:, e0 * C // 16 : e1 * C // 16]
+
+        q_ps = psum2.tile([P, W], F32, name="turned", tag="turned")
+        nc.tensor.transpose(q_ps[:, 0:P], q_rows[:], ident[:])
+        nc.scalar.copy(q_cols[:], q_ps[:, 0:8])
+
+        g_w = [keep.tile([P, C], U32, name=f"g_w{e}", align_bytes=64) for e in range(E)]
+        g_s = [keep.tile([P, C], U8, name=f"g_s{e}", align_bytes=64) for e in range(E)]
+        for e in range(E):
+            nc.vector.tensor_copy(g_w[e][:], dy_w[:].bitcast(U32).indirect(part(list2, e, e + 1)))
+            nc.vector.tensor_copy(g_s[e][:], dy_s[:].indirect(part(list2, e, e + 1)))
+
+        groups = [(0, 1), (1, 3)]
+        res = [keep.tile([P, PACK, C], F32, name=f"res{e}") for e in range(E)]
+        dc = [keep.tile([P, T], F32, name=f"dc{t}") for t in range(PACK)]
+        sig = [keep.tile([P, PACK, C], F32, name=f"sig{e}") for e in range(E)]
+        sig_g = [keep.tile([P, PACK, C], F32, name=f"sig_g{e}") for e in range(E)]
+        neg = [keep.tile([P, PACK, C], F32, name=f"neg{e}") for e in range(E)]
+        one_less = [keep.tile([P, PACK, C], F32, name=f"one_less{e}") for e in range(E)]
+        factor = [keep.tile([P, PACK, C], F32, name=f"factor{e}") for e in range(E)]
+
+        def chunk(c):
+            e, half = divmod(c, 2)
+            cols = slice(half * P, (half + 1) * P)
+            sums = psum2.tile([P, W], F32, name="sums", tag="sums")
+            nc.tensor.matmul_mx(
+                out=sums[:],
+                lhsT=g_w[e][:, cols].bitcast(FP8X4),
+                lhsT_scale=g_s[e][:, cols],
+                rhs=w2_w[:, e, :].bitcast(FP4X4),
+                rhs_scale=w2_s[:, e, :],
+                start=True,
+                stop=True,
+            )
+            gated = ring.tile([P, PACK, P], F32, name="gated", tag="gated")
+            nc.scalar.activation(
+                gated[:], sums[:].rearrange("s (p t) -> s t p", t=PACK), ACT.Copy, scale=q_cols[:, c : c + 1]
+            )
+            turned = psum2.tile([P, W], F32, name="turned", tag="turned")
+            for t in range(PACK):
+                nc.tensor.transpose(turned[:, t * P : (t + 1) * P], gated[:, t, :], ident[:])
+            nc.scalar.copy(res[e][:, :, cols], turned[:].rearrange("p (t s) -> p t s", t=PACK))
+
+        def scatter_dc(e):
+            for t in range(PACK):
+                nc.vector.tensor_copy(dc[t][:].indirect(part(list2, e, e + 1)), res[e][:, t, :])
+
+        def sigmoid_times_gate(e):
+            slots = slice(e * C, (e + 1) * C)
+            nc.scalar.activation(sig[e][:], a_sb[:, :, slots], ACT.Sigmoid)
+            nc.gpsimd.tensor_tensor(
+                sig_g[e][:], sig[e][:], g_sb[:, slots].unsqueeze(1).to_broadcast([P, PACK, C]), MULT
+            )
+
+        def finish_factor(e):
+            slots = slice(e * C, (e + 1) * C)
+            nc.scalar.activation(neg[e][:], a_sb[:, :, slots], ACT.Silu, scale=-1.0)
+            nc.scalar.activation(one_less[e][:], neg[e][:], ACT.Copy, scale=-1.0, bias=1.0)
+            nc.gpsimd.tensor_tensor(factor[e][:], sig_g[e][:], one_less[e][:], MULT)
+
+        chunk(0)
+        chunk(1)
+        scatter_dc(0)
+        sigmoid_times_gate(0)
+        chunk(2)
+        sigmoid_times_gate(1)
+        chunk(3)
+        scatter_dc(1)
+        sigmoid_times_gate(2)
+        chunk(4)
+        chunk(5)
+        scatter_dc(2)
+        for e in range(E):
+            finish_factor(e)
+
+        da = [keep.tile([P, PACK, C], F32, name=f"da{e}") for e in range(E)]
+        da_bf = [keep.tile([P, C, PACK], BF16, name=f"da_bf{e}", align_bytes=64) for e in range(E)]
+        da_w = [keep.tile([P, C], U32, name=f"da_w{e}", align_bytes=64) for e in range(E)]
+        da_s = [keep.tile([P, C], U8, name=f"da_s{e}", align_bytes=64) for e in range(E)]
+        dx = [keep.tile([P, PACK, (e1 - e0) * C], F32, name=f"dx{e0}") for e0, e1 in groups]
+        out_sb = [keep.tile([P, T], F32, name=f"out_sb{k}") for k in range(PACK)]
+
+        def gather(e):
+            for t in range(PACK):
+                nc.vector.tensor_tensor(da[e][:, t, :], dc[t][:].indirect(part(list1, e, e + 1)), factor[e][:, t, :], MULT)
+            nc.scalar.copy(
+                da_bf[e][:].rearrange("p (c i) t -> p c t i", i=4), da[e][:].rearrange("p t (c i) -> p c t i", i=4)
+            )
+
+        def multiply(e):
+            nc.vector.quantize_mx(
+                out=da_w[e][:].bitcast(FP8X4), scales=da_s[e][:], in_=da_bf[e][:].rearrange("p n t -> p (n t)")
+            )
+            gi = 0 if e == 0 else 1
+            c0 = (e - groups[gi][0]) * C
+            for pair in range(2):
+                bank = psum4.tile([P, 2, C], F32, name="bank", tag="bank")
+                for h in range(2):
+                    cols = slice((2 * pair + h) * P, (2 * pair + h + 1) * P)
+                    nc.tensor.matmul_mx(
+                        out=bank[:, h, :],
+                        lhsT=w1_w[:, e, cols].bitcast(FP8X4),
+                        lhsT_scale=w1_s[:, e, cols],
+                        rhs=da_w[e][:].bitcast(FP8X4),
+                        rhs_scale=da_s[e][:],
+                        start=True,
+                        stop=True,
+                    )
+                nc.scalar.copy(dx[gi][:, 2 * pair : 2 * pair + 2, c0 : c0 + C], bank[:])
+
+        def scatter(gi, k):
+            e0, e1 = groups[gi]
+            nc.vector.tensor_copy(out_sb[k][:].indirect(part(list1, e0, e1)), dx[gi][:, k, :])
+
+        gather(0)
+        gather(1)
+        multiply(0)
+        gather(2)
+        multiply(1)
+        scatter(0, 0)
+        multiply(2)
+        for k in range(1, PACK):
+            scatter(0, k)
+        for k in range(PACK):
+            scatter(1, k)
+            nc.sync.dma_start(out[k * P : (k + 1) * P, :], out_sb[k][:])

@@ -13,6 +13,7 @@ FP8X4 = mybir.dt.float8_e4m3fn_x4
 FP4X4 = mybir.dt.float4_e2m1fn_x4
 ACT = mybir.ActivationFunctionType
 MULT = mybir.AluOpType.mult
+ADD = mybir.AluOpType.add
 
 P = 128
 PACK = 4
@@ -39,10 +40,7 @@ def tile_moe_seb_silu_kernel(
         dy_s = keep.tile([P, T], U8, name="dy_s", align_bytes=64)
         w2_w = keep.tile([P, E, 2 * W], U8, name="w2_w", align_bytes=64)
         w2_s = keep.tile([P, E, W], U8, name="w2_s", align_bytes=64)
-        w1_w = keep.tile([P, E, W], I32, name="w1_w", align_bytes=64)
         w1_s = keep.tile([P, E, W], U8, name="w1_s", align_bytes=64)
-        a_sb = keep.tile([P, PACK, T], F32, name="a_sb")
-        g_sb = keep.tile([P, T], F32, name="g_sb")
         q_rows = keep.tile([P, P], F32, name="q_rows")
         q_cols = keep.tile([P, 8], F32, name="q_cols")
         ident = keep.tile([P, P], F32, name="ident")
@@ -50,30 +48,33 @@ def tile_moe_seb_silu_kernel(
         nc.vector.memset(dy_s[:].bitcast(I32), 0)
         nc.vector.memset(w2_s[:].rearrange("p e w -> p (e w)").bitcast(I32), 0)
         nc.vector.memset(w1_s[:].rearrange("p e w -> p (e w)").bitcast(I32), 0)
+        nc.gpsimd.dma_start(q_rows[:], gate2.rearrange("p (c n) -> (p c) n", n=P)[0:P, :])
         make_identity(nc, ident[:])
 
-        def load_planes(plane, scales):
+        warm = keep.tile([P, 1], F32, name="warm")
+        nc.scalar.activation(warm[:], ident[:, 0:1], ACT.Silu)
+
+        def load_planes(queue, plane, scales):
             for quad in range(4):
-                nc.sync.dma_start(
+                queue.dma_start(
                     plane[32 * quad : 32 * quad + 4].bitcast(I32),
                     scales[:, 0, 4 * quad : 4 * quad + 4, :].rearrange("e r w -> r e w").bitcast(I32),
                 )
 
         nc.sync.dma_start(list2[:], offs2)
         nc.sync.dma_start(dy_w[:], dy_words[0].rearrange("p t d -> p (t d)").bitcast(I32))
+        nc.sync.dma_start(w2_w[:].bitcast(I32), w2t_words[:, 0].rearrange("e p w -> p e w").bitcast(I32))
+        nc.sync.dma_start(list1[:], offs)
         for quad in range(4):
             nc.sync.dma_start(
                 dy_s[32 * quad : 32 * quad + 4, :].bitcast(I32),
                 dy_scales[0, 4 * quad : 4 * quad + 4, :].bitcast(I32),
             )
-        nc.sync.dma_start(q_rows[:], gate2.rearrange("p (c n) -> (p c) n", n=P)[0:P, :])
-        nc.sync.dma_start(w2_w[:].bitcast(I32), w2t_words[:, 0].rearrange("e p w -> p e w").bitcast(I32))
-        load_planes(w2_s, w2t_scales)
-        nc.sync.dma_start(a_sb[:], a.rearrange("(p j) w -> p j w", j=PACK))
-        nc.sync.dma_start(g_sb[:], gate1)
-        nc.sync.dma_start(list1[:], offs)
-        nc.sync.dma_start(w1_w[:], w1t_words[:, 0].rearrange("e p k d -> p e (k d)").bitcast(I32))
-        load_planes(w1_s, w1t_scales)
+        load_planes(nc.sync, w2_s, w2t_scales)
+        load_planes(nc.gpsimd, w1_s, w1t_scales)
+
+        def span(lst, c0, c1):
+            return lst[:, c0 * P // 16 : c1 * P // 16]
 
         def part(lst, e0, e1):
             return lst[:, e0 * C // 16 : e1 * C // 16]
@@ -82,93 +83,118 @@ def tile_moe_seb_silu_kernel(
         nc.tensor.transpose(q_ps[:, 0:P], q_rows[:], ident[:])
         nc.scalar.copy(q_cols[:], q_ps[:, 0:8])
 
-        g_w = [keep.tile([P, C], U32, name=f"g_w{e}", align_bytes=64) for e in range(E)]
-        g_s = [keep.tile([P, C], U8, name=f"g_s{e}", align_bytes=64) for e in range(E)]
-        for e in range(E):
-            nc.vector.tensor_copy(g_w[e][:], dy_w[:].bitcast(U32).indirect(part(list2, e, e + 1)))
-            nc.vector.tensor_copy(g_s[e][:], dy_s[:].indirect(part(list2, e, e + 1)))
+        saved = keep.tile([P, (PACK + 1) * T], F32, name="saved", tag="q_rows")
+        a_sb = [saved[:, e * PACK * C : (e + 1) * PACK * C].rearrange("p (j w) -> p j w", j=PACK) for e in range(E)]
+        g_sb = saved[:, PACK * T :]
+        a_hbm = a.rearrange("(p j) w -> p j w", j=PACK)
+        nc.sync.dma_start(a_sb[0], a_hbm[:, :, 0:C])
+        nc.sync.dma_start(g_sb, gate1)
+        for e in range(1, E):
+            nc.sync.dma_start(a_sb[e], a_hbm[:, :, e * C : (e + 1) * C])
+
+        runs = [(0, 1), (1, 3), (3, 6)]
+        g_w = [keep.tile([P, (c1 - c0) * P], U32, name=f"g_w{c0}", align_bytes=64) for c0, c1 in runs]
+        g_s = [keep.tile([P, (c1 - c0) * P], U8, name=f"g_s{c0}", align_bytes=64) for c0, c1 in runs]
+        for r, (c0, c1) in enumerate(runs):
+            nc.vector.tensor_copy(g_w[r][:], dy_w[:].bitcast(U32).indirect(span(list2, c0, c1)))
+            nc.vector.tensor_copy(g_s[r][:], dy_s[:].indirect(span(list2, c0, c1)))
 
         groups = [(0, 1), (1, 3)]
-        res = [keep.tile([P, PACK, C], F32, name=f"res{e}") for e in range(E)]
-        dc = [keep.tile([P, T], F32, name=f"dc{t}") for t in range(PACK)]
-        sig = [keep.tile([P, PACK, C], F32, name=f"sig{e}") for e in range(E)]
-        sig_g = [keep.tile([P, PACK, C], F32, name=f"sig_g{e}") for e in range(E)]
-        neg = [keep.tile([P, PACK, C], F32, name=f"neg{e}") for e in range(E)]
+        res = [keep.tile([P, PACK, (c1 - c0) * P], F32, name=f"res{c0}") for c0, c1 in runs]
+        dc = [keep.tile([P, T], F32, name=f"dc{t}", align_bytes=64) for t in range(PACK)]
+        heirs = {2: "neg", 4: "w1_w", 5: "sig"}
         one_less = [keep.tile([P, PACK, C], F32, name=f"one_less{e}") for e in range(E)]
-        factor = [keep.tile([P, PACK, C], F32, name=f"factor{e}") for e in range(E)]
+        times_g = [keep.tile([P, PACK, C], F32, name=f"times_g{e}") for e in range(E)]
+        factor = [
+            [keep.tile([P, 2, C], F32, name=f"factor{e}_{h}", align_bytes=64) for h in range(2)] for e in range(E)
+        ]
 
-        def chunk(c):
-            e, half = divmod(c, 2)
-            cols = slice(half * P, (half + 1) * P)
-            sums = psum2.tile([P, W], F32, name="sums", tag="sums")
-            nc.tensor.matmul_mx(
-                out=sums[:],
-                lhsT=g_w[e][:, cols].bitcast(FP8X4),
-                lhsT_scale=g_s[e][:, cols],
-                rhs=w2_w[:, e, :].bitcast(FP4X4),
-                rhs_scale=w2_s[:, e, :],
-                start=True,
-                stop=True,
-            )
-            gated = ring.tile([P, PACK, P], F32, name="gated", tag="gated")
-            nc.scalar.activation(
-                gated[:], sums[:].rearrange("s (p t) -> s t p", t=PACK), ACT.Copy, scale=q_cols[:, c : c + 1]
-            )
-            turned = psum2.tile([P, W], F32, name="turned", tag="turned")
+        def run(r):
+            c0, c1 = runs[r]
+            for c in range(c0, c1):
+                e = c * P // C
+                cols = slice((c - c0) * P, (c - c0 + 1) * P)
+                sums = psum2.tile([P, W], F32, name="sums", tag="sums")
+                nc.tensor.matmul_mx(
+                    out=sums[:],
+                    lhsT=g_w[r][:, cols].bitcast(FP8X4),
+                    lhsT_scale=g_s[r][:, cols],
+                    rhs=w2_w[:, e, :].bitcast(FP4X4),
+                    rhs_scale=w2_s[:, e, :],
+                    start=True,
+                    stop=True,
+                )
+                if c in heirs:
+                    gated = keep.tile([P, PACK, P], F32, name=f"gated{c}", tag=heirs[c], align_bytes=64)
+                else:
+                    gated = ring.tile([P, PACK, P], F32, name="gated", tag="gated")
+                nc.scalar.activation(
+                    gated[:], sums[:].rearrange("s (p t) -> s t p", t=PACK), ACT.Copy, scale=q_cols[:, c : c + 1]
+                )
+                turned = psum2.tile([P, W], F32, name="turned", tag="turned")
+                for t in range(PACK):
+                    nc.tensor.transpose(turned[:, t * P : (t + 1) * P], gated[:, t, :], ident[:])
+                nc.scalar.copy(res[r][:, :, cols], turned[:].rearrange("p (t s) -> p t s", t=PACK))
             for t in range(PACK):
-                nc.tensor.transpose(turned[:, t * P : (t + 1) * P], gated[:, t, :], ident[:])
-            nc.scalar.copy(res[e][:, :, cols], turned[:].rearrange("p (t s) -> p t s", t=PACK))
+                nc.vector.tensor_copy(dc[t][:].indirect(span(list2, c0, c1)), res[r][:, t, :])
 
-        def scatter_dc(e):
-            for t in range(PACK):
-                nc.vector.tensor_copy(dc[t][:].indirect(part(list2, e, e + 1)), res[e][:, t, :])
-
-        def sigmoid_times_gate(e):
+        def silu_part(e):
             slots = slice(e * C, (e + 1) * C)
-            nc.scalar.activation(sig[e][:], a_sb[:, :, slots], ACT.Sigmoid)
+            nc.scalar.activation(neg[:, e], a_sb[e], ACT.Silu, scale=-1.0)
+            nc.gpsimd.tensor_scalar(one_less[e][:], neg[:, e], -1.0, 1.0, MULT, ADD)
             nc.gpsimd.tensor_tensor(
-                sig_g[e][:], sig[e][:], g_sb[:, slots].unsqueeze(1).to_broadcast([P, PACK, C]), MULT
+                times_g[e][:], one_less[e][:], g_sb[:, slots].unsqueeze(1).to_broadcast([P, PACK, C]), MULT
             )
 
-        def finish_factor(e):
-            slots = slice(e * C, (e + 1) * C)
-            nc.scalar.activation(neg[e][:], a_sb[:, :, slots], ACT.Silu, scale=-1.0)
-            nc.scalar.activation(one_less[e][:], neg[e][:], ACT.Copy, scale=-1.0, bias=1.0)
-            nc.gpsimd.tensor_tensor(factor[e][:], sig_g[e][:], one_less[e][:], MULT)
+        def sigmoid_part(e):
+            nc.scalar.activation(sig[:, e], a_sb[e], ACT.Sigmoid)
+            for h in range(2):
+                nc.gpsimd.tensor_tensor(
+                    factor[e][h][:], times_g[e][:, 2 * h : 2 * h + 2, :], sig[:, e, 2 * h : 2 * h + 2, :], MULT
+                )
 
-        chunk(0)
-        chunk(1)
-        scatter_dc(0)
-        sigmoid_times_gate(0)
-        chunk(2)
-        sigmoid_times_gate(1)
-        chunk(3)
-        scatter_dc(1)
-        sigmoid_times_gate(2)
-        chunk(4)
-        chunk(5)
-        scatter_dc(2)
+        run(0)
+        run(1)
+        neg = keep.tile([P, E, PACK, C], F32, name="neg", tag="neg", align_bytes=64)
         for e in range(E):
-            finish_factor(e)
+            silu_part(e)
+        run(2)
+        w1_w = keep.tile([P, E, W], I32, name="w1_w", tag="w1_w", align_bytes=64)
+        nc.sync.dma_start(w1_w[:], w1t_words[:, 0].rearrange("e p k d -> p e (k d)").bitcast(I32))
+        sig = keep.tile([P, E, PACK, C], F32, name="sig", tag="sig", align_bytes=64)
+        for e in range(E):
+            sigmoid_part(e)
 
         da = [keep.tile([P, PACK, C], F32, name=f"da{e}") for e in range(E)]
-        da_bf = [keep.tile([P, C, PACK], BF16, name=f"da_bf{e}", align_bytes=64) for e in range(E)]
-        da_w = [keep.tile([P, C], U32, name=f"da_w{e}", align_bytes=64) for e in range(E)]
-        da_s = [keep.tile([P, C], U8, name=f"da_s{e}", align_bytes=64) for e in range(E)]
         dx = [keep.tile([P, PACK, (e1 - e0) * C], F32, name=f"dx{e0}") for e0, e1 in groups]
-        out_sb = [keep.tile([P, T], F32, name=f"out_sb{k}") for k in range(PACK)]
+        da_s = [keep.tile([P, C], U8, name=f"da_s{e}", align_bytes=64) for e in range(E)]
+        da_bf = {}
+        da_w = {}
+        out_sb = {}
 
         def gather(e):
             for t in range(PACK):
-                nc.vector.tensor_tensor(da[e][:, t, :], dc[t][:].indirect(part(list1, e, e + 1)), factor[e][:, t, :], MULT)
-            nc.scalar.copy(
-                da_bf[e][:].rearrange("p (c i) t -> p c t i", i=4), da[e][:].rearrange("p t (c i) -> p c t i", i=4)
-            )
+                nc.vector.tensor_tensor(
+                    da[e][:, t, :], dc[t][:].indirect(part(list1, e, e + 1)), factor[e][t // 2][:, t % 2, :], MULT
+                )
+            for lo, hi in pieces[e]:
+                da_bf[e, lo] = keep.tile([P, hi - lo, PACK], BF16, name=f"da_bf{e}_{lo}", align_bytes=64)
+                nc.scalar.copy(
+                    da_bf[e, lo][:].rearrange("p (c i) t -> p c t i", i=4),
+                    da[e][:, :, lo:hi].rearrange("p t (c i) -> p c t i", i=4),
+                )
+
+        pieces = [[(0, C)], [(0, C)], [(0, P), (P, C)]]
 
         def multiply(e):
-            nc.vector.quantize_mx(
-                out=da_w[e][:].bitcast(FP8X4), scales=da_s[e][:], in_=da_bf[e][:].rearrange("p n t -> p (n t)")
-            )
+            tag = f"factor{e + 1}_0" if e + 1 < E else f"da_w{e}"
+            da_w[e] = keep.tile([P, C], U32, name=f"da_w{e}", tag=tag, align_bytes=64)
+            for lo, hi in pieces[e]:
+                nc.vector.quantize_mx(
+                    out=da_w[e][:, lo:hi].bitcast(FP8X4),
+                    scales=da_s[e][:, lo:hi],
+                    in_=da_bf[e, lo][:].rearrange("p n t -> p (n t)"),
+                )
             gi = 0 if e == 0 else 1
             c0 = (e - groups[gi][0]) * C
             for pair in range(2):
@@ -186,8 +212,12 @@ def tile_moe_seb_silu_kernel(
                     )
                 nc.scalar.copy(dx[gi][:, 2 * pair : 2 * pair + 2, c0 : c0 + C], bank[:])
 
+        out_tags = ["dc0", "dc1", f"da_bf{E - 1}_0", f"da_bf{E - 1}_{P}"]
+
         def scatter(gi, k):
             e0, e1 = groups[gi]
+            if gi == 0:
+                out_sb[k] = keep.tile([P, T], F32, name=f"out_sb{k}", tag=out_tags[k], align_bytes=64)
             nc.vector.tensor_copy(out_sb[k][:].indirect(part(list1, e0, e1)), dx[gi][:, k, :])
 
         gather(0)

@@ -48,9 +48,10 @@ def tile_moe_seb_silu_kernel(
         nc.vector.memset(dy_s[:].bitcast(I32), 0)
         nc.vector.memset(w2_s[:].rearrange("p e w -> p (e w)").bitcast(I32), 0)
         nc.vector.memset(w1_s[:].rearrange("p e w -> p (e w)").bitcast(I32), 0)
-        nc.gpsimd.dma_start(q_rows[:], gate2.rearrange("p (c n) -> (p c) n", n=P)[0:P, :])
+        a_hbm = a.rearrange("(p j) w -> p j w", j=PACK)
+        a_first = keep.tile([P, PACK, C], F32, name="a_first")
         make_identity(nc, ident[:])
-
+        nc.gpsimd.dma_start(a_first[:], a_hbm[:, :, 0:C])
         warm = keep.tile([P, 1], F32, name="warm")
         nc.scalar.activation(warm[:], ident[:, 0:1], ACT.Silu)
 
@@ -70,6 +71,7 @@ def tile_moe_seb_silu_kernel(
                 dy_s[32 * quad : 32 * quad + 4, :].bitcast(I32),
                 dy_scales[0, 4 * quad : 4 * quad + 4, :].bitcast(I32),
             )
+        nc.sync.dma_start(q_rows[:], gate2.rearrange("p (c n) -> (p c) n", n=P)[0:P, :])
         load_planes(nc.sync, w2_s, w2t_scales)
         load_planes(nc.gpsimd, w1_s, w1t_scales)
 
@@ -83,11 +85,11 @@ def tile_moe_seb_silu_kernel(
         nc.tensor.transpose(q_ps[:, 0:P], q_rows[:], ident[:])
         nc.scalar.copy(q_cols[:], q_ps[:, 0:8])
 
-        saved = keep.tile([P, (PACK + 1) * T], F32, name="saved", tag="q_rows")
-        a_sb = [saved[:, e * PACK * C : (e + 1) * PACK * C].rearrange("p (j w) -> p j w", j=PACK) for e in range(E)]
-        g_sb = saved[:, PACK * T :]
-        a_hbm = a.rearrange("(p j) w -> p j w", j=PACK)
-        nc.sync.dma_start(a_sb[0], a_hbm[:, :, 0:C])
+        saved = keep.tile([P, T + (E - 1) * PACK * C], F32, name="saved", tag="q_rows")
+        g_sb = saved[:, 0:T]
+        a_sb = [a_first[:]] + [
+            saved[:, T + (e - 1) * PACK * C : T + e * PACK * C].rearrange("p (j w) -> p j w", j=PACK) for e in range(1, E)
+        ]
         nc.sync.dma_start(g_sb, gate1)
         for e in range(1, E):
             nc.sync.dma_start(a_sb[e], a_hbm[:, :, e * C : (e + 1) * C])
@@ -138,10 +140,10 @@ def tile_moe_seb_silu_kernel(
             for t in range(PACK):
                 nc.vector.tensor_copy(dc[t][:].indirect(span(list2, c0, c1)), res[r][:, t, :])
 
-        def silu_part(e):
+        def silu_part(e, neg):
             slots = slice(e * C, (e + 1) * C)
-            nc.scalar.activation(neg[:, e], a_sb[e], ACT.Silu, scale=-1.0)
-            nc.gpsimd.tensor_scalar(one_less[e][:], neg[:, e], -1.0, 1.0, MULT, ADD)
+            nc.scalar.activation(neg, a_sb[e], ACT.Silu, scale=-1.0)
+            nc.gpsimd.tensor_scalar(one_less[e][:], neg, -1.0, 1.0, MULT, ADD)
             nc.gpsimd.tensor_tensor(
                 times_g[e][:], one_less[e][:], g_sb[:, slots].unsqueeze(1).to_broadcast([P, PACK, C]), MULT
             )
@@ -153,11 +155,13 @@ def tile_moe_seb_silu_kernel(
                     factor[e][h][:], times_g[e][:, 2 * h : 2 * h + 2, :], sig[:, e, 2 * h : 2 * h + 2, :], MULT
                 )
 
+        neg_first = keep.tile([P, PACK, C], F32, name="neg_first")
+        silu_part(0, neg_first[:])
         run(0)
         run(1)
-        neg = keep.tile([P, E, PACK, C], F32, name="neg", tag="neg", align_bytes=64)
-        for e in range(E):
-            silu_part(e)
+        neg_rest = keep.tile([P, E - 1, PACK, C], F32, name="neg_rest", tag="neg", align_bytes=64)
+        for e in range(1, E):
+            silu_part(e, neg_rest[:, e - 1])
         run(2)
         w1_w = keep.tile([P, E, W], I32, name="w1_w", tag="w1_w", align_bytes=64)
         nc.sync.dma_start(w1_w[:], w1t_words[:, 0].rearrange("e p k d -> p e (k d)").bitcast(I32))

@@ -38,42 +38,57 @@ def tile_moe_seb_silu_kernel(
         list2 = keep.tile([P, T // 16], U16, name="list2")
         dy_w = keep.tile([P, T], I32, name="dy_w", align_bytes=64)
         dy_s = keep.tile([P, T], U8, name="dy_s", align_bytes=64)
-        w2_w = keep.tile([P, E, 2 * W], U8, name="w2_w", align_bytes=64)
+        w2_first = keep.tile([P, 2 * W], U8, name="w2_first", align_bytes=64)
         w2_s = keep.tile([P, E, W], U8, name="w2_s", align_bytes=64)
-        w1_s = keep.tile([P, E, W], U8, name="w1_s", align_bytes=64)
-        q_rows = keep.tile([P, P], F32, name="q_rows")
-        q_cols = keep.tile([P, 8], F32, name="q_cols")
+        q_rows = keep.tile([P, P], F32, name="q_rows", tag="q_rows", align_bytes=64)
+        q_cols = keep.tile([P, T // P], F32, name="q_cols")
         ident = keep.tile([P, P], F32, name="ident")
 
         nc.vector.memset(dy_s[:].bitcast(I32), 0)
         nc.vector.memset(w2_s[:].rearrange("p e w -> p (e w)").bitcast(I32), 0)
-        nc.vector.memset(w1_s[:].rearrange("p e w -> p (e w)").bitcast(I32), 0)
-        a_hbm = a.rearrange("(p j) w -> p j w", j=PACK)
-        a_first = keep.tile([P, PACK, C], F32, name="a_first")
         make_identity(nc, ident[:])
-        nc.gpsimd.dma_start(a_first[:], a_hbm[:, :, 0:C])
-        warm = keep.tile([P, 1], F32, name="warm")
+        nc.gpsimd.memset(q_rows[:], 0.0)
+        nc.gpsimd.dma_start(q_rows[0 : T // P, :], gate2[0].rearrange("(c n) -> c n", n=P))
+        a_hbm = a.rearrange("(p j) w -> p j w", j=PACK)
+        warm = keep.tile([P, 1], F32, name="warm", tag="warm")
         nc.scalar.activation(warm[:], ident[:, 0:1], ACT.Silu)
 
-        def load_planes(queue, plane, scales):
+        def load_planes(plane, scales):
             for quad in range(4):
-                queue.dma_start(
+                nc.sync.dma_start(
                     plane[32 * quad : 32 * quad + 4].bitcast(I32),
                     scales[:, 0, 4 * quad : 4 * quad + 4, :].rearrange("e r w -> r e w").bitcast(I32),
                 )
 
         nc.sync.dma_start(list2[:], offs2)
-        nc.sync.dma_start(dy_w[:], dy_words[0].rearrange("p t d -> p (t d)").bitcast(I32))
-        nc.sync.dma_start(w2_w[:].bitcast(I32), w2t_words[:, 0].rearrange("e p w -> p e w").bitcast(I32))
         nc.sync.dma_start(list1[:], offs)
+        nc.sync.dma_start(w2_first[:].bitcast(I32), w2t_words[0, 0].bitcast(I32))
+        nc.sync.dma_start(dy_w[:], dy_words[0].rearrange("p t d -> p (t d)").bitcast(I32))
         for quad in range(4):
             nc.sync.dma_start(
                 dy_s[32 * quad : 32 * quad + 4, :].bitcast(I32),
                 dy_scales[0, 4 * quad : 4 * quad + 4, :].bitcast(I32),
             )
-        nc.sync.dma_start(q_rows[:], gate2.rearrange("p (c n) -> (p c) n", n=P)[0:P, :])
-        load_planes(nc.sync, w2_s, w2t_scales)
-        load_planes(nc.gpsimd, w1_s, w1t_scales)
+        load_planes(w2_s, w2t_scales)
+
+        a_parts = [(0, 0, 2), (0, 2, 4), (1, 0, 4), (2, 0, 4)]
+        saved = keep.tile([P, T + E * PACK * C], F32, name="saved", tag="warm")
+        g_sb = [saved[:, e * C : (e + 1) * C] for e in range(E)]
+        a_sb = [
+            saved[:, T + (e * PACK + t0) * C : T + (e * PACK + t1) * C].rearrange("p (j w) -> p j w", w=C)
+            for e, t0, t1 in a_parts
+        ]
+
+        def load_a(n):
+            e, t0, t1 = a_parts[n]
+            nc.sync.dma_start(a_sb[n], a_hbm[:, t0:t1, e * C : (e + 1) * C])
+
+        load_a(0)
+        nc.sync.dma_start(g_sb[0], gate1[:, 0:C])
+        load_a(1)
+        load_a(2)
+        nc.sync.dma_start(saved[:, C:T], gate1[:, C:T])
+        load_a(3)
 
         def span(lst, c0, c1):
             return lst[:, c0 * P // 16 : c1 * P // 16]
@@ -83,91 +98,125 @@ def tile_moe_seb_silu_kernel(
 
         q_ps = psum2.tile([P, W], F32, name="turned", tag="turned")
         nc.tensor.transpose(q_ps[:, 0:P], q_rows[:], ident[:])
-        nc.scalar.copy(q_cols[:], q_ps[:, 0:8])
+        nc.scalar.copy(q_cols[:], q_ps[:, 0 : T // P])
 
-        saved = keep.tile([P, T + (E - 1) * PACK * C], F32, name="saved", tag="q_rows")
-        g_sb = saved[:, 0:T]
-        a_sb = [a_first[:]] + [
-            saved[:, T + (e - 1) * PACK * C : T + e * PACK * C].rearrange("p (j w) -> p j w", j=PACK) for e in range(1, E)
-        ]
-        nc.sync.dma_start(g_sb, gate1)
-        for e in range(1, E):
-            nc.sync.dma_start(a_sb[e], a_hbm[:, :, e * C : (e + 1) * C])
+        w2_rest = keep.tile([P, E - 1, 2 * W], U8, name="w2_rest", tag="q_rows", align_bytes=64)
+        nc.sync.dma_start(w2_rest[:].bitcast(I32), w2t_words[1:E, 0].rearrange("e p w -> p e w").bitcast(I32))
+        w2_w = [w2_first[:]] + [w2_rest[:, e - 1, :] for e in range(1, E)]
 
         runs = [(0, 1), (1, 3), (3, 6)]
-        g_w = [keep.tile([P, (c1 - c0) * P], U32, name=f"g_w{c0}", align_bytes=64) for c0, c1 in runs]
-        g_s = [keep.tile([P, (c1 - c0) * P], U8, name=f"g_s{c0}", align_bytes=64) for c0, c1 in runs]
-        for r, (c0, c1) in enumerate(runs):
+        g_w = {}
+        g_s = {}
+
+        def gather_words(r, tag):
+            c0, c1 = runs[r]
+            g_w[r] = keep.tile([P, (c1 - c0) * P], U32, name=f"g_w{c0}", tag=tag, align_bytes=64)
             nc.vector.tensor_copy(g_w[r][:], dy_w[:].bitcast(U32).indirect(span(list2, c0, c1)))
+
+        def gather_scales(r):
+            c0, c1 = runs[r]
+            g_s[r] = keep.tile([P, (c1 - c0) * P], U8, name=f"g_s{c0}", align_bytes=64)
             nc.vector.tensor_copy(g_s[r][:], dy_s[:].indirect(span(list2, c0, c1)))
 
+        gather_words(0, "g_w_first")
+        gather_scales(0)
+        gather_words(1, "g_w_second")
+        gather_scales(1)
+
         groups = [(0, 1), (1, 3)]
-        res = [keep.tile([P, PACK, (c1 - c0) * P], F32, name=f"res{c0}") for c0, c1 in runs]
+        spreads = [(0, 1), (1, 2), (2, 4), (4, 6)]
+        res = [keep.tile([P, PACK, (c1 - c0) * P], F32, name=f"res{c0}") for c0, c1 in spreads]
         dc = [keep.tile([P, T], F32, name=f"dc{t}", align_bytes=64) for t in range(PACK)]
-        heirs = {2: "neg", 4: "w1_w", 5: "sig"}
-        one_less = [keep.tile([P, PACK, C], F32, name=f"one_less{e}") for e in range(E)]
+        heirs = {1: "w1_s", 2: "w1_w", 3: "sig"}
+        neg = [keep.tile([P, t1 - t0, C], F32, name=f"neg{e}_{t0}") for e, t0, t1 in a_parts]
+        one_less = [keep.tile([P, t1 - t0, C], F32, name=f"one_less{e}_{t0}") for e, t0, t1 in a_parts]
         times_g = [keep.tile([P, PACK, C], F32, name=f"times_g{e}") for e in range(E)]
         factor = [
             [keep.tile([P, 2, C], F32, name=f"factor{e}_{h}", align_bytes=64) for h in range(2)] for e in range(E)
         ]
 
-        def run(r):
-            c0, c1 = runs[r]
-            for c in range(c0, c1):
-                e = c * P // C
-                cols = slice((c - c0) * P, (c - c0 + 1) * P)
-                sums = psum2.tile([P, W], F32, name="sums", tag="sums")
-                nc.tensor.matmul_mx(
-                    out=sums[:],
-                    lhsT=g_w[r][:, cols].bitcast(FP8X4),
-                    lhsT_scale=g_s[r][:, cols],
-                    rhs=w2_w[:, e, :].bitcast(FP4X4),
-                    rhs_scale=w2_s[:, e, :],
-                    start=True,
-                    stop=True,
-                )
-                if c in heirs:
-                    gated = keep.tile([P, PACK, P], F32, name=f"gated{c}", tag=heirs[c], align_bytes=64)
-                else:
-                    gated = ring.tile([P, PACK, P], F32, name="gated", tag="gated")
-                nc.scalar.activation(
-                    gated[:], sums[:].rearrange("s (p t) -> s t p", t=PACK), ACT.Copy, scale=q_cols[:, c : c + 1]
-                )
-                turned = psum2.tile([P, W], F32, name="turned", tag="turned")
+        def product(c):
+            e = c * P // C
+            r = [n for n, (c0, c1) in enumerate(runs) if c0 <= c < c1][0]
+            s = [n for n, (c0, c1) in enumerate(spreads) if c0 <= c < c1][0]
+            cols = slice((c - runs[r][0]) * P, (c - runs[r][0] + 1) * P)
+            place = slice((c - spreads[s][0]) * P, (c - spreads[s][0] + 1) * P)
+            sums = psum2.tile([P, W], F32, name="sums", tag="sums")
+            nc.tensor.matmul_mx(
+                out=sums[:],
+                lhsT=g_w[r][:, cols].bitcast(FP8X4),
+                lhsT_scale=g_s[r][:, cols],
+                rhs=w2_w[e].bitcast(FP4X4),
+                rhs_scale=w2_s[:, e, :],
+                start=True,
+                stop=True,
+            )
+            if c in heirs:
+                gated = keep.tile([P, PACK, P], F32, name=f"gated{c}", tag=heirs[c], align_bytes=64)
+            else:
+                gated = ring.tile([P, PACK, P], F32, name="gated", tag="gated")
+            if c == 0:
+                by_plane = sums[:].rearrange("s (p t) -> s t p", t=PACK)
                 for t in range(PACK):
-                    nc.tensor.transpose(turned[:, t * P : (t + 1) * P], gated[:, t, :], ident[:])
-                nc.scalar.copy(res[r][:, :, cols], turned[:].rearrange("p (t s) -> p t s", t=PACK))
+                    nc.scalar.activation(gated[:, t, :], by_plane[:, t, :], ACT.Copy, scale=q_cols[:, c : c + 1])
+                    bank = psum4.tile([P, 2, C], F32, name="bank", tag="bank")
+                    nc.tensor.transpose(bank[:, 0, 0:P], gated[:, t, :], ident[:])
+                    nc.scalar.copy(res[s][:, t, place], bank[:, 0, 0:P])
+                return
+            nc.scalar.activation(
+                gated[:], sums[:].rearrange("s (p t) -> s t p", t=PACK), ACT.Copy, scale=q_cols[:, c : c + 1]
+            )
+            turned = psum2.tile([P, W], F32, name="turned", tag="turned")
             for t in range(PACK):
-                nc.vector.tensor_copy(dc[t][:].indirect(span(list2, c0, c1)), res[r][:, t, :])
+                nc.tensor.transpose(turned[:, t * P : (t + 1) * P], gated[:, t, :], ident[:])
+            nc.scalar.copy(res[s][:, :, place], turned[:].rearrange("p (t s) -> p t s", t=PACK))
 
-        def silu_part(e, neg):
-            slots = slice(e * C, (e + 1) * C)
-            nc.scalar.activation(neg, a_sb[e], ACT.Silu, scale=-1.0)
-            nc.gpsimd.tensor_scalar(one_less[e][:], neg, -1.0, 1.0, MULT, ADD)
+        def spread(s):
+            c0, c1 = spreads[s]
+            for t in range(PACK):
+                nc.vector.tensor_copy(dc[t][:].indirect(span(list2, c0, c1)), res[s][:, t, :])
+
+        def silu_part(n):
+            e, t0, t1 = a_parts[n]
+            nc.scalar.activation(neg[n][:], a_sb[n], ACT.Silu, scale=-1.0)
+            nc.gpsimd.tensor_scalar(one_less[n][:], neg[n][:], -1.0, 1.0, MULT, ADD)
             nc.gpsimd.tensor_tensor(
-                times_g[e][:], one_less[e][:], g_sb[:, slots].unsqueeze(1).to_broadcast([P, PACK, C]), MULT
+                times_g[e][:, t0:t1, :], one_less[n][:], g_sb[e].unsqueeze(1).to_broadcast([P, t1 - t0, C]), MULT
             )
 
-        def sigmoid_part(e):
-            nc.scalar.activation(sig[:, e], a_sb[e], ACT.Sigmoid)
-            for h in range(2):
+        def sigmoid_part(n):
+            e, t0, t1 = a_parts[n]
+            nc.scalar.activation(sig[:, e, t0:t1, :], a_sb[n], ACT.Sigmoid)
+            for h in range(t0 // 2, t1 // 2):
                 nc.gpsimd.tensor_tensor(
                     factor[e][h][:], times_g[e][:, 2 * h : 2 * h + 2, :], sig[:, e, 2 * h : 2 * h + 2, :], MULT
                 )
 
-        neg_first = keep.tile([P, PACK, C], F32, name="neg_first")
-        silu_part(0, neg_first[:])
-        run(0)
-        run(1)
-        neg_rest = keep.tile([P, E - 1, PACK, C], F32, name="neg_rest", tag="neg", align_bytes=64)
-        for e in range(1, E):
-            silu_part(e, neg_rest[:, e - 1])
-        run(2)
+        product(0)
+        gather_words(2, "g_w_third")
+        gather_scales(2)
+        spread(0)
+        silu_part(0)
+        silu_part(1)
+        product(1)
+        spread(1)
+        w1_s = keep.tile([P, E, W], U8, name="w1_s", tag="w1_s", align_bytes=64)
+        load_planes(w1_s, w1t_scales)
+        silu_part(2)
+        product(2)
         w1_w = keep.tile([P, E, W], I32, name="w1_w", tag="w1_w", align_bytes=64)
         nc.sync.dma_start(w1_w[:], w1t_words[:, 0].rearrange("e p k d -> p e (k d)").bitcast(I32))
+        silu_part(3)
+        product(3)
+        spread(2)
         sig = keep.tile([P, E, PACK, C], F32, name="sig", tag="sig", align_bytes=64)
-        for e in range(E):
-            sigmoid_part(e)
+        sigmoid_part(0)
+        sigmoid_part(1)
+        product(4)
+        product(5)
+        spread(3)
+        sigmoid_part(2)
+        sigmoid_part(3)
 
         da = [keep.tile([P, PACK, C], F32, name=f"da{e}") for e in range(E)]
         dx = [keep.tile([P, PACK, (e1 - e0) * C], F32, name=f"dx{e0}") for e0, e1 in groups]

@@ -39,19 +39,18 @@ def tile_moe_seb_silu_kernel(
         dy_w = keep.tile([P, T], I32, name="dy_w", align_bytes=64)
         dy_s = keep.tile([P, T], U8, name="dy_s", align_bytes=64)
         w2_first = keep.tile([P, 2 * W], U8, name="w2_first", align_bytes=64)
-        w2_s = keep.tile([P, E, W], U8, name="w2_s", align_bytes=64)
-        q_rows = keep.tile([P, P], F32, name="q_rows", tag="q_rows", align_bytes=64)
+        w2_s_first = keep.tile([P, 1, W], U8, name="w2_s_first", align_bytes=64)
+        q_rows = keep.tile([P, P + 1], F32, name="q_rows", tag="q_rows", align_bytes=64)
         q_cols = keep.tile([P, T // P], F32, name="q_cols")
         ident = keep.tile([P, P], F32, name="ident")
 
         nc.vector.memset(dy_s[:].bitcast(I32), 0)
-        nc.vector.memset(w2_s[:].rearrange("p e w -> p (e w)").bitcast(I32), 0)
-        make_identity(nc, ident[:])
+        nc.vector.memset(w2_s_first[:].rearrange("p e w -> p (e w)").bitcast(I32), 0)
         nc.gpsimd.memset(q_rows[:], 0.0)
-        nc.gpsimd.dma_start(q_rows[0 : T // P, :], gate2[0].rearrange("(c n) -> c n", n=P))
+        nc.gpsimd.dma_start(q_rows[0 : T // P, 0:P], gate2[0].rearrange("(c n) -> c n", n=P))
         a_hbm = a.rearrange("(p j) w -> p j w", j=PACK)
-        warm = keep.tile([P, 1], F32, name="warm", tag="warm")
-        nc.scalar.activation(warm[:], ident[:, 0:1], ACT.Silu)
+        warm = keep.tile([P, 1], F32, name="warm", tag="warm", align_bytes=64)
+        nc.scalar.activation(warm[:], q_rows[:, P : P + 1], ACT.Silu)
 
         def load_planes(plane, scales):
             for quad in range(4):
@@ -61,34 +60,41 @@ def tile_moe_seb_silu_kernel(
                 )
 
         nc.sync.dma_start(list2[:], offs2)
-        nc.sync.dma_start(list1[:], offs)
-        nc.sync.dma_start(w2_first[:].bitcast(I32), w2t_words[0, 0].bitcast(I32))
         nc.sync.dma_start(dy_w[:], dy_words[0].rearrange("p t d -> p (t d)").bitcast(I32))
+        nc.sync.dma_start(w2_first[:].bitcast(I32), w2t_words[0, 0].bitcast(I32))
+        nc.sync.dma_start(list1[:], offs)
         for quad in range(4):
             nc.sync.dma_start(
                 dy_s[32 * quad : 32 * quad + 4, :].bitcast(I32),
                 dy_scales[0, 4 * quad : 4 * quad + 4, :].bitcast(I32),
             )
-        load_planes(w2_s, w2t_scales)
+        load_planes(w2_s_first, w2t_scales[0:1])
 
         a_parts = [(0, 0, 2), (0, 2, 4), (1, 0, 4), (2, 0, 4)]
-        saved = keep.tile([P, T + E * PACK * C], F32, name="saved", tag="warm")
-        g_sb = [saved[:, e * C : (e + 1) * C] for e in range(E)]
-        a_sb = [
-            saved[:, T + (e * PACK + t0) * C : T + (e * PACK + t1) * C].rearrange("p (j w) -> p j w", w=C)
-            for e, t0, t1 in a_parts
-        ]
+        a_sb = {}
+        g_sb = {}
 
-        def load_a(n):
+        def a_piece(n):
             e, t0, t1 = a_parts[n]
-            nc.sync.dma_start(a_sb[n], a_hbm[:, t0:t1, e * C : (e + 1) * C])
+            return a_hbm[:, t0:t1, e * C : (e + 1) * C]
 
-        load_a(0)
-        nc.sync.dma_start(g_sb[0], gate1[:, 0:C])
-        load_a(1)
-        load_a(2)
-        nc.sync.dma_start(saved[:, C:T], gate1[:, C:T])
-        load_a(3)
+        def load_saved(tag, experts, parts):
+            widths = [(a_parts[n][2] - a_parts[n][1]) * C for n in parts]
+            g_width = len(experts) * C
+            saved = keep.tile([P, g_width + sum(widths)], F32, name=f"saved_{tag}", tag=tag, align_bytes=64)
+            nc.sync.dma_start(saved[:, 0:g_width], gate1[:, experts[0] * C : experts[0] * C + g_width])
+            for i, e in enumerate(experts):
+                g_sb[e] = saved[:, i * C : (i + 1) * C]
+            for i, n in enumerate(parts):
+                first = g_width + sum(widths[:i])
+                a_sb[n] = saved[:, first : first + widths[i]].rearrange("p (j w) -> p j w", w=C)
+                nc.sync.dma_start(a_sb[n], a_piece(n))
+
+        a_first = keep.tile([P, 2, C], F32, name="a_first")
+        a_sb[0] = a_first[:]
+        make_identity(nc, ident[:])
+        nc.gpsimd.dma_start(a_first[:], a_piece(0))
+        load_saved("warm", [0, 1], [1, 2])
 
         def span(lst, c0, c1):
             return lst[:, c0 * P // 16 : c1 * P // 16]
@@ -97,12 +103,16 @@ def tile_moe_seb_silu_kernel(
             return lst[:, e0 * C // 16 : e1 * C // 16]
 
         q_ps = psum2.tile([P, W], F32, name="turned", tag="turned")
-        nc.tensor.transpose(q_ps[:, 0:P], q_rows[:], ident[:])
+        nc.tensor.transpose(q_ps[:, 0:P], q_rows[:, 0:P], ident[:])
         nc.scalar.copy(q_cols[:], q_ps[:, 0 : T // P])
 
-        w2_rest = keep.tile([P, E - 1, 2 * W], U8, name="w2_rest", tag="q_rows", align_bytes=64)
-        nc.sync.dma_start(w2_rest[:].bitcast(I32), w2t_words[1:E, 0].rearrange("e p w -> p e w").bitcast(I32))
-        w2_w = [w2_first[:]] + [w2_rest[:, e - 1, :] for e in range(1, E)]
+        w2_rest = keep.tile([P, E - 1, 3 * W], U8, name="w2_rest", tag="q_rows", align_bytes=64)
+        nc.sync.dma_start(
+            w2_rest[:, :, 0 : 2 * W].bitcast(I32), w2t_words[1:E, 0].rearrange("e p w -> p e w").bitcast(I32)
+        )
+        load_planes(w2_rest[:, :, 2 * W : 3 * W], w2t_scales[1:E])
+        w2_s = [w2_s_first[:, 0, :]] + [w2_rest[:, e - 1, 2 * W : 3 * W] for e in range(1, E)]
+        w2_w = [w2_first[:]] + [w2_rest[:, e - 1, 0 : 2 * W] for e in range(1, E)]
 
         runs = [(0, 1), (1, 3), (3, 6)]
         g_w = {}
@@ -127,7 +137,7 @@ def tile_moe_seb_silu_kernel(
         spreads = [(0, 1), (1, 2), (2, 4), (4, 6)]
         res = [keep.tile([P, PACK, (c1 - c0) * P], F32, name=f"res{c0}") for c0, c1 in spreads]
         dc = [keep.tile([P, T], F32, name=f"dc{t}", align_bytes=64) for t in range(PACK)]
-        heirs = {1: "w1_s", 2: "w1_w", 3: "sig"}
+        heirs = {0: "saved_rest", 1: "w1_s", 2: "w1_w", 3: "sig"}
         neg = [keep.tile([P, t1 - t0, C], F32, name=f"neg{e}_{t0}") for e, t0, t1 in a_parts]
         one_less = [keep.tile([P, t1 - t0, C], F32, name=f"one_less{e}_{t0}") for e, t0, t1 in a_parts]
         times_g = [keep.tile([P, PACK, C], F32, name=f"times_g{e}") for e in range(E)]
@@ -147,7 +157,7 @@ def tile_moe_seb_silu_kernel(
                 lhsT=g_w[r][:, cols].bitcast(FP8X4),
                 lhsT_scale=g_s[r][:, cols],
                 rhs=w2_w[e].bitcast(FP4X4),
-                rhs_scale=w2_s[:, e, :],
+                rhs_scale=w2_s[e],
                 start=True,
                 stop=True,
             )
@@ -192,11 +202,12 @@ def tile_moe_seb_silu_kernel(
                     factor[e][h][:], times_g[e][:, 2 * h : 2 * h + 2, :], sig[:, e, 2 * h : 2 * h + 2, :], MULT
                 )
 
+        silu_part(0)
         product(0)
+        load_saved("saved_rest", [2], [3])
         gather_words(2, "g_w_third")
         gather_scales(2)
         spread(0)
-        silu_part(0)
         silu_part(1)
         product(1)
         spread(1)

@@ -82,19 +82,17 @@ def tile_moe_seb_silu_kernel(
             widths = [(a_parts[n][2] - a_parts[n][1]) * C for n in parts]
             g_width = len(experts) * C
             saved = keep.tile([P, g_width + sum(widths)], F32, name=f"saved_{tag}", tag=tag, align_bytes=64)
-            nc.sync.dma_start(saved[:, 0:g_width], gate1[:, experts[0] * C : experts[0] * C + g_width])
             for i, e in enumerate(experts):
                 g_sb[e] = saved[:, i * C : (i + 1) * C]
             for i, n in enumerate(parts):
                 first = g_width + sum(widths[:i])
                 a_sb[n] = saved[:, first : first + widths[i]].rearrange("p (j w) -> p j w", w=C)
                 nc.sync.dma_start(a_sb[n], a_piece(n))
+                if i == 0:
+                    nc.sync.dma_start(saved[:, 0:g_width], gate1[:, experts[0] * C : experts[0] * C + g_width])
 
-        a_first = keep.tile([P, 2, C], F32, name="a_first")
-        a_sb[0] = a_first[:]
         make_identity(nc, ident[:])
-        nc.gpsimd.dma_start(a_first[:], a_piece(0))
-        load_saved("warm", [0, 1], [1, 2])
+        load_saved("warm", [0, 1], [0, 1, 2])
 
         def span(lst, c0, c1):
             return lst[:, c0 * P // 16 : c1 * P // 16]
@@ -137,12 +135,12 @@ def tile_moe_seb_silu_kernel(
         spreads = [(0, 1), (1, 2), (2, 4), (4, 6)]
         res = [keep.tile([P, PACK, (c1 - c0) * P], F32, name=f"res{c0}") for c0, c1 in spreads]
         dc = [keep.tile([P, T], F32, name=f"dc{t}", align_bytes=64) for t in range(PACK)]
-        heirs = {0: "saved_rest", 1: "w1_s", 2: "w1_w", 3: "sig"}
-        neg = [keep.tile([P, t1 - t0, C], F32, name=f"neg{e}_{t0}") for e, t0, t1 in a_parts]
+        heirs = {0: "neg_first", 1: "saved_rest", 2: "w1_s", 3: "sig", 4: "w1_w"}
         one_less = [keep.tile([P, t1 - t0, C], F32, name=f"one_less{e}_{t0}") for e, t0, t1 in a_parts]
         times_g = [keep.tile([P, PACK, C], F32, name=f"times_g{e}") for e in range(E)]
         factor = [
-            [keep.tile([P, 2, C], F32, name=f"factor{e}_{h}", align_bytes=64) for h in range(2)] for e in range(E)
+            [keep.tile([P, 2, (e1 - e0) * C], F32, name=f"factor{e0}_{h}", align_bytes=64) for h in range(2)]
+            for e0, e1 in groups
         ]
 
         def product(c):
@@ -188,8 +186,13 @@ def tile_moe_seb_silu_kernel(
 
         def silu_part(n):
             e, t0, t1 = a_parts[n]
-            nc.scalar.activation(neg[n][:], a_sb[n], ACT.Silu, scale=-1.0)
-            nc.gpsimd.tensor_scalar(one_less[n][:], neg[n][:], -1.0, 1.0, MULT, ADD)
+            tag = "neg_first" if n == 0 else f"neg{n}"
+            neg = keep.tile([P, t1 - t0, C], F32, name=f"neg{n}", tag=tag, align_bytes=64)
+            nc.scalar.activation(neg[:], a_sb[n], ACT.Silu, scale=-1.0)
+            if e == E - 1:
+                nc.scalar.activation(one_less[n][:], neg[:], ACT.Copy, scale=-1.0, bias=1.0)
+            else:
+                nc.gpsimd.tensor_scalar(one_less[n][:], neg[:], -1.0, 1.0, MULT, ADD)
             nc.gpsimd.tensor_tensor(
                 times_g[e][:, t0:t1, :], one_less[n][:], g_sb[e].unsqueeze(1).to_broadcast([P, t1 - t0, C]), MULT
             )
@@ -197,86 +200,94 @@ def tile_moe_seb_silu_kernel(
         def sigmoid_part(n):
             e, t0, t1 = a_parts[n]
             nc.scalar.activation(sig[:, e, t0:t1, :], a_sb[n], ACT.Sigmoid)
-            for h in range(t0 // 2, t1 // 2):
+
+        def factor_part(gi, h):
+            e0, e1 = groups[gi]
+            for e in range(e0, e1):
                 nc.gpsimd.tensor_tensor(
-                    factor[e][h][:], times_g[e][:, 2 * h : 2 * h + 2, :], sig[:, e, 2 * h : 2 * h + 2, :], MULT
+                    factor[gi][h][:, :, (e - e0) * C : (e - e0 + 1) * C],
+                    times_g[e][:, 2 * h : 2 * h + 2, :],
+                    sig[:, e, 2 * h : 2 * h + 2, :],
+                    MULT,
                 )
 
-        silu_part(0)
         product(0)
-        load_saved("saved_rest", [2], [3])
         gather_words(2, "g_w_third")
         gather_scales(2)
         spread(0)
-        silu_part(1)
+        silu_part(0)
         product(1)
+        load_saved("saved_rest", [2], [3])
         spread(1)
-        w1_s = keep.tile([P, E, W], U8, name="w1_s", tag="w1_s", align_bytes=64)
-        load_planes(w1_s, w1t_scales)
+        silu_part(1)
         silu_part(2)
         product(2)
-        w1_w = keep.tile([P, E, W], I32, name="w1_w", tag="w1_w", align_bytes=64)
-        nc.sync.dma_start(w1_w[:], w1t_words[:, 0].rearrange("e p k d -> p e (k d)").bitcast(I32))
-        silu_part(3)
+        w1_s = keep.tile([P, E, W], U8, name="w1_s", tag="w1_s", align_bytes=64)
+        load_planes(w1_s, w1t_scales)
         product(3)
         spread(2)
+        silu_part(3)
         sig = keep.tile([P, E, PACK, C], F32, name="sig", tag="sig", align_bytes=64)
         sigmoid_part(0)
+        factor_part(0, 0)
         sigmoid_part(1)
+        factor_part(0, 1)
         product(4)
+        w1_w = keep.tile([P, E, W], I32, name="w1_w", tag="w1_w", align_bytes=64)
+        nc.sync.dma_start(w1_w[:], w1t_words[:, 0].rearrange("e p k d -> p e (k d)").bitcast(I32))
         product(5)
         spread(3)
         sigmoid_part(2)
         sigmoid_part(3)
+        factor_part(1, 0)
+        factor_part(1, 1)
 
-        da = [keep.tile([P, PACK, C], F32, name=f"da{e}") for e in range(E)]
-        dx = [keep.tile([P, PACK, (e1 - e0) * C], F32, name=f"dx{e0}") for e0, e1 in groups]
-        da_s = [keep.tile([P, C], U8, name=f"da_s{e}", align_bytes=64) for e in range(E)]
-        da_bf = {}
-        da_w = {}
+        widths = [(e1 - e0) * C for e0, e1 in groups]
+        da = [keep.tile([P, PACK, n], F32, name=f"da{n}", tag=f"da{n}", align_bytes=64) for n in widths]
+        dx = [keep.tile([P, PACK, n], F32, name=f"dx{n}") for n in widths]
+        da_s = [keep.tile([P, n], U8, name=f"da_s{n}", align_bytes=64) for n in widths]
+        da_bf = [keep.tile([P, n, PACK], BF16, name=f"da_bf{n}", tag=f"da_bf{n}", align_bytes=64) for n in widths]
         out_sb = {}
 
-        def gather(e):
-            for t in range(PACK):
+        def gather(gi, planes):
+            e0, e1 = groups[gi]
+            for t in planes:
                 nc.vector.tensor_tensor(
-                    da[e][:, t, :], dc[t][:].indirect(part(list1, e, e + 1)), factor[e][t // 2][:, t % 2, :], MULT
-                )
-            for lo, hi in pieces[e]:
-                da_bf[e, lo] = keep.tile([P, hi - lo, PACK], BF16, name=f"da_bf{e}_{lo}", align_bytes=64)
-                nc.scalar.copy(
-                    da_bf[e, lo][:].rearrange("p (c i) t -> p c t i", i=4),
-                    da[e][:, :, lo:hi].rearrange("p t (c i) -> p c t i", i=4),
+                    da[gi][:, t, :], dc[t][:].indirect(part(list1, e0, e1)), factor[gi][t // 2][:, t % 2, :], MULT
                 )
 
-        pieces = [[(0, C)], [(0, C)], [(0, P), (P, C)]]
+        def weave(gi):
+            nc.scalar.copy(
+                da_bf[gi][:].rearrange("p (c i) t -> p c t i", i=4),
+                da[gi][:].rearrange("p t (c i) -> p c t i", i=4),
+            )
 
-        def multiply(e):
-            tag = f"factor{e + 1}_0" if e + 1 < E else f"da_w{e}"
-            da_w[e] = keep.tile([P, C], U32, name=f"da_w{e}", tag=tag, align_bytes=64)
-            for lo, hi in pieces[e]:
-                nc.vector.quantize_mx(
-                    out=da_w[e][:, lo:hi].bitcast(FP8X4),
-                    scales=da_s[e][:, lo:hi],
-                    in_=da_bf[e, lo][:].rearrange("p n t -> p (n t)"),
-                )
-            gi = 0 if e == 0 else 1
-            c0 = (e - groups[gi][0]) * C
+        def multiply(gi, tag):
+            e0, e1 = groups[gi]
+            da_w = keep.tile([P, widths[gi]], U32, name=f"da_w{gi}", tag=tag, align_bytes=64)
+            nc.vector.quantize_mx(
+                out=da_w[:].bitcast(FP8X4),
+                scales=da_s[gi][:],
+                in_=da_bf[gi][:].rearrange("p n t -> p (n t)"),
+            )
             for pair in range(2):
-                bank = psum4.tile([P, 2, C], F32, name="bank", tag="bank")
-                for h in range(2):
-                    cols = slice((2 * pair + h) * P, (2 * pair + h + 1) * P)
-                    nc.tensor.matmul_mx(
-                        out=bank[:, h, :],
-                        lhsT=w1_w[:, e, cols].bitcast(FP8X4),
-                        lhsT_scale=w1_s[:, e, cols],
-                        rhs=da_w[e][:].bitcast(FP8X4),
-                        rhs_scale=da_s[e][:],
-                        start=True,
-                        stop=True,
-                    )
-                nc.scalar.copy(dx[gi][:, 2 * pair : 2 * pair + 2, c0 : c0 + C], bank[:])
+                for e in range(e0, e1):
+                    slots = slice((e - e0) * C, (e - e0 + 1) * C)
+                    bank = psum4.tile([P, 2, C], F32, name="bank", tag="bank")
+                    for h in range(2):
+                        cols = slice((2 * pair + h) * P, (2 * pair + h + 1) * P)
+                        nc.tensor.matmul_mx(
+                            out=bank[:, h, :],
+                            lhsT=w1_w[:, e, cols].bitcast(FP8X4),
+                            lhsT_scale=w1_s[:, e, cols],
+                            rhs=da_w[:, slots].bitcast(FP8X4),
+                            rhs_scale=da_s[gi][:, slots],
+                            start=True,
+                            stop=True,
+                        )
+                    nc.scalar.copy(dx[gi][:, 2 * pair : 2 * pair + 2, slots], bank[:])
 
-        out_tags = ["dc0", "dc1", f"da_bf{E - 1}_0", f"da_bf{E - 1}_{P}"]
+        out_tags = ["dc3", "dc2", f"da_bf{widths[1]}", f"da{widths[1]}"]
 
         def scatter(gi, k):
             e0, e1 = groups[gi]
@@ -284,15 +295,17 @@ def tile_moe_seb_silu_kernel(
                 out_sb[k] = keep.tile([P, T], F32, name=f"out_sb{k}", tag=out_tags[k], align_bytes=64)
             nc.vector.tensor_copy(out_sb[k][:].indirect(part(list1, e0, e1)), dx[gi][:, k, :])
 
-        gather(0)
-        gather(1)
-        multiply(0)
-        gather(2)
-        multiply(1)
+        gather(0, range(PACK))
+        weave(0)
+        gather(1, range(0, 2))
+        multiply(0, "factor1_0")
+        gather(1, range(2, PACK))
+        weave(1)
         scatter(0, 0)
-        multiply(2)
-        for k in range(1, PACK):
-            scatter(0, k)
+        scatter(0, 1)
+        multiply(1, "da_w1")
+        scatter(0, 2)
+        scatter(0, 3)
         for k in range(PACK):
             scatter(1, k)
             nc.sync.dma_start(out[k * P : (k + 1) * P, :], out_sb[k][:])

@@ -132,7 +132,7 @@ def tile_moe_seb_silu_kernel(
         gather_scales(1)
 
         groups = [(0, 1), (1, 3)]
-        spreads = [(0, 1), (1, 2), (2, 4), (4, 6)]
+        spreads = [(0, 1), (1, 2), (2, 4), (4, 5), (5, 6)]
         res = [keep.tile([P, PACK, (c1 - c0) * P], F32, name=f"res{c0}") for c0, c1 in spreads]
         dc = [keep.tile([P, T], F32, name=f"dc{t}", align_bytes=64) for t in range(PACK)]
         heirs = {0: "neg_first", 1: "saved_rest", 2: "w1_s", 3: "sig", 4: "w1_w"}
@@ -165,11 +165,15 @@ def tile_moe_seb_silu_kernel(
                 gated = ring.tile([P, PACK, P], F32, name="gated", tag="gated")
             if c == 0:
                 by_plane = sums[:].rearrange("s (p t) -> s t p", t=PACK)
+                for t0, t1 in [(0, 1), (1, PACK)]:
+                    nc.vector.tensor_scalar_mul(gated[:, t0:t1, :], by_plane[:, t0:t1, :], q_cols[:, c : c + 1])
                 for t in range(PACK):
-                    nc.scalar.activation(gated[:, t, :], by_plane[:, t, :], ACT.Copy, scale=q_cols[:, c : c + 1])
                     bank = psum4.tile([P, 2, C], F32, name="bank", tag="bank")
                     nc.tensor.transpose(bank[:, 0, 0:P], gated[:, t, :], ident[:])
-                    nc.scalar.copy(res[s][:, t, place], bank[:, 0, 0:P])
+                    if t == 0:
+                        nc.vector.tensor_copy(res[s][:, t, place], bank[:, 0, 0:P])
+                    else:
+                        nc.scalar.copy(res[s][:, t, place], bank[:, 0, 0:P])
                 return
             nc.scalar.activation(
                 gated[:], sums[:].rearrange("s (p t) -> s t p", t=PACK), ACT.Copy, scale=q_cols[:, c : c + 1]
@@ -186,7 +190,7 @@ def tile_moe_seb_silu_kernel(
 
         def silu_part(n):
             e, t0, t1 = a_parts[n]
-            tag = "neg_first" if n == 0 else f"neg{n}"
+            tag = "neg_first" if n == 1 else f"neg{n}"
             neg = keep.tile([P, t1 - t0, C], F32, name=f"neg{n}", tag=tag, align_bytes=64)
             nc.scalar.activation(neg[:], a_sb[n], ACT.Silu, scale=-1.0)
             if e == E - 1:
@@ -197,13 +201,13 @@ def tile_moe_seb_silu_kernel(
                 times_g[e][:, t0:t1, :], one_less[n][:], g_sb[e].unsqueeze(1).to_broadcast([P, t1 - t0, C]), MULT
             )
 
-        def sigmoid_part(n):
-            e, t0, t1 = a_parts[n]
-            nc.scalar.activation(sig[:, e, t0:t1, :], a_sb[n], ACT.Sigmoid)
-
-        def factor_part(gi, h):
-            e0, e1 = groups[gi]
-            for e in range(e0, e1):
+        def sigmoid_part(e, t0, t1):
+            n = [i for i, (pe, p0, p1) in enumerate(a_parts) if pe == e and p0 <= t0 < p1][0]
+            p0 = a_parts[n][1]
+            nc.scalar.activation(sig[:, e, t0:t1, :], a_sb[n][:, t0 - p0 : t1 - p0, :], ACT.Sigmoid)
+            gi = [i for i, (e0, e1) in enumerate(groups) if e0 <= e < e1][0]
+            e0 = groups[gi][0]
+            for h in range(t0 // 2, t1 // 2):
                 nc.gpsimd.tensor_tensor(
                     factor[gi][h][:, :, (e - e0) * C : (e - e0 + 1) * C],
                     times_g[e][:, 2 * h : 2 * h + 2, :],
@@ -211,11 +215,11 @@ def tile_moe_seb_silu_kernel(
                     MULT,
                 )
 
-        product(0)
         gather_words(2, "g_w_third")
         gather_scales(2)
-        spread(0)
         silu_part(0)
+        product(0)
+        spread(0)
         product(1)
         load_saved("saved_rest", [2], [3])
         spread(1)
@@ -228,38 +232,34 @@ def tile_moe_seb_silu_kernel(
         spread(2)
         silu_part(3)
         sig = keep.tile([P, E, PACK, C], F32, name="sig", tag="sig", align_bytes=64)
-        sigmoid_part(0)
-        factor_part(0, 0)
-        sigmoid_part(1)
-        factor_part(0, 1)
+        sigmoid_part(0, 0, 2)
+        sigmoid_part(0, 2, 4)
         product(4)
+        spread(3)
         w1_w = keep.tile([P, E, W], I32, name="w1_w", tag="w1_w", align_bytes=64)
         nc.sync.dma_start(w1_w[:], w1t_words[:, 0].rearrange("e p k d -> p e (k d)").bitcast(I32))
+        sigmoid_part(1, 0, 4)
         product(5)
-        spread(3)
-        sigmoid_part(2)
-        sigmoid_part(3)
-        factor_part(1, 0)
-        factor_part(1, 1)
+        spread(4)
+        sigmoid_part(2, 0, 2)
+        sigmoid_part(2, 2, 4)
 
         widths = [(e1 - e0) * C for e0, e1 in groups]
-        da = [keep.tile([P, PACK, n], F32, name=f"da{n}", tag=f"da{n}", align_bytes=64) for n in widths]
         dx = [keep.tile([P, PACK, n], F32, name=f"dx{n}") for n in widths]
         da_s = [keep.tile([P, n], U8, name=f"da_s{n}", align_bytes=64) for n in widths]
         da_bf = [keep.tile([P, n, PACK], BF16, name=f"da_bf{n}", tag=f"da_bf{n}", align_bytes=64) for n in widths]
         out_sb = {}
 
-        def gather(gi, planes):
+        def gather(gi, t0, t1, tag):
             e0, e1 = groups[gi]
-            for t in planes:
+            da = keep.tile([P, t1 - t0, widths[gi]], F32, name=f"da{gi}_{t0}", tag=tag, align_bytes=64)
+            for t in range(t0, t1):
                 nc.vector.tensor_tensor(
-                    da[gi][:, t, :], dc[t][:].indirect(part(list1, e0, e1)), factor[gi][t // 2][:, t % 2, :], MULT
+                    da[:, t - t0, :], dc[t][:].indirect(part(list1, e0, e1)), factor[gi][t // 2][:, t % 2, :], MULT
                 )
-
-        def weave(gi):
             nc.scalar.copy(
-                da_bf[gi][:].rearrange("p (c i) t -> p c t i", i=4),
-                da[gi][:].rearrange("p t (c i) -> p c t i", i=4),
+                da_bf[gi][:, :, t0:t1].rearrange("p (c i) t -> p c t i", i=4),
+                da[:].rearrange("p t (c i) -> p c t i", i=4),
             )
 
         def multiply(gi, tag):
@@ -287,7 +287,7 @@ def tile_moe_seb_silu_kernel(
                         )
                     nc.scalar.copy(dx[gi][:, 2 * pair : 2 * pair + 2, slots], bank[:])
 
-        out_tags = ["dc3", "dc2", f"da_bf{widths[1]}", f"da{widths[1]}"]
+        out_tags = ["dc3", "dc2", f"da_bf{widths[1]}", f"da_bf{widths[0]}"]
 
         def scatter(gi, k):
             e0, e1 = groups[gi]
@@ -295,12 +295,10 @@ def tile_moe_seb_silu_kernel(
                 out_sb[k] = keep.tile([P, T], F32, name=f"out_sb{k}", tag=out_tags[k], align_bytes=64)
             nc.vector.tensor_copy(out_sb[k][:].indirect(part(list1, e0, e1)), dx[gi][:, k, :])
 
-        gather(0, range(PACK))
-        weave(0)
-        gather(1, range(0, 2))
+        gather(0, 0, PACK, "da0")
+        gather(1, 0, 2, "da1")
         multiply(0, "factor1_0")
-        gather(1, range(2, PACK))
-        weave(1)
+        gather(1, 2, PACK, f"da_bf{widths[0]}")
         scatter(0, 0)
         scatter(0, 1)
         multiply(1, "da_w1")

@@ -132,7 +132,7 @@ def tile_moe_seb_silu_kernel(
         gather_scales(1)
 
         groups = [(0, 1), (1, 3)]
-        spreads = [(0, 1), (1, 2), (2, 4), (4, 5), (5, 6)]
+        spreads = [(c, c + 1) for c in range(T // P)]
         res = [keep.tile([P, PACK, (c1 - c0) * P], F32, name=f"res{c0}") for c0, c1 in spreads]
         dc = [keep.tile([P, T], F32, name=f"dc{t}", align_bytes=64) for t in range(PACK)]
         heirs = {0: "neg_first", 1: "saved_rest", 2: "w1_s", 3: "sig", 4: "w1_w"}
@@ -226,21 +226,22 @@ def tile_moe_seb_silu_kernel(
         silu_part(1)
         silu_part(2)
         product(2)
+        spread(2)
         w1_s = keep.tile([P, E, W], U8, name="w1_s", tag="w1_s", align_bytes=64)
         load_planes(w1_s, w1t_scales)
         product(3)
-        spread(2)
+        spread(3)
         silu_part(3)
         sig = keep.tile([P, E, PACK, C], F32, name="sig", tag="sig", align_bytes=64)
         sigmoid_part(0, 0, 2)
         sigmoid_part(0, 2, 4)
         product(4)
-        spread(3)
+        spread(4)
         w1_w = keep.tile([P, E, W], I32, name="w1_w", tag="w1_w", align_bytes=64)
         nc.sync.dma_start(w1_w[:], w1t_words[:, 0].rearrange("e p k d -> p e (k d)").bitcast(I32))
         sigmoid_part(1, 0, 4)
         product(5)
-        spread(4)
+        spread(5)
         sigmoid_part(2, 0, 2)
         sigmoid_part(2, 2, 4)
 
@@ -270,24 +271,27 @@ def tile_moe_seb_silu_kernel(
                 scales=da_s[gi][:],
                 in_=da_bf[gi][:].rearrange("p n t -> p (n t)"),
             )
-            for pair in range(2):
-                for e in range(e0, e1):
+            blocks = [(k, e) for k in range(PACK) for e in range(e0, e1)]
+            for first in range(0, len(blocks), 2):
+                bank = psum4.tile([P, 2, C], F32, name="bank", tag="bank")
+                for h, (k, e) in enumerate(blocks[first : first + 2]):
                     slots = slice((e - e0) * C, (e - e0 + 1) * C)
-                    bank = psum4.tile([P, 2, C], F32, name="bank", tag="bank")
-                    for h in range(2):
-                        cols = slice((2 * pair + h) * P, (2 * pair + h + 1) * P)
-                        nc.tensor.matmul_mx(
-                            out=bank[:, h, :],
-                            lhsT=w1_w[:, e, cols].bitcast(FP8X4),
-                            lhsT_scale=w1_s[:, e, cols],
-                            rhs=da_w[:, slots].bitcast(FP8X4),
-                            rhs_scale=da_s[gi][:, slots],
-                            start=True,
-                            stop=True,
-                        )
-                    nc.scalar.copy(dx[gi][:, 2 * pair : 2 * pair + 2, slots], bank[:])
+                    cols = slice(k * P, (k + 1) * P)
+                    nc.tensor.matmul_mx(
+                        out=bank[:, h, :],
+                        lhsT=w1_w[:, e, cols].bitcast(FP8X4),
+                        lhsT_scale=w1_s[:, e, cols],
+                        rhs=da_w[:, slots].bitcast(FP8X4),
+                        rhs_scale=da_s[gi][:, slots],
+                        start=True,
+                        stop=True,
+                    )
+                nc.scalar.copy(
+                    dx[gi][:].rearrange("p k n -> p (k n)")[:, first * C : (first + 2) * C],
+                    bank[:].rearrange("p h n -> p (h n)"),
+                )
 
-        out_tags = ["dc3", "dc2", f"da_bf{widths[1]}", f"da_bf{widths[0]}"]
+        out_tags = ["dc2", "dc3", "dc1", f"da_bf{widths[1]}"]
 
         def scatter(gi, k):
             e0, e1 = groups[gi]
@@ -295,10 +299,11 @@ def tile_moe_seb_silu_kernel(
                 out_sb[k] = keep.tile([P, T], F32, name=f"out_sb{k}", tag=out_tags[k], align_bytes=64)
             nc.vector.tensor_copy(out_sb[k][:].indirect(part(list1, e0, e1)), dx[gi][:, k, :])
 
-        gather(0, 0, PACK, "da0")
+        gather(0, 0, 2, "da0_low")
+        gather(0, 2, PACK, "da0_high")
         gather(1, 0, 2, "da1")
-        multiply(0, "factor1_0")
-        gather(1, 2, PACK, f"da_bf{widths[0]}")
+        multiply(0, "dc0")
+        gather(1, 2, PACK, "dc1")
         scatter(0, 0)
         scatter(0, 1)
         multiply(1, "da_w1")

@@ -21,7 +21,13 @@ T = 768
 E = 3
 C = 256
 W = 512
+CHUNKS = T // P
+PER_COLUMN = 16
 FLOPS = 2 * 2 * W * W * T
+
+RUNS = [(0, 1), (1, 3), (3, 6)]
+PIECES = [(0, 0, 2), (0, 2, 4), (1, 0, 4), (2, 0, 4)]
+GROUPS = [(0, 1), (1, 3)]
 
 
 def tile_moe_seb_silu_kernel(
@@ -30,32 +36,32 @@ def tile_moe_seb_silu_kernel(
     nc = tc.nc
     with ExitStack() as ctx:
         keep = ctx.enter_context(tc.tile_pool(name="keep", bufs=1))
-        ring = ctx.enter_context(tc.tile_pool(name="ring", bufs=3))
         psum2 = ctx.enter_context(tc.psum_pool(name="psum2", bufs=2))
         psum4 = ctx.enter_context(tc.psum_pool(name="psum4", bufs=4))
 
-        list1 = keep.tile([P, T // 16], U16, name="list1")
-        list2 = keep.tile([P, T // 16], U16, name="list2")
+        list1 = keep.tile([P, T // PER_COLUMN], U16, name="list1")
+        list2 = keep.tile([P, T // PER_COLUMN], U16, name="list2")
         dy_w = keep.tile([P, T], I32, name="dy_w", align_bytes=64)
         dy_s = keep.tile([P, T], U8, name="dy_s", align_bytes=64)
         w2_first = keep.tile([P, 2 * W], U8, name="w2_first", align_bytes=64)
         w2_s_first = keep.tile([P, 1, W], U8, name="w2_s_first", align_bytes=64)
-        q_rows = keep.tile([P, P + 1], F32, name="q_rows", tag="q_rows", align_bytes=64)
-        q_cols = keep.tile([P, T // P], F32, name="q_cols")
+        q_rows = keep.tile([P, P], F32, name="q_rows", tag="q_rows", align_bytes=64)
+        q_cols = keep.tile([P, CHUNKS], F32, name="q_cols")
         ident = keep.tile([P, P], F32, name="ident")
 
         nc.vector.memset(dy_s[:].bitcast(I32), 0)
         nc.vector.memset(w2_s_first[:].rearrange("p e w -> p (e w)").bitcast(I32), 0)
+        zero = keep.tile([P, 1], F32, name="zero", tag="zero", align_bytes=64)
+        nc.gpsimd.memset(zero[:], 0.0)
         nc.gpsimd.memset(q_rows[:], 0.0)
-        nc.gpsimd.dma_start(q_rows[0 : T // P, 0:P], gate2[0].rearrange("(c n) -> c n", n=P))
-        a_hbm = a.rearrange("(p j) w -> p j w", j=PACK)
-        warm = keep.tile([P, 1], F32, name="warm", tag="warm", align_bytes=64)
-        nc.scalar.activation(warm[:], q_rows[:, P : P + 1], ACT.Silu)
+        nc.gpsimd.dma_start(q_rows[0:CHUNKS, :], gate2[0].rearrange("(c n) -> c n", n=P))
+        a_planes = a.rearrange("(p t) w -> p t w", t=PACK)
+        nc.scalar.activation(ident[:], zero[:].to_broadcast([P, P]), ACT.Silu)
 
-        def load_planes(plane, scales):
+        def load_scale_rows(tile, scales):
             for quad in range(4):
                 nc.sync.dma_start(
-                    plane[32 * quad : 32 * quad + 4].bitcast(I32),
+                    tile[32 * quad : 32 * quad + 4].bitcast(I32),
                     scales[:, 0, 4 * quad : 4 * quad + 4, :].rearrange("e r w -> r e w").bitcast(I32),
                 )
 
@@ -68,247 +74,225 @@ def tile_moe_seb_silu_kernel(
                 dy_s[32 * quad : 32 * quad + 4, :].bitcast(I32),
                 dy_scales[0, 4 * quad : 4 * quad + 4, :].bitcast(I32),
             )
-        load_planes(w2_s_first, w2t_scales[0:1])
+        load_scale_rows(w2_s_first, w2t_scales[0:1])
 
-        a_parts = [(0, 0, 2), (0, 2, 4), (1, 0, 4), (2, 0, 4)]
         a_sb = {}
         g_sb = {}
 
-        def a_piece(n):
-            e, t0, t1 = a_parts[n]
-            return a_hbm[:, t0:t1, e * C : (e + 1) * C]
-
-        def load_saved(tag, experts, parts):
-            widths = [(a_parts[n][2] - a_parts[n][1]) * C for n in parts]
+        def load_saved(tag, experts, pieces):
+            widths = [(PIECES[n][2] - PIECES[n][1]) * C for n in pieces]
             g_width = len(experts) * C
             saved = keep.tile([P, g_width + sum(widths)], F32, name=f"saved_{tag}", tag=tag, align_bytes=64)
             for i, e in enumerate(experts):
                 g_sb[e] = saved[:, i * C : (i + 1) * C]
-            for i, n in enumerate(parts):
-                first = g_width + sum(widths[:i])
-                a_sb[n] = saved[:, first : first + widths[i]].rearrange("p (j w) -> p j w", w=C)
-                nc.sync.dma_start(a_sb[n], a_piece(n))
+            for i, n in enumerate(pieces):
+                e, t0, t1 = PIECES[n]
+                start = g_width + sum(widths[:i])
+                a_sb[n] = saved[:, start : start + widths[i]].rearrange("p (t w) -> p t w", w=C)
+                nc.sync.dma_start(a_sb[n], a_planes[:, t0:t1, e * C : (e + 1) * C])
                 if i == 0:
                     nc.sync.dma_start(saved[:, 0:g_width], gate1[:, experts[0] * C : experts[0] * C + g_width])
 
-        make_identity(nc, ident[:])
-        load_saved("warm", [0, 1], [0, 1, 2])
+        make_identity(nc, ident[:], nomemset=True)
+        load_saved("zero", [0, 1], [0, 1, 2])
 
-        def span(lst, c0, c1):
-            return lst[:, c0 * P // 16 : c1 * P // 16]
+        def chunk_entries(c0, c1):
+            return list2[:, c0 * P // PER_COLUMN : c1 * P // PER_COLUMN]
 
-        def part(lst, e0, e1):
-            return lst[:, e0 * C // 16 : e1 * C // 16]
+        def expert_entries(e0, e1):
+            return list1[:, e0 * C // PER_COLUMN : e1 * C // PER_COLUMN]
 
-        q_ps = psum2.tile([P, W], F32, name="turned", tag="turned")
-        nc.tensor.transpose(q_ps[:, 0:P], q_rows[:, 0:P], ident[:])
-        nc.scalar.copy(q_cols[:], q_ps[:, 0 : T // P])
+        q_turned = psum2.tile([P, W], F32, name="turned", tag="turned")
+        nc.tensor.transpose(q_turned[:, 0:P], q_rows[:], ident[:])
+        nc.scalar.copy(q_cols[:], q_turned[:, 0:CHUNKS])
 
         w2_rest = keep.tile([P, E - 1, 3 * W], U8, name="w2_rest", tag="q_rows", align_bytes=64)
         nc.sync.dma_start(
             w2_rest[:, :, 0 : 2 * W].bitcast(I32), w2t_words[1:E, 0].rearrange("e p w -> p e w").bitcast(I32)
         )
-        load_planes(w2_rest[:, :, 2 * W : 3 * W], w2t_scales[1:E])
+        load_scale_rows(w2_rest[:, :, 2 * W : 3 * W], w2t_scales[1:E])
         w2_s = [w2_s_first[:, 0, :]] + [w2_rest[:, e - 1, 2 * W : 3 * W] for e in range(1, E)]
         w2_w = [w2_first[:]] + [w2_rest[:, e - 1, 0 : 2 * W] for e in range(1, E)]
 
-        runs = [(0, 1), (1, 3), (3, 6)]
-        g_w = {}
-        g_s = {}
+        slot_w = {}
+        slot_s = {}
 
-        def gather_words(r, tag):
-            c0, c1 = runs[r]
-            g_w[r] = keep.tile([P, (c1 - c0) * P], U32, name=f"g_w{c0}", tag=tag, align_bytes=64)
-            nc.vector.tensor_copy(g_w[r][:], dy_w[:].bitcast(U32).indirect(span(list2, c0, c1)))
+        def gather_run(r):
+            c0, c1 = RUNS[r]
+            slot_w[r] = keep.tile([P, (c1 - c0) * P], U32, name=f"slot_w{r}", align_bytes=64)
+            nc.vector.tensor_copy(slot_w[r][:], dy_w[:].bitcast(U32).indirect(chunk_entries(c0, c1)))
+            slot_s[r] = keep.tile([P, (c1 - c0) * P], U8, name=f"slot_s{r}", align_bytes=64)
+            nc.vector.tensor_copy(slot_s[r][:], dy_s[:].indirect(chunk_entries(c0, c1)))
 
-        def gather_scales(r):
-            c0, c1 = runs[r]
-            g_s[r] = keep.tile([P, (c1 - c0) * P], U8, name=f"g_s{c0}", align_bytes=64)
-            nc.vector.tensor_copy(g_s[r][:], dy_s[:].indirect(span(list2, c0, c1)))
+        gather_run(0)
+        gather_run(1)
 
-        gather_words(0, "g_w_first")
-        gather_scales(0)
-        gather_words(1, "g_w_second")
-        gather_scales(1)
-
-        groups = [(0, 1), (1, 3)]
-        spreads = [(c, c + 1) for c in range(T // P)]
-        res = [keep.tile([P, PACK, (c1 - c0) * P], F32, name=f"res{c0}") for c0, c1 in spreads]
+        planes = [keep.tile([P, PACK, P], F32, name=f"planes{c}") for c in range(CHUNKS)]
         dc = [keep.tile([P, T], F32, name=f"dc{t}", align_bytes=64) for t in range(PACK)]
-        heirs = {0: "neg_first", 1: "saved_rest", 2: "w1_s", 3: "sig", 4: "w1_w"}
-        one_less = [keep.tile([P, t1 - t0, C], F32, name=f"one_less{e}_{t0}") for e, t0, t1 in a_parts]
+        gated_tags = ["second_silu", "saved_rest", "w1_s", "sig", "w1_w", "gated_last"]
+        one_less = [keep.tile([P, t1 - t0, C], F32, name=f"one_less{e}_{t0}") for e, t0, t1 in PIECES]
         times_g = [keep.tile([P, PACK, C], F32, name=f"times_g{e}") for e in range(E)]
         factor = [
             [keep.tile([P, 2, (e1 - e0) * C], F32, name=f"factor{e0}_{h}", align_bytes=64) for h in range(2)]
-            for e0, e1 in groups
+            for e0, e1 in GROUPS
         ]
 
         def product(c):
-            e = c * P // C
-            r = [n for n, (c0, c1) in enumerate(runs) if c0 <= c < c1][0]
-            s = [n for n, (c0, c1) in enumerate(spreads) if c0 <= c < c1][0]
-            cols = slice((c - runs[r][0]) * P, (c - runs[r][0] + 1) * P)
-            place = slice((c - spreads[s][0]) * P, (c - spreads[s][0] + 1) * P)
+            r = [n for n, (c0, c1) in enumerate(RUNS) if c0 <= c < c1][0]
+            cols = slice((c - RUNS[r][0]) * P, (c - RUNS[r][0] + 1) * P)
             sums = psum2.tile([P, W], F32, name="sums", tag="sums")
             nc.tensor.matmul_mx(
                 out=sums[:],
-                lhsT=g_w[r][:, cols].bitcast(FP8X4),
-                lhsT_scale=g_s[r][:, cols],
-                rhs=w2_w[e].bitcast(FP4X4),
-                rhs_scale=w2_s[e],
+                lhsT=slot_w[r][:, cols].bitcast(FP8X4),
+                lhsT_scale=slot_s[r][:, cols],
+                rhs=w2_w[c * P // C].bitcast(FP4X4),
+                rhs_scale=w2_s[c * P // C],
                 start=True,
                 stop=True,
             )
-            if c in heirs:
-                gated = keep.tile([P, PACK, P], F32, name=f"gated{c}", tag=heirs[c], align_bytes=64)
-            else:
-                gated = ring.tile([P, PACK, P], F32, name="gated", tag="gated")
-            if c == 0:
-                by_plane = sums[:].rearrange("s (p t) -> s t p", t=PACK)
-                for t0, t1 in [(0, 1), (1, PACK)]:
-                    nc.vector.tensor_scalar_mul(gated[:, t0:t1, :], by_plane[:, t0:t1, :], q_cols[:, c : c + 1])
-                for t in range(PACK):
-                    bank = psum4.tile([P, 2, C], F32, name="bank", tag="bank")
-                    nc.tensor.transpose(bank[:, 0, 0:P], gated[:, t, :], ident[:])
-                    if t == 0:
-                        nc.vector.tensor_copy(res[s][:, t, place], bank[:, 0, 0:P])
-                    else:
-                        nc.scalar.copy(res[s][:, t, place], bank[:, 0, 0:P])
-                return
-            nc.scalar.activation(
-                gated[:], sums[:].rearrange("s (p t) -> s t p", t=PACK), ACT.Copy, scale=q_cols[:, c : c + 1]
-            )
+            gated = keep.tile([P, PACK, P], F32, name=f"gated{c}", tag=gated_tags[c], align_bytes=64)
+            return sums[:].rearrange("s (p t) -> s t p", t=PACK), gated
+
+        def scatter_chunk(c):
+            for t in range(PACK):
+                nc.vector.tensor_copy(dc[t][:].indirect(chunk_entries(c, c + 1)), planes[c][:, t, :])
+
+        def first_chunk():
+            sums, gated = product(0)
+            for t0, t1 in [(0, 1), (1, PACK)]:
+                nc.vector.tensor_scalar_mul(gated[:, t0:t1, :], sums[:, t0:t1, :], q_cols[:, 0:1])
+            for t in range(PACK):
+                bank = psum4.tile([P, 2, C], F32, name="bank", tag="bank")
+                nc.tensor.transpose(bank[:, 0, 0:P], gated[:, t, :], ident[:])
+                copy = nc.vector.tensor_copy if t == 0 else nc.scalar.copy
+                copy(planes[0][:, t, :], bank[:, 0, 0:P])
+            scatter_chunk(0)
+
+        def turn_chunk(c):
+            sums, gated = product(c)
+            nc.scalar.activation(gated[:], sums, ACT.Copy, scale=q_cols[:, c : c + 1])
             turned = psum2.tile([P, W], F32, name="turned", tag="turned")
             for t in range(PACK):
                 nc.tensor.transpose(turned[:, t * P : (t + 1) * P], gated[:, t, :], ident[:])
-            nc.scalar.copy(res[s][:, :, place], turned[:].rearrange("p (t s) -> p t s", t=PACK))
+            nc.scalar.copy(planes[c][:], turned[:].rearrange("p (t s) -> p t s", t=PACK))
 
-        def spread(s):
-            c0, c1 = spreads[s]
-            for t in range(PACK):
-                nc.vector.tensor_copy(dc[t][:].indirect(span(list2, c0, c1)), res[s][:, t, :])
-
-        def silu_part(n):
-            e, t0, t1 = a_parts[n]
-            tag = "neg_first" if n == 1 else f"neg{n}"
-            neg = keep.tile([P, t1 - t0, C], F32, name=f"neg{n}", tag=tag, align_bytes=64)
-            nc.scalar.activation(neg[:], a_sb[n], ACT.Silu, scale=-1.0)
+        def silu_piece(n, tag):
+            e, t0, t1 = PIECES[n]
+            silu = keep.tile([P, t1 - t0, C], F32, name=f"silu{n}", tag=tag, align_bytes=64)
+            nc.scalar.activation(silu[:], a_sb[n], ACT.Silu, scale=-1.0)
             if e == E - 1:
-                nc.scalar.activation(one_less[n][:], neg[:], ACT.Copy, scale=-1.0, bias=1.0)
+                nc.scalar.activation(one_less[n][:], silu[:], ACT.Copy, scale=-1.0, bias=1.0)
             else:
-                nc.gpsimd.tensor_scalar(one_less[n][:], neg[:], -1.0, 1.0, MULT, ADD)
+                nc.gpsimd.tensor_scalar(one_less[n][:], silu[:], -1.0, 1.0, MULT, ADD)
             nc.gpsimd.tensor_tensor(
                 times_g[e][:, t0:t1, :], one_less[n][:], g_sb[e].unsqueeze(1).to_broadcast([P, t1 - t0, C]), MULT
             )
 
-        def sigmoid_part(e, t0, t1):
-            n = [i for i, (pe, p0, p1) in enumerate(a_parts) if pe == e and p0 <= t0 < p1][0]
-            p0 = a_parts[n][1]
+        def sigmoid_piece(e, t0, t1):
+            n = [i for i, (pe, p0, p1) in enumerate(PIECES) if pe == e and p0 <= t0 < p1][0]
+            p0 = PIECES[n][1]
             nc.scalar.activation(sig[:, e, t0:t1, :], a_sb[n][:, t0 - p0 : t1 - p0, :], ACT.Sigmoid)
-            gi = [i for i, (e0, e1) in enumerate(groups) if e0 <= e < e1][0]
-            e0 = groups[gi][0]
+            group = [i for i, (e0, e1) in enumerate(GROUPS) if e0 <= e < e1][0]
+            e0 = GROUPS[group][0]
             for h in range(t0 // 2, t1 // 2):
                 nc.gpsimd.tensor_tensor(
-                    factor[gi][h][:, :, (e - e0) * C : (e - e0 + 1) * C],
+                    factor[group][h][:, :, (e - e0) * C : (e - e0 + 1) * C],
                     times_g[e][:, 2 * h : 2 * h + 2, :],
                     sig[:, e, 2 * h : 2 * h + 2, :],
                     MULT,
                 )
 
-        gather_words(2, "g_w_third")
-        gather_scales(2)
-        silu_part(0)
-        product(0)
-        spread(0)
-        product(1)
+        gather_run(2)
+        silu_piece(0, "silu0")
+        first_chunk()
+        turn_chunk(1)
         load_saved("saved_rest", [2], [3])
-        spread(1)
-        silu_part(1)
-        silu_part(2)
-        product(2)
-        spread(2)
+        scatter_chunk(1)
+        silu_piece(1, "second_silu")
+        silu_piece(2, "silu2")
+        turn_chunk(2)
+        scatter_chunk(2)
         w1_s = keep.tile([P, E, W], U8, name="w1_s", tag="w1_s", align_bytes=64)
-        load_planes(w1_s, w1t_scales)
-        product(3)
-        spread(3)
-        silu_part(3)
+        load_scale_rows(w1_s, w1t_scales)
+        turn_chunk(3)
+        scatter_chunk(3)
+        silu_piece(3, "silu3")
         sig = keep.tile([P, E, PACK, C], F32, name="sig", tag="sig", align_bytes=64)
-        sigmoid_part(0, 0, 2)
-        sigmoid_part(0, 2, 4)
-        product(4)
-        spread(4)
+        sigmoid_piece(0, 0, 2)
+        sigmoid_piece(0, 2, PACK)
+        turn_chunk(4)
+        scatter_chunk(4)
         w1_w = keep.tile([P, E, W], I32, name="w1_w", tag="w1_w", align_bytes=64)
         nc.sync.dma_start(w1_w[:], w1t_words[:, 0].rearrange("e p k d -> p e (k d)").bitcast(I32))
-        sigmoid_part(1, 0, 4)
-        product(5)
-        spread(5)
-        sigmoid_part(2, 0, 2)
-        sigmoid_part(2, 2, 4)
+        sigmoid_piece(1, 0, PACK)
+        turn_chunk(5)
+        scatter_chunk(5)
+        sigmoid_piece(2, 0, 2)
+        sigmoid_piece(2, 2, PACK)
 
-        widths = [(e1 - e0) * C for e0, e1 in groups]
-        dx = [keep.tile([P, PACK, n], F32, name=f"dx{n}") for n in widths]
-        da_s = [keep.tile([P, n], U8, name=f"da_s{n}", align_bytes=64) for n in widths]
-        da_bf = [keep.tile([P, n, PACK], BF16, name=f"da_bf{n}", tag=f"da_bf{n}", align_bytes=64) for n in widths]
+        group_slots = [(e1 - e0) * C for e0, e1 in GROUPS]
+        dx = [keep.tile([P, PACK, n], F32, name=f"dx{n}") for n in group_slots]
+        da_s = [keep.tile([P, n], U8, name=f"da_s{n}", align_bytes=64) for n in group_slots]
+        da_bf = [keep.tile([P, n, PACK], BF16, name=f"da_bf{n}", tag=f"da_bf{n}", align_bytes=64) for n in group_slots]
         out_sb = {}
 
-        def gather(gi, t0, t1, tag):
-            e0, e1 = groups[gi]
-            da = keep.tile([P, t1 - t0, widths[gi]], F32, name=f"da{gi}_{t0}", tag=tag, align_bytes=64)
-            for t in range(t0, t1):
+        def gather_half(group, h, tag):
+            e0, e1 = GROUPS[group]
+            da = keep.tile([P, 2, group_slots[group]], F32, name=f"da{group}_{h}", tag=tag, align_bytes=64)
+            for t in range(2):
                 nc.vector.tensor_tensor(
-                    da[:, t - t0, :], dc[t][:].indirect(part(list1, e0, e1)), factor[gi][t // 2][:, t % 2, :], MULT
+                    da[:, t, :], dc[2 * h + t][:].indirect(expert_entries(e0, e1)), factor[group][h][:, t, :], MULT
                 )
             nc.scalar.copy(
-                da_bf[gi][:, :, t0:t1].rearrange("p (c i) t -> p c t i", i=4),
+                da_bf[group][:, :, 2 * h : 2 * h + 2].rearrange("p (c i) t -> p c t i", i=4),
                 da[:].rearrange("p t (c i) -> p c t i", i=4),
             )
 
-        def multiply(gi, tag):
-            e0, e1 = groups[gi]
-            da_w = keep.tile([P, widths[gi]], U32, name=f"da_w{gi}", tag=tag, align_bytes=64)
+        def multiply(group, tag):
+            e0, e1 = GROUPS[group]
+            da_w = keep.tile([P, group_slots[group]], U32, name=f"da_w{group}", tag=tag, align_bytes=64)
             nc.vector.quantize_mx(
                 out=da_w[:].bitcast(FP8X4),
-                scales=da_s[gi][:],
-                in_=da_bf[gi][:].rearrange("p n t -> p (n t)"),
+                scales=da_s[group][:],
+                in_=da_bf[group][:].rearrange("p n t -> p (n t)"),
             )
             blocks = [(k, e) for k in range(PACK) for e in range(e0, e1)]
-            for first in range(0, len(blocks), 2):
+            for pair in range(0, len(blocks), 2):
                 bank = psum4.tile([P, 2, C], F32, name="bank", tag="bank")
-                for h, (k, e) in enumerate(blocks[first : first + 2]):
+                for j, (k, e) in enumerate(blocks[pair : pair + 2]):
                     slots = slice((e - e0) * C, (e - e0 + 1) * C)
-                    cols = slice(k * P, (k + 1) * P)
+                    rows = slice(k * P, (k + 1) * P)
                     nc.tensor.matmul_mx(
-                        out=bank[:, h, :],
-                        lhsT=w1_w[:, e, cols].bitcast(FP8X4),
-                        lhsT_scale=w1_s[:, e, cols],
+                        out=bank[:, j, :],
+                        lhsT=w1_w[:, e, rows].bitcast(FP8X4),
+                        lhsT_scale=w1_s[:, e, rows],
                         rhs=da_w[:, slots].bitcast(FP8X4),
-                        rhs_scale=da_s[gi][:, slots],
+                        rhs_scale=da_s[group][:, slots],
                         start=True,
                         stop=True,
                     )
                 nc.scalar.copy(
-                    dx[gi][:].rearrange("p k n -> p (k n)")[:, first * C : (first + 2) * C],
-                    bank[:].rearrange("p h n -> p (h n)"),
+                    dx[group][:].rearrange("p k n -> p (k n)")[:, pair * C : (pair + 2) * C],
+                    bank[:].rearrange("p j n -> p (j n)"),
                 )
 
-        out_tags = ["dc2", "dc3", "dc1", f"da_bf{widths[1]}"]
+        def scatter_out(group, k):
+            nc.vector.tensor_copy(out_sb[k][:].indirect(expert_entries(*GROUPS[group])), dx[group][:, k, :])
 
-        def scatter(gi, k):
-            e0, e1 = groups[gi]
-            if gi == 0:
-                out_sb[k] = keep.tile([P, T], F32, name=f"out_sb{k}", tag=out_tags[k], align_bytes=64)
-            nc.vector.tensor_copy(out_sb[k][:].indirect(part(list1, e0, e1)), dx[gi][:, k, :])
+        def first_scatter(k, tag):
+            out_sb[k] = keep.tile([P, T], F32, name=f"out_sb{k}", tag=tag, align_bytes=64)
+            scatter_out(0, k)
 
-        gather(0, 0, 2, "da0_low")
-        gather(0, 2, PACK, "da0_high")
-        gather(1, 0, 2, "da1")
+        gather_half(0, 0, "da0_low")
+        gather_half(0, 1, "da0_high")
+        gather_half(1, 0, "da1_low")
         multiply(0, "dc0")
-        gather(1, 2, PACK, "dc1")
-        scatter(0, 0)
-        scatter(0, 1)
+        gather_half(1, 1, "dc1")
+        first_scatter(0, "dc2")
+        first_scatter(1, "dc3")
         multiply(1, "da_w1")
-        scatter(0, 2)
-        scatter(0, 3)
+        first_scatter(2, "dc1")
+        first_scatter(3, f"da_bf{group_slots[1]}")
         for k in range(PACK):
-            scatter(1, k)
+            scatter_out(1, k)
             nc.sync.dma_start(out[k * P : (k + 1) * P, :], out_sb[k][:])

@@ -26,6 +26,7 @@ PER_COLUMN = 16
 FLOPS = 2 * 2 * W * W * T
 
 RUNS = [(0, 1), (1, 3), (3, 6)]
+SCALE_RUNS = [(0, 1), (1, 3), (3, 4), (4, 6)]
 PIECES = [(0, 0, 2), (0, 2, 4), (1, 0, 4), (2, 0, 4)]
 GROUPS = [(0, 1), (1, 3)]
 
@@ -36,6 +37,7 @@ def tile_moe_seb_silu_kernel(
     nc = tc.nc
     with ExitStack() as ctx:
         keep = ctx.enter_context(tc.tile_pool(name="keep", bufs=1))
+        head = ctx.enter_context(tc.tile_pool(name="head", bufs=1))
         psum2 = ctx.enter_context(tc.psum_pool(name="psum2", bufs=2))
         psum4 = ctx.enter_context(tc.psum_pool(name="psum4", bufs=4))
 
@@ -45,7 +47,7 @@ def tile_moe_seb_silu_kernel(
         dy_s = keep.tile([P, T], U8, name="dy_s", align_bytes=64)
         w2_first = keep.tile([P, 2 * W], U8, name="w2_first", align_bytes=64)
         w2_s_first = keep.tile([P, 1, W], U8, name="w2_s_first", align_bytes=64)
-        q_rows = keep.tile([P, P], F32, name="q_rows", tag="q_rows", align_bytes=64)
+        q_rows = head.tile([P, P], F32, name="q_rows", align_bytes=64, offset=10 * P)
         q_cols = keep.tile([P, CHUNKS], F32, name="q_cols")
         ident = keep.tile([P, P], F32, name="ident")
 
@@ -104,9 +106,11 @@ def tile_moe_seb_silu_kernel(
 
         q_turned = psum2.tile([P, W], F32, name="turned", tag="turned")
         nc.tensor.transpose(q_turned[:, 0:P], q_rows[:], ident[:])
+        q_first = keep.tile([P, 1], F32, name="q_first", tag="q_first", align_bytes=64)
+        nc.scalar.copy(q_first[:], q_turned[:, 0:1])
         nc.scalar.copy(q_cols[:], q_turned[:, 0:CHUNKS])
 
-        w2_rest = keep.tile([P, E - 1, 3 * W], U8, name="w2_rest", tag="q_rows", align_bytes=64)
+        w2_rest = head.tile([P, E - 1, 3 * W], U8, name="w2_rest", align_bytes=64, offset=12 * P)
         nc.sync.dma_start(
             w2_rest[:, :, 0 : 2 * W].bitcast(I32), w2t_words[1:E, 0].rearrange("e p w -> p e w").bitcast(I32)
         )
@@ -119,9 +123,16 @@ def tile_moe_seb_silu_kernel(
 
         def gather_run(r):
             c0, c1 = RUNS[r]
-            slot_w[r] = keep.tile([P, (c1 - c0) * P], U32, name=f"slot_w{r}", align_bytes=64)
+            if r == len(RUNS) - 1:
+                slot_w[r] = head.tile([P, (c1 - c0) * P], U32, name=f"slot_w{r}", align_bytes=64, offset=0)
+            else:
+                slot_w[r] = keep.tile([P, (c1 - c0) * P], U32, name=f"slot_w{r}", align_bytes=64)
             nc.vector.tensor_copy(slot_w[r][:], dy_w[:].bitcast(U32).indirect(chunk_entries(c0, c1)))
-            slot_s[r] = keep.tile([P, (c1 - c0) * P], U8, name=f"slot_s{r}", align_bytes=64)
+            gather_scales(r, f"slot_s{r}")
+
+        def gather_scales(r, tag):
+            c0, c1 = SCALE_RUNS[r]
+            slot_s[r] = keep.tile([P, (c1 - c0) * P], U8, name=f"slot_s{r}", tag=tag, align_bytes=64)
             nc.vector.tensor_copy(slot_s[r][:], dy_s[:].indirect(chunk_entries(c0, c1)))
 
         gather_run(0)
@@ -140,11 +151,13 @@ def tile_moe_seb_silu_kernel(
         def product(c):
             r = [n for n, (c0, c1) in enumerate(RUNS) if c0 <= c < c1][0]
             cols = slice((c - RUNS[r][0]) * P, (c - RUNS[r][0] + 1) * P)
+            rs = [n for n, (c0, c1) in enumerate(SCALE_RUNS) if c0 <= c < c1][0]
+            cols_s = slice((c - SCALE_RUNS[rs][0]) * P, (c - SCALE_RUNS[rs][0] + 1) * P)
             sums = psum2.tile([P, W], F32, name="sums", tag="sums")
             nc.tensor.matmul_mx(
                 out=sums[:],
                 lhsT=slot_w[r][:, cols].bitcast(FP8X4),
-                lhsT_scale=slot_s[r][:, cols],
+                lhsT_scale=slot_s[rs][:, cols_s],
                 rhs=w2_w[c * P // C].bitcast(FP4X4),
                 rhs_scale=w2_s[c * P // C],
                 start=True,
@@ -159,8 +172,9 @@ def tile_moe_seb_silu_kernel(
 
         def first_chunk():
             sums, gated = product(0)
-            for t0, t1 in [(0, 1), (1, PACK)]:
-                nc.vector.tensor_scalar_mul(gated[:, t0:t1, :], sums[:, t0:t1, :], q_cols[:, 0:1])
+            nc.vector.tensor_scalar_mul(gated[:, 0:1, :], sums[:, 0:1, :], q_first[:])
+            nc.vector.tensor_scalar_mul(gated[:, 1:PACK, :], sums[:, 1:PACK, :], q_cols[:, 0:1])
+            gather_scales(len(SCALE_RUNS) - 1, "q_first")
             for t in range(PACK):
                 bank = psum4.tile([P, 2, C], F32, name="bank", tag="bank")
                 nc.tensor.transpose(bank[:, 0, 0:P], gated[:, t, :], ident[:])

@@ -1,7 +1,6 @@
 from contextlib import ExitStack
 
 import concourse.mybir as mybir
-from concourse.masks import make_identity
 
 F32 = mybir.dt.float32
 BF16 = mybir.dt.bfloat16
@@ -21,14 +20,8 @@ T = 768
 E = 3
 C = 256
 W = 512
-CHUNKS = T // P
 PER_COLUMN = 16
 FLOPS = 2 * 2 * W * W * T
-
-RUNS = [(0, 1), (1, 3), (3, 6)]
-SCALE_RUNS = [(0, 1), (1, 3), (3, 4), (4, 6)]
-PIECES = [(0, 0, 2), (0, 2, 4), (1, 0, 4), (2, 0, 4)]
-GROUPS = [(0, 1), (1, 3)]
 
 
 def tile_moe_seb_silu_kernel(
@@ -37,276 +30,245 @@ def tile_moe_seb_silu_kernel(
     nc = tc.nc
     with ExitStack() as ctx:
         keep = ctx.enter_context(tc.tile_pool(name="keep", bufs=1))
-        head = ctx.enter_context(tc.tile_pool(name="head", bufs=1))
-        psum2 = ctx.enter_context(tc.psum_pool(name="psum2", bufs=2))
-        psum4 = ctx.enter_context(tc.psum_pool(name="psum4", bufs=4))
+        psum = ctx.enter_context(tc.psum_pool(name="psum", bufs=8))
+
+        def tile(shape, dtype, name, tag=None):
+            return keep.tile(shape, dtype, name=name, tag=tag or name, align_bytes=64)
+
+        def entries(listed, s0, s1):
+            return listed[:, s0 // PER_COLUMN : s1 // PER_COLUMN]
 
         list1 = keep.tile([P, T // PER_COLUMN], U16, name="list1")
         list2 = keep.tile([P, T // PER_COLUMN], U16, name="list2")
-        dy_w = keep.tile([P, T], I32, name="dy_w", align_bytes=64)
-        dy_s = keep.tile([P, T], U8, name="dy_s", align_bytes=64)
-        w2_first = keep.tile([P, 2 * W], U8, name="w2_first", align_bytes=64)
-        w2_s_first = keep.tile([P, 1, W], U8, name="w2_s_first", align_bytes=64)
-        q_rows = head.tile([P, P], F32, name="q_rows", align_bytes=64, offset=10 * P)
-        q_cols = keep.tile([P, CHUNKS], F32, name="q_cols")
-        ident = keep.tile([P, P], F32, name="ident")
-
-        nc.vector.memset(dy_s[:].bitcast(I32), 0)
-        nc.vector.memset(w2_s_first[:].rearrange("p e w -> p (e w)").bitcast(I32), 0)
-        zero = keep.tile([P, 1], F32, name="zero", tag="zero", align_bytes=64)
-        nc.gpsimd.memset(zero[:], 0.0)
-        nc.gpsimd.memset(q_rows[:], 0.0)
-        nc.gpsimd.dma_start(q_rows[0:CHUNKS, :], gate2[0].rearrange("(c n) -> c n", n=P))
+        dy_w = tile([P, T], I32, "dy_w")
+        dy_s = tile([P, T], U8, "dy_s")
+        w2_w_first = tile([P, 1, 2 * W], U8, "w2_w_first")
+        w2_s_first = tile([P, 1, W], U8, "w2_s_first")
+        w2_w_rest = tile([P, E - 1, 2 * W], U8, "w2_w_rest")
+        w2_s_rest = tile([P, E - 1, W], U8, "w2_s_rest")
+        a_sb = [tile([P, PACK, C], F32, f"a{e}") for e in range(E)]
+        g_sb = tile([P, T], F32, "g_sb")
+        q_sb = tile([P, T], F32, "q_sb")
         a_planes = a.rearrange("(p t) w -> p t w", t=PACK)
-        nc.scalar.activation(ident[:], zero[:].to_broadcast([P, P]), ACT.Silu)
 
-        def load_scale_rows(tile, scales):
+        def load_scale_rows(into, scales):
             for quad in range(4):
                 nc.sync.dma_start(
-                    tile[32 * quad : 32 * quad + 4].bitcast(I32),
+                    into[32 * quad : 32 * quad + 4].bitcast(I32),
                     scales[:, 0, 4 * quad : 4 * quad + 4, :].rearrange("e r w -> r e w").bitcast(I32),
                 )
 
+        def load_scale_rows_repeated(into, rows):
+            words = rows.shape[1] // 4
+            for quad in range(4):
+                nc.sync.dma_start(
+                    into[32 * quad : 32 * quad + 32].bitcast(I32),
+                    rows[4 * quad : 4 * quad + 4, :].bitcast(I32).unsqueeze(0).to_broadcast([8, 4, words]),
+                )
+
+        nc.gpsimd.memset(w2_s_rest[:].rearrange("p e w -> p (e w)").bitcast(I32), 0)
+        load_scale_rows_repeated(dy_s, dy_scales[0])
         nc.sync.dma_start(list2[:], offs2)
         nc.sync.dma_start(dy_w[:], dy_words[0].rearrange("p t d -> p (t d)").bitcast(I32))
-        nc.sync.dma_start(w2_first[:].bitcast(I32), w2t_words[0, 0].bitcast(I32))
+        nc.sync.dma_start(w2_w_first[:, 0, :].bitcast(I32), w2t_words[0, 0].bitcast(I32))
+        nc.sync.dma_start(a_sb[0][:], a_planes[:, :, 0:C])
+        load_scale_rows_repeated(w2_s_first[:, 0, :], w2t_scales[0, 0])
+        nc.sync.dma_start(q_sb[:], gate2)
+        nc.sync.dma_start(w2_w_rest[:].bitcast(I32), w2t_words[1:E, 0].rearrange("e p w -> p e w").bitcast(I32))
+        nc.sync.dma_start(g_sb[:], gate1)
         nc.sync.dma_start(list1[:], offs)
-        for quad in range(4):
-            nc.sync.dma_start(
-                dy_s[32 * quad : 32 * quad + 4, :].bitcast(I32),
-                dy_scales[0, 4 * quad : 4 * quad + 4, :].bitcast(I32),
-            )
-        load_scale_rows(w2_s_first, w2t_scales[0:1])
+        load_scale_rows(w2_s_rest, w2t_scales[1:E])
+        for e in range(1, E):
+            nc.sync.dma_start(a_sb[e][:], a_planes[:, :, e * C : (e + 1) * C])
 
-        a_sb = {}
-        g_sb = {}
+        w2_w_raw = [w2_w_first[:, 0, :]] + [w2_w_rest[:, e - 1, :] for e in range(1, E)]
+        w2_s_raw = [w2_s_first[:, 0, :]] + [w2_s_rest[:, e - 1, :] for e in range(1, E)]
+        w2_w = [tile([P, PACK, P], U16, f"w2_w{e}") for e in range(E)]
+        w2_s = [tile([P, PACK, P], U8, f"w2_s{e}") for e in range(E)]
 
-        def load_saved(tag, experts, pieces):
-            widths = [(PIECES[n][2] - PIECES[n][1]) * C for n in pieces]
-            g_width = len(experts) * C
-            saved = keep.tile([P, g_width + sum(widths)], F32, name=f"saved_{tag}", tag=tag, align_bytes=64)
-            for i, e in enumerate(experts):
-                g_sb[e] = saved[:, i * C : (i + 1) * C]
-            for i, n in enumerate(pieces):
-                e, t0, t1 = PIECES[n]
-                start = g_width + sum(widths[:i])
-                a_sb[n] = saved[:, start : start + widths[i]].rearrange("p (t w) -> p t w", w=C)
-                nc.sync.dma_start(a_sb[n], a_planes[:, t0:t1, e * C : (e + 1) * C])
-                if i == 0:
-                    nc.sync.dma_start(saved[:, 0:g_width], gate1[:, experts[0] * C : experts[0] * C + g_width])
+        def permute_words(e):
+            nc.gpsimd.tensor_copy(w2_w[e][:], w2_w_raw[e].bitcast(U16).rearrange("p (m t) -> p t m", t=PACK))
 
-        make_identity(nc, ident[:], nomemset=True)
-        load_saved("zero", [0, 1], [0, 1, 2])
-
-        def chunk_entries(c0, c1):
-            return list2[:, c0 * P // PER_COLUMN : c1 * P // PER_COLUMN]
-
-        def expert_entries(e0, e1):
-            return list1[:, e0 * C // PER_COLUMN : e1 * C // PER_COLUMN]
-
-        q_turned = psum2.tile([P, W], F32, name="turned", tag="turned")
-        nc.tensor.transpose(q_turned[:, 0:P], q_rows[:], ident[:])
-        q_first = keep.tile([P, 1], F32, name="q_first", tag="q_first", align_bytes=64)
-        nc.scalar.copy(q_first[:], q_turned[:, 0:1])
-        nc.scalar.copy(q_cols[:], q_turned[:, 0:CHUNKS])
-
-        w2_rest = head.tile([P, E - 1, 3 * W], U8, name="w2_rest", align_bytes=64, offset=12 * P)
-        nc.sync.dma_start(
-            w2_rest[:, :, 0 : 2 * W].bitcast(I32), w2t_words[1:E, 0].rearrange("e p w -> p e w").bitcast(I32)
-        )
-        load_scale_rows(w2_rest[:, :, 2 * W : 3 * W], w2t_scales[1:E])
-        w2_s = [w2_s_first[:, 0, :]] + [w2_rest[:, e - 1, 2 * W : 3 * W] for e in range(1, E)]
-        w2_w = [w2_first[:]] + [w2_rest[:, e - 1, 0 : 2 * W] for e in range(1, E)]
+        def permute_scales(e, t0, t1):
+            nc.gpsimd.tensor_copy(w2_s[e][:, t0:t1, :], w2_s_raw[e].rearrange("p (m t) -> p t m", t=PACK)[:, t0:t1, :])
 
         slot_w = {}
         slot_s = {}
 
-        def gather_run(r):
-            c0, c1 = RUNS[r]
-            if r == len(RUNS) - 1:
-                slot_w[r] = head.tile([P, (c1 - c0) * P], U32, name=f"slot_w{r}", align_bytes=64, offset=0)
-            else:
-                slot_w[r] = keep.tile([P, (c1 - c0) * P], U32, name=f"slot_w{r}", align_bytes=64)
-            nc.vector.tensor_copy(slot_w[r][:], dy_w[:].bitcast(U32).indirect(chunk_entries(c0, c1)))
-            gather_scales(r, f"slot_s{r}")
+        def gather_slots(e, tag_w=None, tag_s=None):
+            slot_w[e] = tile([P, C], U32, f"slot_w{e}", tag_w)
+            slot_s[e] = tile([P, C], U8, f"slot_s{e}", tag_s)
+            nc.vector.tensor_copy(slot_w[e][:], dy_w[:].bitcast(U32).indirect(entries(list2, e * C, (e + 1) * C)))
+            nc.vector.tensor_copy(slot_s[e][:], dy_s[:].indirect(entries(list2, e * C, (e + 1) * C)))
 
-        def gather_scales(r, tag):
-            c0, c1 = SCALE_RUNS[r]
-            slot_s[r] = keep.tile([P, (c1 - c0) * P], U8, name=f"slot_s{r}", tag=tag, align_bytes=64)
-            nc.vector.tensor_copy(slot_s[r][:], dy_s[:].indirect(chunk_entries(c0, c1)))
+        gated = {}
+        dc = [tile([P, T], F32, f"dc{t}") for t in range(PACK)]
 
-        gather_run(0)
-        gather_run(1)
-
-        planes = [keep.tile([P, PACK, P], F32, name=f"planes{c}") for c in range(CHUNKS)]
-        dc = [keep.tile([P, T], F32, name=f"dc{t}", align_bytes=64) for t in range(PACK)]
-        gated_tags = ["second_silu", "saved_rest", "w1_s", "sig", "w1_w", "gated_last"]
-        one_less = [keep.tile([P, t1 - t0, C], F32, name=f"one_less{e}_{t0}") for e, t0, t1 in PIECES]
-        times_g = [keep.tile([P, PACK, C], F32, name=f"times_g{e}") for e in range(E)]
-        factor = [
-            [keep.tile([P, 2, (e1 - e0) * C], F32, name=f"factor{e0}_{h}", align_bytes=64) for h in range(2)]
-            for e0, e1 in GROUPS
-        ]
-
-        def product(c):
-            r = [n for n, (c0, c1) in enumerate(RUNS) if c0 <= c < c1][0]
-            cols = slice((c - RUNS[r][0]) * P, (c - RUNS[r][0] + 1) * P)
-            rs = [n for n, (c0, c1) in enumerate(SCALE_RUNS) if c0 <= c < c1][0]
-            cols_s = slice((c - SCALE_RUNS[rs][0]) * P, (c - SCALE_RUNS[rs][0] + 1) * P)
-            sums = psum2.tile([P, W], F32, name="sums", tag="sums")
-            nc.tensor.matmul_mx(
-                out=sums[:],
-                lhsT=slot_w[r][:, cols].bitcast(FP8X4),
-                lhsT_scale=slot_s[rs][:, cols_s],
-                rhs=w2_w[c * P // C].bitcast(FP4X4),
-                rhs_scale=w2_s[c * P // C],
-                start=True,
-                stop=True,
+        def second_layer(e, t0, t1):
+            bank = psum.tile([P, 2, C], F32, name="bank", tag="bank")
+            for t in range(t0, t1):
+                nc.tensor.matmul_mx(
+                    out=bank[:, t - t0, :],
+                    lhsT=w2_w[e][:, t, :].bitcast(U8).bitcast(FP4X4),
+                    lhsT_scale=w2_s[e][:, t, :],
+                    rhs=slot_w[e][:].bitcast(FP8X4),
+                    rhs_scale=slot_s[e][:],
+                    start=True,
+                    stop=True,
+                )
+            times_q = tile([P, t1 - t0, C], F32, f"gated{e}_{t0}")
+            nc.vector.tensor_tensor(
+                times_q[:],
+                bank[:, 0 : t1 - t0, :],
+                q_sb[:, e * C : (e + 1) * C].unsqueeze(1).to_broadcast([P, t1 - t0, C]),
+                MULT,
             )
-            gated = keep.tile([P, PACK, P], F32, name=f"gated{c}", tag=gated_tags[c], align_bytes=64)
-            return sums[:].rearrange("s (p t) -> s t p", t=PACK), gated
+            for t in range(t0, t1):
+                gated[e, t] = times_q[:, t - t0, :]
 
-        def scatter_chunk(c):
-            for t in range(PACK):
-                nc.vector.tensor_copy(dc[t][:].indirect(chunk_entries(c, c + 1)), planes[c][:, t, :])
-
-        def first_chunk():
-            sums, gated = product(0)
-            nc.vector.tensor_scalar_mul(gated[:, 0:1, :], sums[:, 0:1, :], q_first[:])
-            nc.vector.tensor_scalar_mul(gated[:, 1:PACK, :], sums[:, 1:PACK, :], q_cols[:, 0:1])
-            gather_scales(len(SCALE_RUNS) - 1, "q_first")
-            for t in range(PACK):
-                bank = psum4.tile([P, 2, C], F32, name="bank", tag="bank")
-                nc.tensor.transpose(bank[:, 0, 0:P], gated[:, t, :], ident[:])
-                copy = nc.vector.tensor_copy if t == 0 else nc.scalar.copy
-                copy(planes[0][:, t, :], bank[:, 0, 0:P])
-            scatter_chunk(0)
-
-        def turn_chunk(c):
-            sums, gated = product(c)
-            nc.scalar.activation(gated[:], sums, ACT.Copy, scale=q_cols[:, c : c + 1])
-            turned = psum2.tile([P, W], F32, name="turned", tag="turned")
-            for t in range(PACK):
-                nc.tensor.transpose(turned[:, t * P : (t + 1) * P], gated[:, t, :], ident[:])
-            nc.scalar.copy(planes[c][:], turned[:].rearrange("p (t s) -> p t s", t=PACK))
-
-        def silu_piece(n, tag):
-            e, t0, t1 = PIECES[n]
-            silu = keep.tile([P, t1 - t0, C], F32, name=f"silu{n}", tag=tag, align_bytes=64)
-            nc.scalar.activation(silu[:], a_sb[n], ACT.Silu, scale=-1.0)
-            if e == E - 1:
-                nc.scalar.activation(one_less[n][:], silu[:], ACT.Copy, scale=-1.0, bias=1.0)
+        def scatter(engine, window, values):
+            if engine == "vector":
+                nc.vector.tensor_copy(window, values)
             else:
-                nc.gpsimd.tensor_scalar(one_less[n][:], silu[:], -1.0, 1.0, MULT, ADD)
+                nc.scalar.activation(window, values, ACT.Copy)
+
+        def scatter_dc(e, t):
+            scatter(["scalar", "vector"][t % 2], dc[t][:].indirect(entries(list2, e * C, (e + 1) * C)), gated[e, t])
+
+        silu = {}
+        times_g = [tile([P, PACK, C], F32, f"times_g{e}") for e in range(E)]
+
+        def silu_of(e, tag=None):
+            silu[e] = tile([P, PACK, C], F32, f"silu{e}", tag)
+            nc.scalar.activation(silu[e][:], a_sb[e][:], ACT.Silu, scale=-1.0)
+
+        def factor_half(e, h):
+            planes = slice(2 * h, 2 * h + 2)
+            one_less = tile([P, 2, C], F32, f"one_less{e}_{h}")
+            nc.gpsimd.tensor_scalar(one_less[:], silu[e][:, planes, :], -1.0, 1.0, MULT, ADD)
             nc.gpsimd.tensor_tensor(
-                times_g[e][:, t0:t1, :], one_less[n][:], g_sb[e].unsqueeze(1).to_broadcast([P, t1 - t0, C]), MULT
+                times_g[e][:, planes, :],
+                one_less[:],
+                g_sb[:, e * C : (e + 1) * C].unsqueeze(1).to_broadcast([P, 2, C]),
+                MULT,
             )
 
-        def sigmoid_piece(e, t0, t1):
-            n = [i for i, (pe, p0, p1) in enumerate(PIECES) if pe == e and p0 <= t0 < p1][0]
-            p0 = PIECES[n][1]
-            nc.scalar.activation(sig[:, e, t0:t1, :], a_sb[n][:, t0 - p0 : t1 - p0, :], ACT.Sigmoid)
-            group = [i for i, (e0, e1) in enumerate(GROUPS) if e0 <= e < e1][0]
-            e0 = GROUPS[group][0]
-            for h in range(t0 // 2, t1 // 2):
-                nc.gpsimd.tensor_tensor(
-                    factor[group][h][:, :, (e - e0) * C : (e - e0 + 1) * C],
-                    times_g[e][:, 2 * h : 2 * h + 2, :],
-                    sig[:, e, 2 * h : 2 * h + 2, :],
-                    MULT,
-                )
-
-        gather_run(2)
-        silu_piece(0, "silu0")
-        first_chunk()
-        turn_chunk(1)
-        load_saved("saved_rest", [2], [3])
-        scatter_chunk(1)
-        silu_piece(1, "second_silu")
-        silu_piece(2, "silu2")
-        turn_chunk(2)
-        scatter_chunk(2)
-        w1_s = keep.tile([P, E, W], U8, name="w1_s", tag="w1_s", align_bytes=64)
-        load_scale_rows(w1_s, w1t_scales)
-        turn_chunk(3)
-        scatter_chunk(3)
-        silu_piece(3, "silu3")
-        sig = keep.tile([P, E, PACK, C], F32, name="sig", tag="sig", align_bytes=64)
-        sigmoid_piece(0, 0, 2)
-        sigmoid_piece(0, 2, PACK)
-        turn_chunk(4)
-        scatter_chunk(4)
-        w1_w = keep.tile([P, E, W], I32, name="w1_w", tag="w1_w", align_bytes=64)
+        silu_of(0)
+        permute_words(0)
+        permute_scales(0, 0, 2)
+        permute_scales(0, 2, PACK)
+        gather_slots(0)
+        gather_slots(1)
+        for t in range(PACK):
+            second_layer(0, t, t + 1)
+        permute_words(1)
+        permute_scales(1, 0, PACK)
+        factor_half(0, 0)
+        scatter_dc(0, 0)
+        scatter_dc(0, 1)
+        gather_slots(2, "w2_w0", "w2_s0")
+        w1_w = tile([P, E, W], I32, "w1_w", "dy_w")
+        w1_s = tile([P, E, W], U8, "w1_s", "dy_s")
         nc.sync.dma_start(w1_w[:], w1t_words[:, 0].rearrange("e p k d -> p e (k d)").bitcast(I32))
-        sigmoid_piece(1, 0, PACK)
-        turn_chunk(5)
-        scatter_chunk(5)
-        sigmoid_piece(2, 0, 2)
-        sigmoid_piece(2, 2, PACK)
+        load_scale_rows(w1_s, w1t_scales)
+        second_layer(1, 0, 2)
+        second_layer(1, 2, PACK)
+        permute_words(2)
+        permute_scales(2, 0, PACK)
+        factor_half(0, 1)
+        scatter_dc(0, 2)
+        scatter_dc(0, 3)
+        silu_of(1, "gated0_0")
+        factor_half(1, 0)
+        factor_half(1, 1)
+        scatter_dc(1, 0)
+        scatter_dc(1, 1)
+        silu_of(2, "gated0_2")
+        factor_half(2, 0)
+        factor_half(2, 1)
+        second_layer(2, 0, 2)
+        second_layer(2, 2, PACK)
+        scatter_dc(1, 2)
+        scatter_dc(1, 3)
+        for t in range(PACK):
+            scatter_dc(2, t)
 
-        group_slots = [(e1 - e0) * C for e0, e1 in GROUPS]
-        dx = [keep.tile([P, PACK, n], F32, name=f"dx{n}") for n in group_slots]
-        da_s = [keep.tile([P, n], U8, name=f"da_s{n}", align_bytes=64) for n in group_slots]
-        da_bf = [keep.tile([P, n, PACK], BF16, name=f"da_bf{n}", tag=f"da_bf{n}", align_bytes=64) for n in group_slots]
-        out_sb = {}
+        sig = {}
+        picked = {}
+        da_bf = [tile([P, C, PACK], BF16, f"da_bf{e}") for e in range(E)]
+        da_w = [tile([P, C], U32, f"da_w{e}") for e in range(E)]
+        da_s = [tile([P, C], U8, f"da_s{e}") for e in range(E)]
+        out_sb = [tile([P, T], F32, f"out_sb{k}") for k in range(PACK)]
+        dx = {}
 
-        def gather_half(group, h, tag):
-            e0, e1 = GROUPS[group]
-            da = keep.tile([P, 2, group_slots[group]], F32, name=f"da{group}_{h}", tag=tag, align_bytes=64)
-            for t in range(2):
+        def sigmoid_of(e, tag=None):
+            sig[e] = tile([P, PACK, C], F32, f"sig{e}", tag)
+            nc.scalar.activation(sig[e][:], a_sb[e][:], ACT.Sigmoid)
+
+        def gather_dc(e, tag=None):
+            picked[e] = tile([P, PACK, C], F32, f"picked{e}", tag)
+            for t in (0, 2, 1, 3):
                 nc.vector.tensor_tensor(
-                    da[:, t, :], dc[2 * h + t][:].indirect(expert_entries(e0, e1)), factor[group][h][:, t, :], MULT
+                    picked[e][:, t, :], dc[t][:].indirect(entries(list1, e * C, (e + 1) * C)), times_g[e][:, t, :], MULT
                 )
-            nc.scalar.copy(
-                da_bf[group][:, :, 2 * h : 2 * h + 2].rearrange("p (c i) t -> p c t i", i=4),
-                da[:].rearrange("p t (c i) -> p c t i", i=4),
-            )
 
-        def multiply(group, tag):
-            e0, e1 = GROUPS[group]
-            da_w = keep.tile([P, group_slots[group]], U32, name=f"da_w{group}", tag=tag, align_bytes=64)
+        def quantise(e):
+            nc.vector.tensor_tensor(
+                da_bf[e][:].rearrange("p (c i) t -> p c t i", i=4),
+                picked[e][:].rearrange("p t (c i) -> p c t i", i=4),
+                sig[e][:].rearrange("p t (c i) -> p c t i", i=4),
+                MULT,
+            )
             nc.vector.quantize_mx(
-                out=da_w[:].bitcast(FP8X4),
-                scales=da_s[group][:],
-                in_=da_bf[group][:].rearrange("p n t -> p (n t)"),
+                out=da_w[e][:].bitcast(FP8X4), scales=da_s[e][:], in_=da_bf[e][:].rearrange("p n t -> p (n t)")
             )
-            blocks = [(k, e) for k in range(PACK) for e in range(e0, e1)]
-            for pair in range(0, len(blocks), 2):
-                bank = psum4.tile([P, 2, C], F32, name="bank", tag="bank")
-                for j, (k, e) in enumerate(blocks[pair : pair + 2]):
-                    slots = slice((e - e0) * C, (e - e0 + 1) * C)
-                    rows = slice(k * P, (k + 1) * P)
-                    nc.tensor.matmul_mx(
-                        out=bank[:, j, :],
-                        lhsT=w1_w[:, e, rows].bitcast(FP8X4),
-                        lhsT_scale=w1_s[:, e, rows],
-                        rhs=da_w[:, slots].bitcast(FP8X4),
-                        rhs_scale=da_s[group][:, slots],
-                        start=True,
-                        stop=True,
-                    )
-                nc.scalar.copy(
-                    dx[group][:].rearrange("p k n -> p (k n)")[:, pair * C : (pair + 2) * C],
-                    bank[:].rearrange("p j n -> p (j n)"),
+
+        def first_layer(e, k0, copy):
+            bank = psum.tile([P, 2, C], F32, name="bank", tag="bank")
+            for k in range(k0, k0 + 2):
+                rows = slice(k * P, (k + 1) * P)
+                nc.tensor.matmul_mx(
+                    out=bank[:, k - k0, :],
+                    lhsT=w1_w[:, e, rows].bitcast(FP8X4),
+                    lhsT_scale=w1_s[:, e, rows],
+                    rhs=da_w[e][:].bitcast(FP8X4),
+                    rhs_scale=da_s[e][:],
+                    start=True,
+                    stop=True,
                 )
+            sums = tile([P, 2, C], F32, f"dx{e}_{k0}")
+            copy(sums[:], bank[:])
+            for k in range(k0, k0 + 2):
+                dx[e, k] = sums[:, k - k0, :]
 
-        def scatter_out(group, k):
-            nc.vector.tensor_copy(out_sb[k][:].indirect(expert_entries(*GROUPS[group])), dx[group][:, k, :])
+        def scatter_out(engine, e, k, s0=0, s1=C):
+            scatter(engine, out_sb[k][:].indirect(entries(list1, e * C + s0, e * C + s1)), dx[e, k][:, s0:s1])
 
-        def first_scatter(k, tag):
-            out_sb[k] = keep.tile([P, T], F32, name=f"out_sb{k}", tag=tag, align_bytes=64)
-            scatter_out(0, k)
-
-        gather_half(0, 0, "da0_low")
-        gather_half(0, 1, "da0_high")
-        gather_half(1, 0, "da1_low")
-        multiply(0, "dc0")
-        gather_half(1, 1, "dc1")
-        first_scatter(0, "dc2")
-        first_scatter(1, "dc3")
-        multiply(1, "da_w1")
-        first_scatter(2, "dc1")
-        first_scatter(3, f"da_bf{group_slots[1]}")
+        sigmoid_of(0, "gated0_2")
+        sigmoid_of(1, "gated2_0")
+        sigmoid_of(2, "gated2_2")
+        gather_dc(0)
+        quantise(0)
+        first_layer(0, 2, nc.scalar.copy)
+        first_layer(0, 0, nc.scalar.copy)
+        gather_dc(1, "a0")
+        quantise(1)
+        scatter_out("scalar", 0, 3, 0, C // 2)
+        scatter_out("scalar", 0, 2)
+        scatter_out("scalar", 0, 0)
+        scatter_out("scalar", 0, 1)
+        first_layer(1, 0, nc.scalar.copy)
+        gather_dc(2, "a1")
+        quantise(2)
+        first_layer(1, 2, nc.vector.tensor_copy)
+        scatter_out("scalar", 1, 0)
+        scatter_out("scalar", 1, 1)
+        scatter_out("vector", 0, 3, C // 2, C)
+        scatter_out("vector", 1, 2)
+        first_layer(2, 0, nc.scalar.copy)
+        first_layer(2, 2, nc.vector.tensor_copy)
+        scatter_out("vector", 1, 3)
         for k in range(PACK):
-            scatter_out(1, k)
-            nc.sync.dma_start(out[k * P : (k + 1) * P, :], out_sb[k][:])
+            engine = ["scalar", "vector"][k // 2]
+            scatter_out(engine, 2, k)
+            [nc.scalar, nc.sync][k // 2].dma_start(out[k * P : (k + 1) * P, :], out_sb[k][:])

@@ -30,9 +30,12 @@ def tile_moe_seb_silu_kernel(
     nc = tc.nc
     with ExitStack() as ctx:
         keep = ctx.enter_context(tc.tile_pool(name="keep", bufs=1))
+        head = ctx.enter_context(tc.tile_pool(name="head", bufs=1))
         psum = ctx.enter_context(tc.psum_pool(name="psum", bufs=8))
 
-        def tile(shape, dtype, name, tag=None):
+        def tile(shape, dtype, name, tag=None, offset=None):
+            if offset is not None:
+                return head.tile(shape, dtype, name=name, align_bytes=64, offset=offset)
             return keep.tile(shape, dtype, name=name, tag=tag or name, align_bytes=64)
 
         def entries(listed, s0, s1):
@@ -42,11 +45,10 @@ def tile_moe_seb_silu_kernel(
         list2 = keep.tile([P, T // PER_COLUMN], U16, name="list2")
         dy_w = tile([P, T], I32, "dy_w")
         dy_s = tile([P, T], U8, "dy_s")
-        w2_w_first = tile([P, 1, 2 * W], U8, "w2_w_first")
-        w2_s_first = tile([P, 1, W], U8, "w2_s_first")
-        w2_w_rest = tile([P, E - 1, 2 * W], U8, "w2_w_rest")
-        w2_s_rest = tile([P, E - 1, W], U8, "w2_s_rest")
-        a_sb = [tile([P, PACK, C], F32, f"a{e}") for e in range(E)]
+        w2_w_raw = tile([P, E, 2 * W], U8, "w2_w_raw")
+        w2_s_raw_first = tile([P, 1, W], U8, "w2_s_raw_first", offset=0)
+        w2_s_raw_rest = tile([P, E - 1, W], U8, "w2_s_raw_rest")
+        a_sb = tile([P, PACK, T], F32, "a_sb")
         g_sb = tile([P, T], F32, "g_sb")
         q_sb = tile([P, T], F32, "q_sb")
         a_planes = a.rearrange("(p t) w -> p t w", t=PACK)
@@ -66,39 +68,44 @@ def tile_moe_seb_silu_kernel(
                     rows[4 * quad : 4 * quad + 4, :].bitcast(I32).unsqueeze(0).to_broadcast([8, 4, words]),
                 )
 
-        nc.gpsimd.memset(w2_s_rest[:].rearrange("p e w -> p (e w)").bitcast(I32), 0)
+        nc.gpsimd.memset(w2_s_raw_rest[:].rearrange("p e w -> p (e w)").bitcast(I32), 0)
         load_scale_rows_repeated(dy_s, dy_scales[0])
         nc.sync.dma_start(list2[:], offs2)
         nc.sync.dma_start(dy_w[:], dy_words[0].rearrange("p t d -> p (t d)").bitcast(I32))
-        nc.sync.dma_start(w2_w_first[:, 0, :].bitcast(I32), w2t_words[0, 0].bitcast(I32))
-        nc.sync.dma_start(a_sb[0][:], a_planes[:, :, 0:C])
-        load_scale_rows_repeated(w2_s_first[:, 0, :], w2t_scales[0, 0])
+        nc.sync.dma_start(a_sb[:, 0, :], a_planes[:, 0, :])
+        nc.sync.dma_start(w2_w_raw[:].bitcast(I32), w2t_words[:, 0].rearrange("e p w -> p e w").bitcast(I32))
+        load_scale_rows_repeated(w2_s_raw_first[:, 0, :], w2t_scales[0, 0])
         nc.sync.dma_start(q_sb[:], gate2)
-        nc.sync.dma_start(w2_w_rest[:].bitcast(I32), w2t_words[1:E, 0].rearrange("e p w -> p e w").bitcast(I32))
         nc.sync.dma_start(g_sb[:], gate1)
+        for t in range(1, PACK):
+            nc.sync.dma_start(a_sb[:, t, :], a_planes[:, t, :])
         nc.sync.dma_start(list1[:], offs)
-        load_scale_rows(w2_s_rest, w2t_scales[1:E])
-        for e in range(1, E):
-            nc.sync.dma_start(a_sb[e][:], a_planes[:, :, e * C : (e + 1) * C])
+        load_scale_rows(w2_s_raw_rest, w2t_scales[1:E])
 
-        w2_w_raw = [w2_w_first[:, 0, :]] + [w2_w_rest[:, e - 1, :] for e in range(1, E)]
-        w2_s_raw = [w2_s_first[:, 0, :]] + [w2_s_rest[:, e - 1, :] for e in range(1, E)]
-        w2_w = [tile([P, PACK, P], U16, f"w2_w{e}") for e in range(E)]
-        w2_s = [tile([P, PACK, P], U8, f"w2_s{e}") for e in range(E)]
+        w2_w = {}
+        w2_s_first = tile([P, 1, PACK, P], U8, "w2_s_first")
+        w2_s_rest = tile([P, E - 1, PACK, P], U8, "w2_s_rest")
+        w2_s = [w2_s_first[:, 0]] + [w2_s_rest[:, e - 1] for e in range(1, E)]
+        first_planes = w2_s_raw_first[:].rearrange("p e (m t) -> p e t m", t=PACK)
+        rest_planes = w2_s_raw_rest[:].rearrange("p e (m t) -> p e t m", t=PACK)
 
-        def permute_words(e):
-            nc.gpsimd.tensor_copy(w2_w[e][:], w2_w_raw[e].bitcast(U16).rearrange("p (m t) -> p t m", t=PACK))
-
-        def permute_scales(e, t0, t1):
-            nc.gpsimd.tensor_copy(w2_s[e][:, t0:t1, :], w2_s_raw[e].rearrange("p (m t) -> p t m", t=PACK)[:, t0:t1, :])
+        def permute_words(e0, e1, offset=None):
+            planes = tile([P, e1 - e0, PACK, P], U16, f"w2_w{e0}", offset=offset)
+            nc.scalar.copy(planes[:], w2_w_raw[:, e0:e1].bitcast(U16).rearrange("p e (m t) -> p e t m", t=PACK))
+            for e in range(e0, e1):
+                w2_w[e] = planes[:, e - e0]
 
         slot_w = {}
         slot_s = {}
 
-        def gather_slots(e, tag_w=None, tag_s=None):
-            slot_w[e] = tile([P, C], U32, f"slot_w{e}", tag_w)
-            slot_s[e] = tile([P, C], U8, f"slot_s{e}", tag_s)
-            nc.vector.tensor_copy(slot_w[e][:], dy_w[:].bitcast(U32).indirect(entries(list2, e * C, (e + 1) * C)))
+        def gather_words(e0, e1):
+            words = tile([P, (e1 - e0) * C], U32, f"slot_w{e0}")
+            nc.vector.tensor_copy(words[:], dy_w[:].bitcast(U32).indirect(entries(list2, e0 * C, e1 * C)))
+            for e in range(e0, e1):
+                slot_w[e] = words[:, (e - e0) * C : (e - e0 + 1) * C]
+
+        def gather_scales(e, tag=None, offset=None):
+            slot_s[e] = tile([P, C], U8, f"slot_s{e}", tag, offset)
             nc.vector.tensor_copy(slot_s[e][:], dy_s[:].indirect(entries(list2, e * C, (e + 1) * C)))
 
         gated = {}
@@ -111,7 +118,7 @@ def tile_moe_seb_silu_kernel(
                     out=bank[:, t - t0, :],
                     lhsT=w2_w[e][:, t, :].bitcast(U8).bitcast(FP4X4),
                     lhsT_scale=w2_s[e][:, t, :],
-                    rhs=slot_w[e][:].bitcast(FP8X4),
+                    rhs=slot_w[e].bitcast(FP8X4),
                     rhs_scale=slot_s[e][:],
                     start=True,
                     stop=True,
@@ -132,143 +139,129 @@ def tile_moe_seb_silu_kernel(
             else:
                 nc.scalar.activation(window, values, ACT.Copy)
 
-        def scatter_dc(e, t):
-            scatter(["scalar", "vector"][t % 2], dc[t][:].indirect(entries(list2, e * C, (e + 1) * C)), gated[e, t])
+        def scatter_dc(engine, e, t, s0=0, s1=C):
+            scatter(engine, dc[t][:].indirect(entries(list2, e * C + s0, e * C + s1)), gated[e, t][:, s0:s1])
 
-        silu = {}
-        times_g = [tile([P, PACK, C], F32, f"times_g{e}") for e in range(E)]
+        times_g = tile([P, PACK, T], F32, "times_g")
 
-        def silu_of(e, tag=None):
-            silu[e] = tile([P, PACK, C], F32, f"silu{e}", tag)
-            nc.scalar.activation(silu[e][:], a_sb[e][:], ACT.Silu, scale=-1.0)
+        def factor(t, tag=None, tag_less=None):
+            silu = tile([P, T], F32, f"silu{t}", tag)
+            one_less = tile([P, T], F32, f"one_less{t}", tag_less)
+            nc.scalar.activation(silu[:], a_sb[:, t, :], ACT.Silu, scale=-1.0)
+            nc.gpsimd.tensor_scalar(one_less[:], silu[:], -1.0, 1.0, MULT, ADD)
+            nc.gpsimd.tensor_tensor(times_g[:, t, :], one_less[:], g_sb[:], MULT)
 
-        def factor_half(e, h):
-            planes = slice(2 * h, 2 * h + 2)
-            one_less = tile([P, 2, C], F32, f"one_less{e}_{h}")
-            nc.gpsimd.tensor_scalar(one_less[:], silu[e][:, planes, :], -1.0, 1.0, MULT, ADD)
-            nc.gpsimd.tensor_tensor(
-                times_g[e][:, planes, :],
-                one_less[:],
-                g_sb[:, e * C : (e + 1) * C].unsqueeze(1).to_broadcast([P, 2, C]),
-                MULT,
-            )
-
-        silu_of(0)
-        permute_words(0)
-        permute_scales(0, 0, 2)
-        permute_scales(0, 2, PACK)
-        gather_slots(0)
-        gather_slots(1)
+        gather_words(0, 1)
+        gather_scales(0)
+        permute_words(0, 1)
+        nc.vector.tensor_copy(w2_s_first[:, :, 0:2], first_planes[:, :, 0:2])
+        nc.vector.tensor_copy(w2_s_first[:, :, 2:PACK], first_planes[:, :, 2:PACK])
+        factor(0)
+        gather_words(1, E)
+        gather_scales(1, offset=0)
+        permute_words(1, E)
+        second_layer(0, 0, 1)
+        second_layer(0, 1, 2)
+        second_layer(0, 2, PACK)
+        gather_scales(2, "w2_s_first")
         for t in range(PACK):
-            second_layer(0, t, t + 1)
-        permute_words(1)
-        permute_scales(1, 0, PACK)
-        factor_half(0, 0)
-        scatter_dc(0, 0)
-        scatter_dc(0, 1)
-        gather_slots(2, "w2_w0", "w2_s0")
+            scatter_dc(["scalar", "vector"][t // 2], 0, t)
+        nc.gpsimd.tensor_copy(w2_s_rest[:], rest_planes)
+        factor(1, "gated0_0", "w2_s_raw_rest")
+        for t0 in (0, 2):
+            for e in range(1, E):
+                second_layer(e, t0, t0 + 2)
         w1_w = tile([P, E, W], I32, "w1_w", "dy_w")
         w1_s = tile([P, E, W], U8, "w1_s", "dy_s")
         nc.sync.dma_start(w1_w[:], w1t_words[:, 0].rearrange("e p k d -> p e (k d)").bitcast(I32))
         load_scale_rows(w1_s, w1t_scales)
-        second_layer(1, 0, 2)
-        second_layer(1, 2, PACK)
-        permute_words(2)
-        permute_scales(2, 0, PACK)
-        factor_half(0, 1)
-        scatter_dc(0, 2)
-        scatter_dc(0, 3)
-        silu_of(1, "gated0_0")
-        factor_half(1, 0)
-        factor_half(1, 1)
-        scatter_dc(1, 0)
-        scatter_dc(1, 1)
-        silu_of(2, "gated0_2")
-        factor_half(2, 0)
-        factor_half(2, 1)
-        second_layer(2, 0, 2)
-        second_layer(2, 2, PACK)
-        scatter_dc(1, 2)
-        scatter_dc(1, 3)
-        for t in range(PACK):
-            scatter_dc(2, t)
+        factor(2, "gated0_1", "gated0_0")
+        factor(3, "w2_w_raw", "gated0_1")
+        for e in range(1, E):
+            for t in range(PACK):
+                scatter_dc(["scalar", "vector"][t // 2], e, t)
 
-        sig = {}
+        sig = tile([P, T // 4, PACK, 4], F32, "sig", "gated2_0")
         picked = {}
-        da_bf = [tile([P, C, PACK], BF16, f"da_bf{e}") for e in range(E)]
         da_w = [tile([P, C], U32, f"da_w{e}") for e in range(E)]
         da_s = [tile([P, C], U8, f"da_s{e}") for e in range(E)]
         out_sb = [tile([P, T], F32, f"out_sb{k}") for k in range(PACK)]
-        dx = {}
 
-        def sigmoid_of(e, tag=None):
-            sig[e] = tile([P, PACK, C], F32, f"sig{e}", tag)
-            nc.scalar.activation(sig[e][:], a_sb[e][:], ACT.Sigmoid)
+        def sigmoid_of(e):
+            nc.scalar.activation(
+                sig[:, e * C // 4 : (e + 1) * C // 4],
+                a_sb[:, :, e * C : (e + 1) * C].rearrange("p t (c i) -> p c t i", i=4),
+                ACT.Sigmoid,
+            )
 
-        def gather_dc(e, tag=None):
-            picked[e] = tile([P, PACK, C], F32, f"picked{e}", tag)
-            for t in (0, 2, 1, 3):
+        def gather_dc(e0, e1, tag=None):
+            both = tile([P, PACK, (e1 - e0) * C], F32, f"picked{e0}", tag)
+            for t in range(PACK):
                 nc.vector.tensor_tensor(
-                    picked[e][:, t, :], dc[t][:].indirect(entries(list1, e * C, (e + 1) * C)), times_g[e][:, t, :], MULT
+                    both[:, t, :], dc[t][:].indirect(entries(list1, e0 * C, e1 * C)), times_g[:, t, e0 * C : e1 * C], MULT
+                )
+            for e in range(e0, e1):
+                picked[e] = both[:, :, (e - e0) * C : (e - e0 + 1) * C]
+
+        def quantise(parts):
+            rounded = [tile([P, s1 - s0, PACK], BF16, f"da_bf{e}_{s0}") for e, s0, s1 in parts]
+            for n, (e, s0, s1) in enumerate(parts):
+                nc.vector.tensor_tensor(
+                    rounded[n][:].rearrange("p (c i) t -> p c t i", i=4),
+                    picked[e][:, :, s0:s1].rearrange("p t (c i) -> p c t i", i=4),
+                    sig[:, (e * C + s0) // 4 : (e * C + s1) // 4],
+                    MULT,
+                )
+            for n, (e, s0, s1) in enumerate(parts):
+                nc.vector.quantize_mx(
+                    out=da_w[e][:, s0:s1].bitcast(FP8X4),
+                    scales=da_s[e][:, s0:s1],
+                    in_=rounded[n][:].rearrange("p n t -> p (n t)"),
                 )
 
-        def quantise(e):
-            nc.vector.tensor_tensor(
-                da_bf[e][:].rearrange("p (c i) t -> p c t i", i=4),
-                picked[e][:].rearrange("p t (c i) -> p c t i", i=4),
-                sig[e][:].rearrange("p t (c i) -> p c t i", i=4),
-                MULT,
-            )
-            nc.vector.quantize_mx(
-                out=da_w[e][:].bitcast(FP8X4), scales=da_s[e][:], in_=da_bf[e][:].rearrange("p n t -> p (n t)")
-            )
-
-        def first_layer(e, k0, copy):
-            bank = psum.tile([P, 2, C], F32, name="bank", tag="bank")
-            for k in range(k0, k0 + 2):
+        def first_layer(e, k0, k1, s0, s1, copy, into):
+            bank = psum.tile([P, k1 - k0, s1 - s0], F32, name="bank", tag="bank")
+            for k in range(k0, k1):
                 rows = slice(k * P, (k + 1) * P)
                 nc.tensor.matmul_mx(
                     out=bank[:, k - k0, :],
                     lhsT=w1_w[:, e, rows].bitcast(FP8X4),
                     lhsT_scale=w1_s[:, e, rows],
-                    rhs=da_w[e][:].bitcast(FP8X4),
-                    rhs_scale=da_s[e][:],
+                    rhs=da_w[e][:, s0:s1].bitcast(FP8X4),
+                    rhs_scale=da_s[e][:, s0:s1],
                     start=True,
                     stop=True,
                 )
-            sums = tile([P, 2, C], F32, f"dx{e}_{k0}")
-            copy(sums[:], bank[:])
-            for k in range(k0, k0 + 2):
-                dx[e, k] = sums[:, k - k0, :]
+            copy(into, bank[:])
 
-        def scatter_out(engine, e, k, s0=0, s1=C):
-            scatter(engine, out_sb[k][:].indirect(entries(list1, e * C + s0, e * C + s1)), dx[e, k][:, s0:s1])
+        def scatter_out(engine, e, k, values, s0=0, s1=C):
+            scatter(engine, out_sb[k][:].indirect(entries(list1, e * C + s0, e * C + s1)), values)
 
-        sigmoid_of(0, "gated0_2")
-        sigmoid_of(1, "gated2_0")
-        sigmoid_of(2, "gated2_2")
-        gather_dc(0)
-        quantise(0)
-        first_layer(0, 2, nc.scalar.copy)
-        first_layer(0, 0, nc.scalar.copy)
-        gather_dc(1, "a0")
-        quantise(1)
-        scatter_out("scalar", 0, 3, 0, C // 2)
-        scatter_out("scalar", 0, 2)
-        scatter_out("scalar", 0, 0)
-        scatter_out("scalar", 0, 1)
-        first_layer(1, 0, nc.scalar.copy)
-        gather_dc(2, "a1")
-        quantise(2)
-        first_layer(1, 2, nc.vector.tensor_copy)
-        scatter_out("scalar", 1, 0)
-        scatter_out("scalar", 1, 1)
-        scatter_out("vector", 0, 3, C // 2, C)
-        scatter_out("vector", 1, 2)
-        first_layer(2, 0, nc.scalar.copy)
-        first_layer(2, 2, nc.vector.tensor_copy)
-        scatter_out("vector", 1, 3)
-        for k in range(PACK):
-            engine = ["scalar", "vector"][k // 2]
-            scatter_out(engine, 2, k)
-            [nc.scalar, nc.sync][k // 2].dma_start(out[k * P : (k + 1) * P, :], out_sb[k][:])
+        def store(queue, k):
+            queue.dma_start(out[k * P : (k + 1) * P, :], out_sb[k][:])
+
+        half = C // 2
+        for e in range(E):
+            sigmoid_of(e)
+        gather_dc(0, 1)
+        quantise([(0, 0, half), (0, half, C)])
+        dx_first = tile([P, PACK, C], F32, "dx_first")
+        first_layer(0, 0, PACK, 0, half, nc.scalar.copy, dx_first[:, :, 0:half])
+        scatter_out("scalar", 0, 2, dx_first[:, 2, 0:half], 0, half)
+        first_layer(0, 0, PACK, half, C, nc.scalar.copy, dx_first[:, :, half:C])
+        gather_dc(1, 2, "da_bf0_0")
+        scatter_out("scalar", 0, 3, dx_first[:, 3, :])
+        scatter_out("scalar", 0, 2, dx_first[:, 2, half:C], half, C)
+        scatter_out("scalar", 0, 0, dx_first[:, 0, :])
+        scatter_out("scalar", 0, 1, dx_first[:, 1, :])
+        quantise([(1, 0, C)])
+        gather_dc(2, E, "da_bf0_0")
+        quantise([(2, 0, C)])
+        for e in range(1, E):
+            for k0, engine, copy, queue in ((0, "scalar", nc.scalar.copy, nc.scalar), (2, "vector", nc.vector.tensor_copy, nc.sync)):
+                dx = tile([P, 2, C], F32, f"dx{e}_{k0}", "da_bf0_0" if (e, k0) == (1, 2) else None)
+                first_layer(e, k0, k0 + 2, 0, C, copy, dx[:])
+                for k in range(k0, k0 + 2):
+                    scatter_out(engine, e, k, dx[:, k - k0, :])
+                    if e == E - 1:
+                        store(queue, k)

@@ -30,12 +30,9 @@ def tile_moe_seb_silu_kernel(
     nc = tc.nc
     with ExitStack() as ctx:
         keep = ctx.enter_context(tc.tile_pool(name="keep", bufs=1))
-        head = ctx.enter_context(tc.tile_pool(name="head", bufs=1))
         psum = ctx.enter_context(tc.psum_pool(name="psum", bufs=8))
 
-        def tile(shape, dtype, name, tag=None, offset=None):
-            if offset is not None:
-                return head.tile(shape, dtype, name=name, align_bytes=64, offset=offset)
+        def tile(shape, dtype, name, tag=None):
             return keep.tile(shape, dtype, name=name, tag=tag or name, align_bytes=64)
 
         def entries(listed, s0, s1):
@@ -46,7 +43,7 @@ def tile_moe_seb_silu_kernel(
         dy_w = tile([P, T], I32, "dy_w")
         dy_s = tile([P, T], U8, "dy_s")
         w2_w_raw = tile([P, E, 2 * W], U8, "w2_w_raw")
-        w2_s_raw_first = tile([P, 1, W], U8, "w2_s_raw_first", offset=0)
+        w2_s_raw_first = tile([P, 1, W], U8, "w2_s_raw_first")
         w2_s_raw_rest = tile([P, E - 1, W], U8, "w2_s_raw_rest")
         a_sb = tile([P, PACK, T], F32, "a_sb")
         g_sb = tile([P, T], F32, "g_sb")
@@ -89,8 +86,8 @@ def tile_moe_seb_silu_kernel(
         first_planes = w2_s_raw_first[:].rearrange("p e (m t) -> p e t m", t=PACK)
         rest_planes = w2_s_raw_rest[:].rearrange("p e (m t) -> p e t m", t=PACK)
 
-        def permute_words(e0, e1, offset=None):
-            planes = tile([P, e1 - e0, PACK, P], U16, f"w2_w{e0}", offset=offset)
+        def permute_words(e0, e1):
+            planes = tile([P, e1 - e0, PACK, P], U16, f"w2_w{e0}")
             nc.scalar.copy(planes[:], w2_w_raw[:, e0:e1].bitcast(U16).rearrange("p e (m t) -> p e t m", t=PACK))
             for e in range(e0, e1):
                 w2_w[e] = planes[:, e - e0]
@@ -104,14 +101,15 @@ def tile_moe_seb_silu_kernel(
             for e in range(e0, e1):
                 slot_w[e] = words[:, (e - e0) * C : (e - e0 + 1) * C]
 
-        def gather_scales(e, tag=None, offset=None):
-            slot_s[e] = tile([P, C], U8, f"slot_s{e}", tag, offset)
-            nc.vector.tensor_copy(slot_s[e][:], dy_s[:].indirect(entries(list2, e * C, (e + 1) * C)))
+        def gather_scales(e0, e1, tag=None):
+            scales = tile([P, (e1 - e0) * C], U8, f"slot_s{e0}", tag)
+            nc.vector.tensor_copy(scales[:], dy_s[:].indirect(entries(list2, e0 * C, e1 * C)))
+            for e in range(e0, e1):
+                slot_s[e] = scales[:, (e - e0) * C : (e - e0 + 1) * C]
 
-        gated = {}
-        dc = [tile([P, T], F32, f"dc{t}") for t in range(PACK)]
+        dc = {}
 
-        def second_layer(e, t0, t1):
+        def second_layer(e, t0, t1, into):
             bank = psum.tile([P, 2, C], F32, name="bank", tag="bank")
             for t in range(t0, t1):
                 nc.tensor.matmul_mx(
@@ -119,19 +117,16 @@ def tile_moe_seb_silu_kernel(
                     lhsT=w2_w[e][:, t, :].bitcast(U8).bitcast(FP4X4),
                     lhsT_scale=w2_s[e][:, t, :],
                     rhs=slot_w[e].bitcast(FP8X4),
-                    rhs_scale=slot_s[e][:],
+                    rhs_scale=slot_s[e],
                     start=True,
                     stop=True,
                 )
-            times_q = tile([P, t1 - t0, C], F32, f"gated{e}_{t0}")
             nc.vector.tensor_tensor(
-                times_q[:],
+                into,
                 bank[:, 0 : t1 - t0, :],
                 q_sb[:, e * C : (e + 1) * C].unsqueeze(1).to_broadcast([P, t1 - t0, C]),
                 MULT,
             )
-            for t in range(t0, t1):
-                gated[e, t] = times_q[:, t - t0, :]
 
         def scatter(engine, window, values):
             if engine == "vector":
@@ -139,8 +134,8 @@ def tile_moe_seb_silu_kernel(
             else:
                 nc.scalar.activation(window, values, ACT.Copy)
 
-        def scatter_dc(engine, e, t, s0=0, s1=C):
-            scatter(engine, dc[t][:].indirect(entries(list2, e * C + s0, e * C + s1)), gated[e, t][:, s0:s1])
+        def scatter_dc(engine, t, e0, e1, values):
+            scatter(engine, dc[t][:].indirect(entries(list2, e0 * C, e1 * C)), values)
 
         times_g = tile([P, PACK, T], F32, "times_g")
 
@@ -152,36 +147,45 @@ def tile_moe_seb_silu_kernel(
             nc.gpsimd.tensor_tensor(times_g[:, t, :], one_less[:], g_sb[:], MULT)
 
         gather_words(0, 1)
-        gather_scales(0)
+        gather_scales(0, 1)
         permute_words(0, 1)
         nc.vector.tensor_copy(w2_s_first[:, :, 0:2], first_planes[:, :, 0:2])
         nc.vector.tensor_copy(w2_s_first[:, :, 2:PACK], first_planes[:, :, 2:PACK])
         factor(0)
         gather_words(1, E)
-        gather_scales(1, offset=0)
+        gather_scales(1, E, "w2_s_raw_first")
         permute_words(1, E)
-        second_layer(0, 0, 1)
-        second_layer(0, 1, 2)
-        second_layer(0, 2, PACK)
-        gather_scales(2, "w2_s_first")
+        first = [tile([P, 1, C], F32, f"gated_first{t}") for t in range(2)]
+        for t in range(2):
+            second_layer(0, t, t + 1, first[t][:])
+        first_high = tile([P, 2, C], F32, "gated_first_high")
+        second_layer(0, 2, PACK, first_high[:])
         for t in range(PACK):
-            scatter_dc(["scalar", "vector"][t // 2], 0, t)
+            dc[t] = tile([P, T], F32, f"dc{t}", "one_less0" if t == 1 else None)
+        for t in range(2):
+            scatter_dc("scalar", t, 0, 1, first[t][:, 0, :])
+            scatter_dc("vector", 2 + t, 0, 1, first_high[:, t, :])
         nc.gpsimd.tensor_copy(w2_s_rest[:], rest_planes)
-        factor(1, "gated0_0", "w2_s_raw_rest")
-        for t0 in (0, 2):
-            for e in range(1, E):
-                second_layer(e, t0, t0 + 2)
+        factor(1, "w2_w_raw", "w2_s_raw_rest")
+        low = {e: tile([P, 2, C], F32, f"gated_low{e}") for e in range(1, E)}
+        high = tile([P, 2, (E - 1) * C], F32, "gated_high")
+        second_layer(1, 0, 2, low[1][:])
+        for e in range(1, E):
+            second_layer(e, 2, PACK, high[:, :, (e - 1) * C : e * C])
+        second_layer(2, 0, 2, low[2][:])
         w1_w = tile([P, E, W], I32, "w1_w", "dy_w")
         w1_s = tile([P, E, W], U8, "w1_s", "dy_s")
         nc.sync.dma_start(w1_w[:], w1t_words[:, 0].rearrange("e p k d -> p e (k d)").bitcast(I32))
         load_scale_rows(w1_s, w1t_scales)
-        factor(2, "gated0_1", "gated0_0")
-        factor(3, "w2_w_raw", "gated0_1")
+        factor(2, "gated_first0", "w2_w_raw")
+        factor(3, "gated_first1", "gated_first0")
+        for t in range(2):
+            scatter_dc("vector", 2 + t, 1, E, high[:, t, :])
         for e in range(1, E):
-            for t in range(PACK):
-                scatter_dc(["scalar", "vector"][t // 2], e, t)
+            for t in range(2):
+                scatter_dc("scalar", t, e, e + 1, low[e][:, t, :])
 
-        sig = tile([P, T // 4, PACK, 4], F32, "sig", "gated2_0")
+        sig = tile([P, T // 4, PACK, 4], F32, "sig", "gated_low2")
         picked = {}
         da_w = [tile([P, C], U32, f"da_w{e}") for e in range(E)]
         da_s = [tile([P, C], U8, f"da_s{e}") for e in range(E)]
@@ -257,11 +261,17 @@ def tile_moe_seb_silu_kernel(
         quantise([(1, 0, C)])
         gather_dc(2, E, "da_bf0_0")
         quantise([(2, 0, C)])
+        dx = {}
+        for e, k0, copy, tag in (
+            (1, 0, nc.scalar.copy, None),
+            (1, 2, nc.vector.tensor_copy, "da_bf0_0"),
+            (2, 2, nc.scalar.copy, None),
+            (2, 0, nc.scalar.copy, None),
+        ):
+            dx[e, k0] = tile([P, 2, C], F32, f"dx{e}_{k0}", tag)
+            first_layer(e, k0, k0 + 2, 0, C, copy, dx[e, k0][:])
         for e in range(1, E):
-            for k0, engine, copy, queue in ((0, "scalar", nc.scalar.copy, nc.scalar), (2, "vector", nc.vector.tensor_copy, nc.sync)):
-                dx = tile([P, 2, C], F32, f"dx{e}_{k0}", "da_bf0_0" if (e, k0) == (1, 2) else None)
-                first_layer(e, k0, k0 + 2, 0, C, copy, dx[:])
-                for k in range(k0, k0 + 2):
-                    scatter_out(engine, e, k, dx[:, k - k0, :])
-                    if e == E - 1:
-                        store(queue, k)
+            for k in range(PACK):
+                scatter_out(["scalar", "vector"][k // 2], e, k, dx[e, k - k % 2][:, k % 2, :])
+                if e == E - 1:
+                    store([nc.scalar, nc.sync][k // 2], k)

@@ -30,9 +30,13 @@ def tile_moe_seb_silu_kernel(
     nc = tc.nc
     with ExitStack() as ctx:
         keep = ctx.enter_context(tc.tile_pool(name="keep", bufs=1))
+        late = ctx.enter_context(tc.tile_pool(name="late", bufs=1))
+        chain = ctx.enter_context(tc.tile_pool(name="chain", bufs=1))
         psum = ctx.enter_context(tc.psum_pool(name="psum", bufs=8))
 
-        def tile(shape, dtype, name, tag=None):
+        def tile(shape, dtype, name, tag=None, offset=None):
+            if offset is not None:
+                return chain.tile(shape, dtype, name=name, align_bytes=64, offset=offset)
             return keep.tile(shape, dtype, name=name, tag=tag or name, align_bytes=64)
 
         def entries(listed, s0, s1):
@@ -43,11 +47,10 @@ def tile_moe_seb_silu_kernel(
         dy_w = tile([P, T], I32, "dy_w")
         dy_s = tile([P, T], U8, "dy_s")
         w2_w_raw = tile([P, E, 2 * W], U8, "w2_w_raw")
-        w2_s_raw_first = tile([P, 1, W], U8, "w2_s_raw_first")
+        a_first = tile([P, 1, T], F32, "a_first")
+        w2_s_raw_first = tile([P, 1, W], U8, "w2_s_raw_first", offset=0)
         w2_s_raw_rest = tile([P, E - 1, W], U8, "w2_s_raw_rest")
-        a_sb = tile([P, PACK, T], F32, "a_sb")
-        g_sb = tile([P, T], F32, "g_sb")
-        q_sb = tile([P, T], F32, "q_sb")
+        zero = late.tile([P, (PACK + 1) * T], I32, name="zero", offset=0)
         a_planes = a.rearrange("(p t) w -> p t w", t=PACK)
 
         def load_scale_rows(into, scales):
@@ -65,24 +68,33 @@ def tile_moe_seb_silu_kernel(
                     rows[4 * quad : 4 * quad + 4, :].bitcast(I32).unsqueeze(0).to_broadcast([8, 4, words]),
                 )
 
-        nc.gpsimd.memset(w2_s_raw_rest[:].rearrange("p e w -> p (e w)").bitcast(I32), 0)
+        nc.gpsimd.memset(zero[:, 0:1], 0)
+        nc.vector.tensor_copy(
+            w2_s_raw_rest[:].rearrange("p e w -> p (e w)").bitcast(I32),
+            zero[:, 0:1].to_broadcast([P, (E - 1) * W // 4]),
+        )
         load_scale_rows_repeated(dy_s, dy_scales[0])
         nc.sync.dma_start(list2[:], offs2)
         nc.sync.dma_start(dy_w[:], dy_words[0].rearrange("p t d -> p (t d)").bitcast(I32))
-        nc.sync.dma_start(a_sb[:, 0, :], a_planes[:, 0, :])
+        nc.sync.dma_start(a_first[:], a_planes[:, 0:1, :])
         nc.sync.dma_start(w2_w_raw[:].bitcast(I32), w2t_words[:, 0].rearrange("e p w -> p e w").bitcast(I32))
         load_scale_rows_repeated(w2_s_raw_first[:, 0, :], w2t_scales[0, 0])
-        nc.sync.dma_start(q_sb[:], gate2)
-        nc.sync.dma_start(g_sb[:], gate1)
-        for t in range(1, PACK):
-            nc.sync.dma_start(a_sb[:, t, :], a_planes[:, t, :])
         nc.sync.dma_start(list1[:], offs)
+        q_sb = late.tile([P, T], F32, name="q_sb", offset=0)
+        g_sb = late.tile([P, T], F32, name="g_sb", offset=4 * T)
+        a_rest = late.tile([P, PACK - 1, T], F32, name="a_rest", offset=8 * T)
+        nc.sync.dma_start(a_rest[:, 0, :], a_planes[:, 1, :])
+        nc.sync.dma_start(q_sb[:, 0:C], gate2[:, 0:C])
         load_scale_rows(w2_s_raw_rest, w2t_scales[1:E])
+        nc.sync.dma_start(g_sb[:], gate1)
+        for t in range(2, PACK):
+            nc.sync.dma_start(a_rest[:, t - 1, :], a_planes[:, t, :])
+        nc.sync.dma_start(q_sb[:, C:T], gate2[:, C:T])
+        a_sb = [a_first[:, 0, :]] + [a_rest[:, t - 1, :] for t in range(1, PACK)]
 
         w2_w = {}
         w2_s_first = tile([P, 1, PACK, P], U8, "w2_s_first")
-        w2_s_rest = tile([P, E - 1, PACK, P], U8, "w2_s_rest")
-        w2_s = [w2_s_first[:, 0]] + [w2_s_rest[:, e - 1] for e in range(1, E)]
+        w2_s = {0: w2_s_first[:, 0]}
         first_planes = w2_s_raw_first[:].rearrange("p e (m t) -> p e t m", t=PACK)
         rest_planes = w2_s_raw_rest[:].rearrange("p e (m t) -> p e t m", t=PACK)
 
@@ -101,13 +113,13 @@ def tile_moe_seb_silu_kernel(
             for e in range(e0, e1):
                 slot_w[e] = words[:, (e - e0) * C : (e - e0 + 1) * C]
 
-        def gather_scales(e0, e1, tag=None):
-            scales = tile([P, (e1 - e0) * C], U8, f"slot_s{e0}", tag)
+        def gather_scales(e0, e1, tag=None, offset=None):
+            scales = tile([P, (e1 - e0) * C], U8, f"slot_s{e0}", tag, offset)
             nc.vector.tensor_copy(scales[:], dy_s[:].indirect(entries(list2, e0 * C, e1 * C)))
             for e in range(e0, e1):
                 slot_s[e] = scales[:, (e - e0) * C : (e - e0 + 1) * C]
 
-        dc = {}
+        dc = [tile([P, T], F32, f"dc{t}") for t in range(PACK)]
 
         def second_layer(e, t0, t1, into):
             bank = psum.tile([P, 2, C], F32, name="bank", tag="bank")
@@ -139,10 +151,10 @@ def tile_moe_seb_silu_kernel(
 
         times_g = tile([P, PACK, T], F32, "times_g")
 
-        def factor(t, tag=None, tag_less=None):
+        def factor(t, tag=None, offset=None):
             silu = tile([P, T], F32, f"silu{t}", tag)
-            one_less = tile([P, T], F32, f"one_less{t}", tag_less)
-            nc.scalar.activation(silu[:], a_sb[:, t, :], ACT.Silu, scale=-1.0)
+            one_less = tile([P, T], F32, f"one_less{t}", offset=offset)
+            nc.scalar.activation(silu[:], a_sb[t], ACT.Silu, scale=-1.0)
             nc.gpsimd.tensor_scalar(one_less[:], silu[:], -1.0, 1.0, MULT, ADD)
             nc.gpsimd.tensor_tensor(times_g[:, t, :], one_less[:], g_sb[:], MULT)
 
@@ -151,52 +163,50 @@ def tile_moe_seb_silu_kernel(
         permute_words(0, 1)
         nc.vector.tensor_copy(w2_s_first[:, :, 0:2], first_planes[:, :, 0:2])
         nc.vector.tensor_copy(w2_s_first[:, :, 2:PACK], first_planes[:, :, 2:PACK])
-        factor(0)
+        factor(0, offset=C)
+        w2_s_rest = tile([P, E - 1, PACK, P], U8, "w2_s_rest", "silu0")
+        nc.gpsimd.tensor_copy(w2_s_rest[:], rest_planes)
+        for e in range(1, E):
+            w2_s[e] = w2_s_rest[:, e - 1]
         gather_words(1, E)
-        gather_scales(1, E, "w2_s_raw_first")
+        gather_scales(1, 2, offset=0)
         permute_words(1, E)
         first = [tile([P, 1, C], F32, f"gated_first{t}") for t in range(2)]
         for t in range(2):
             second_layer(0, t, t + 1, first[t][:])
         first_high = tile([P, 2, C], F32, "gated_first_high")
         second_layer(0, 2, PACK, first_high[:])
-        for t in range(PACK):
-            dc[t] = tile([P, T], F32, f"dc{t}", "one_less0" if t == 1 else None)
+        gather_scales(2, E, "w2_w0")
         for t in range(2):
             scatter_dc("scalar", t, 0, 1, first[t][:, 0, :])
             scatter_dc("vector", 2 + t, 0, 1, first_high[:, t, :])
-        nc.gpsimd.tensor_copy(w2_s_rest[:], rest_planes)
-        factor(1, "w2_w_raw", "w2_s_raw_rest")
-        low = {e: tile([P, 2, C], F32, f"gated_low{e}") for e in range(1, E)}
-        high = tile([P, 2, (E - 1) * C], F32, "gated_high")
-        second_layer(1, 0, 2, low[1][:])
-        for e in range(1, E):
-            second_layer(e, 2, PACK, high[:, :, (e - 1) * C : e * C])
-        second_layer(2, 0, 2, low[2][:])
+        factor(1)
+        rest = [tile([P, 2, (E - 1) * C], F32, f"gated_rest{h}") for h in range(2)]
+        for e, h in ((1, 0), (1, 1), (2, 1), (2, 0)):
+            second_layer(e, 2 * h, 2 * h + 2, rest[h][:, :, (e - 1) * C : e * C])
         w1_w = tile([P, E, W], I32, "w1_w", "dy_w")
         w1_s = tile([P, E, W], U8, "w1_s", "dy_s")
         nc.sync.dma_start(w1_w[:], w1t_words[:, 0].rearrange("e p k d -> p e (k d)").bitcast(I32))
         load_scale_rows(w1_s, w1t_scales)
-        factor(2, "gated_first0", "w2_w_raw")
-        factor(3, "gated_first1", "gated_first0")
-        for t in range(2):
-            scatter_dc("vector", 2 + t, 1, E, high[:, t, :])
+        factor(2, "gated_first0")
+        factor(3, "gated_first1")
         for e in range(1, E):
-            for t in range(2):
-                scatter_dc("scalar", t, e, e + 1, low[e][:, t, :])
+            for t in range(PACK):
+                scatter_dc(["scalar", "vector"][t // 2], t, e, e + 1, rest[t // 2][:, t % 2, (e - 1) * C : e * C])
 
-        sig = tile([P, T // 4, PACK, 4], F32, "sig", "gated_low2")
+        sig = tile([P, T // 4, PACK, 4], F32, "sig", "gated_rest0")
         picked = {}
         da_w = [tile([P, C], U32, f"da_w{e}") for e in range(E)]
         da_s = [tile([P, C], U8, f"da_s{e}") for e in range(E)]
         out_sb = [tile([P, T], F32, f"out_sb{k}") for k in range(PACK)]
 
-        def sigmoid_of(e):
-            nc.scalar.activation(
-                sig[:, e * C // 4 : (e + 1) * C // 4],
-                a_sb[:, :, e * C : (e + 1) * C].rearrange("p t (c i) -> p c t i", i=4),
-                ACT.Sigmoid,
-            )
+        def sigmoid_of(e0, e1):
+            for planes, t0, t1 in ((a_first, 0, 1), (a_rest, 1, PACK)):
+                nc.scalar.activation(
+                    sig[:, e0 * C // 4 : e1 * C // 4, t0:t1, :],
+                    planes[:, :, e0 * C : e1 * C].rearrange("p t (c i) -> p c t i", i=4),
+                    ACT.Sigmoid,
+                )
 
         def gather_dc(e0, e1, tag=None):
             both = tile([P, PACK, (e1 - e0) * C], F32, f"picked{e0}", tag)
@@ -245,8 +255,8 @@ def tile_moe_seb_silu_kernel(
             queue.dma_start(out[k * P : (k + 1) * P, :], out_sb[k][:])
 
         half = C // 2
-        for e in range(E):
-            sigmoid_of(e)
+        sigmoid_of(0, 1)
+        sigmoid_of(1, E)
         gather_dc(0, 1)
         quantise([(0, 0, half), (0, half, C)])
         dx_first = tile([P, PACK, C], F32, "dx_first")
@@ -265,7 +275,7 @@ def tile_moe_seb_silu_kernel(
         for e, k0, copy, tag in (
             (1, 0, nc.scalar.copy, None),
             (1, 2, nc.vector.tensor_copy, "da_bf0_0"),
-            (2, 2, nc.scalar.copy, None),
+            (2, 2, nc.vector.tensor_copy, None),
             (2, 0, nc.scalar.copy, None),
         ):
             dx[e, k0] = tile([P, 2, C], F32, f"dx{e}_{k0}", tag)

@@ -48,8 +48,8 @@ def tile_moe_seb_silu_kernel(
         dy_s = tile([P, T], U8, "dy_s")
         w2_w_raw = tile([P, E, 2 * W], U8, "w2_w_raw")
         a_first = tile([P, 1, T], F32, "a_first")
-        w2_s_raw_first = tile([P, 1, W], U8, "w2_s_raw_first", offset=0)
-        w2_s_raw_rest = tile([P, E - 1, W], U8, "w2_s_raw_rest")
+        w2_s_raw_first = tile([P, E - 1, W], U8, "w2_s_raw_first", offset=0)
+        w2_s_raw_last = tile([P, 1, W], U8, "w2_s_raw_last")
         zero = late.tile([P, (PACK + 1) * T], I32, name="zero", offset=0)
         a_planes = a.rearrange("(p t) w -> p t w", t=PACK)
 
@@ -69,23 +69,23 @@ def tile_moe_seb_silu_kernel(
                 )
 
         nc.gpsimd.memset(zero[:, 0:1], 0)
-        nc.vector.tensor_copy(
-            w2_s_raw_rest[:].rearrange("p e w -> p (e w)").bitcast(I32),
-            zero[:, 0:1].to_broadcast([P, (E - 1) * W // 4]),
-        )
+        for raw, experts in ((w2_s_raw_first, E - 1), (w2_s_raw_last, 1)):
+            nc.vector.tensor_copy(
+                raw[:].rearrange("p e w -> p (e w)").bitcast(I32), zero[:, 0:1].to_broadcast([P, experts * W // 4])
+            )
         load_scale_rows_repeated(dy_s, dy_scales[0])
         nc.sync.dma_start(list2[:], offs2)
         nc.sync.dma_start(dy_w[:], dy_words[0].rearrange("p t d -> p (t d)").bitcast(I32))
         nc.sync.dma_start(a_first[:], a_planes[:, 0:1, :])
         nc.sync.dma_start(w2_w_raw[:].bitcast(I32), w2t_words[:, 0].rearrange("e p w -> p e w").bitcast(I32))
-        load_scale_rows_repeated(w2_s_raw_first[:, 0, :], w2t_scales[0, 0])
         nc.sync.dma_start(list1[:], offs)
+        load_scale_rows(w2_s_raw_first, w2t_scales[0 : E - 1])
         q_sb = late.tile([P, T], F32, name="q_sb", offset=0)
         g_sb = late.tile([P, T], F32, name="g_sb", offset=4 * T)
         a_rest = late.tile([P, PACK - 1, T], F32, name="a_rest", offset=8 * T)
         nc.sync.dma_start(a_rest[:, 0, :], a_planes[:, 1, :])
         nc.sync.dma_start(q_sb[:, 0:C], gate2[:, 0:C])
-        load_scale_rows(w2_s_raw_rest, w2t_scales[1:E])
+        load_scale_rows(w2_s_raw_last, w2t_scales[E - 1 : E])
         nc.sync.dma_start(g_sb[:], gate1)
         for t in range(2, PACK):
             nc.sync.dma_start(a_rest[:, t - 1, :], a_planes[:, t, :])
@@ -93,10 +93,11 @@ def tile_moe_seb_silu_kernel(
         a_sb = [a_first[:, 0, :]] + [a_rest[:, t - 1, :] for t in range(1, PACK)]
 
         w2_w = {}
-        w2_s_first = tile([P, 1, PACK, P], U8, "w2_s_first")
-        w2_s = {0: w2_s_first[:, 0]}
-        first_planes = w2_s_raw_first[:].rearrange("p e (m t) -> p e t m", t=PACK)
-        rest_planes = w2_s_raw_rest[:].rearrange("p e (m t) -> p e t m", t=PACK)
+        w2_s = {}
+
+        def permute_scales(e, raw, engine, tag=None):
+            w2_s[e] = tile([P, PACK, P], U8, f"w2_s{e}", tag)
+            engine.tensor_copy(w2_s[e][:], raw.rearrange("p (m t) -> p t m", t=PACK))
 
         def permute_words(e0, e1):
             planes = tile([P, e1 - e0, PACK, P], U16, f"w2_w{e0}")
@@ -146,8 +147,8 @@ def tile_moe_seb_silu_kernel(
             else:
                 nc.scalar.activation(window, values, ACT.Copy)
 
-        def scatter_dc(engine, t, e0, e1, values):
-            scatter(engine, dc[t][:].indirect(entries(list2, e0 * C, e1 * C)), values)
+        def scatter_dc(engine, t, s0, s1, values):
+            scatter(engine, dc[t][:].indirect(entries(list2, s0, s1)), values)
 
         times_g = tile([P, PACK, T], F32, "times_g")
 
@@ -161,13 +162,10 @@ def tile_moe_seb_silu_kernel(
         gather_words(0, 1)
         gather_scales(0, 1)
         permute_words(0, 1)
-        nc.vector.tensor_copy(w2_s_first[:, :, 0:2], first_planes[:, :, 0:2])
-        nc.vector.tensor_copy(w2_s_first[:, :, 2:PACK], first_planes[:, :, 2:PACK])
+        for e in range(E - 1):
+            permute_scales(e, w2_s_raw_first[:, e, :], nc.vector)
         factor(0, offset=C)
-        w2_s_rest = tile([P, E - 1, PACK, P], U8, "w2_s_rest", "silu0")
-        nc.gpsimd.tensor_copy(w2_s_rest[:], rest_planes)
-        for e in range(1, E):
-            w2_s[e] = w2_s_rest[:, e - 1]
+        permute_scales(E - 1, w2_s_raw_last[:, 0, :], nc.gpsimd, "silu0")
         gather_words(1, E)
         gather_scales(1, 2, offset=0)
         permute_words(1, E)
@@ -177,9 +175,12 @@ def tile_moe_seb_silu_kernel(
         first_high = tile([P, 2, C], F32, "gated_first_high")
         second_layer(0, 2, PACK, first_high[:])
         gather_scales(2, E, "w2_w0")
+        half = C // 2
         for t in range(2):
-            scatter_dc("scalar", t, 0, 1, first[t][:, 0, :])
-            scatter_dc("vector", 2 + t, 0, 1, first_high[:, t, :])
+            scatter_dc("scalar", t, 0, C, first[t][:, 0, :])
+        scatter_dc("vector", 2, 0, half, first_high[:, 0, 0:half])
+        scatter_dc("vector", 3, 0, C, first_high[:, 1, :])
+        scatter_dc("scalar", 2, half, C, first_high[:, 0, half:C])
         factor(1)
         rest = [tile([P, 2, (E - 1) * C], F32, f"gated_rest{h}") for h in range(2)]
         for e, h in ((1, 0), (1, 1), (2, 1), (2, 0)):
@@ -192,7 +193,7 @@ def tile_moe_seb_silu_kernel(
         factor(3, "gated_first1")
         for e in range(1, E):
             for t in range(PACK):
-                scatter_dc(["scalar", "vector"][t // 2], t, e, e + 1, rest[t // 2][:, t % 2, (e - 1) * C : e * C])
+                scatter_dc(["scalar", "vector"][t // 2], t, e * C, (e + 1) * C, rest[t // 2][:, t % 2, (e - 1) * C : e * C])
 
         sig = tile([P, T // 4, PACK, 4], F32, "sig", "gated_rest0")
         picked = {}
@@ -200,13 +201,12 @@ def tile_moe_seb_silu_kernel(
         da_s = [tile([P, C], U8, f"da_s{e}") for e in range(E)]
         out_sb = [tile([P, T], F32, f"out_sb{k}") for k in range(PACK)]
 
-        def sigmoid_of(e0, e1):
-            for planes, t0, t1 in ((a_first, 0, 1), (a_rest, 1, PACK)):
-                nc.scalar.activation(
-                    sig[:, e0 * C // 4 : e1 * C // 4, t0:t1, :],
-                    planes[:, :, e0 * C : e1 * C].rearrange("p t (c i) -> p c t i", i=4),
-                    ACT.Sigmoid,
-                )
+        def sigmoid_of(planes, t0, t1, s0, s1):
+            nc.scalar.activation(
+                sig[:, s0 // 4 : s1 // 4, t0:t1, :],
+                planes[:, :, s0:s1].rearrange("p t (c i) -> p c t i", i=4),
+                ACT.Sigmoid,
+            )
 
         def gather_dc(e0, e1, tag=None):
             both = tile([P, PACK, (e1 - e0) * C], F32, f"picked{e0}", tag)
@@ -254,9 +254,11 @@ def tile_moe_seb_silu_kernel(
         def store(queue, k):
             queue.dma_start(out[k * P : (k + 1) * P, :], out_sb[k][:])
 
-        half = C // 2
-        sigmoid_of(0, 1)
-        sigmoid_of(1, E)
+        sigmoid_of(a_first, 0, 1, 0, C)
+        sigmoid_of(a_rest, 1, PACK, 0, half)
+        sigmoid_of(a_rest, 1, PACK, half, C)
+        sigmoid_of(a_first, 0, 1, C, T)
+        sigmoid_of(a_rest, 1, PACK, C, T)
         gather_dc(0, 1)
         quantise([(0, 0, half), (0, half, C)])
         dx_first = tile([P, PACK, C], F32, "dx_first")

@@ -31,12 +31,9 @@ def tile_moe_seb_silu_kernel(
     with ExitStack() as ctx:
         keep = ctx.enter_context(tc.tile_pool(name="keep", bufs=1))
         late = ctx.enter_context(tc.tile_pool(name="late", bufs=1))
-        chain = ctx.enter_context(tc.tile_pool(name="chain", bufs=1))
         psum = ctx.enter_context(tc.psum_pool(name="psum", bufs=8))
 
-        def tile(shape, dtype, name, tag=None, offset=None):
-            if offset is not None:
-                return chain.tile(shape, dtype, name=name, align_bytes=64, offset=offset)
+        def tile(shape, dtype, name, tag=None):
             return keep.tile(shape, dtype, name=name, tag=tag or name, align_bytes=64)
 
         def entries(listed, s0, s1):
@@ -48,8 +45,7 @@ def tile_moe_seb_silu_kernel(
         dy_s = tile([P, T], U8, "dy_s")
         w2_w_raw = tile([P, E, 2 * W], U8, "w2_w_raw")
         a_first = tile([P, 1, T], F32, "a_first")
-        w2_s_raw_first = tile([P, E - 1, W], U8, "w2_s_raw_first", offset=0)
-        w2_s_raw_last = tile([P, 1, W], U8, "w2_s_raw_last")
+        w2_s_raw = tile([P, E, W], U8, "w2_s_raw")
         zero = late.tile([P, (PACK + 1) * T], I32, name="zero", offset=0)
         a_planes = a.rearrange("(p t) w -> p t w", t=PACK)
 
@@ -69,23 +65,21 @@ def tile_moe_seb_silu_kernel(
                 )
 
         nc.gpsimd.memset(zero[:, 0:1], 0)
-        for raw, experts in ((w2_s_raw_first, E - 1), (w2_s_raw_last, 1)):
-            nc.vector.tensor_copy(
-                raw[:].rearrange("p e w -> p (e w)").bitcast(I32), zero[:, 0:1].to_broadcast([P, experts * W // 4])
-            )
+        nc.vector.tensor_copy(
+            w2_s_raw[:].rearrange("p e w -> p (e w)").bitcast(I32), zero[:, 0:1].to_broadcast([P, E * W // 4])
+        )
         load_scale_rows_repeated(dy_s, dy_scales[0])
         nc.sync.dma_start(list2[:], offs2)
         nc.sync.dma_start(dy_w[:], dy_words[0].rearrange("p t d -> p (t d)").bitcast(I32))
         nc.sync.dma_start(a_first[:], a_planes[:, 0:1, :])
         nc.sync.dma_start(w2_w_raw[:].bitcast(I32), w2t_words[:, 0].rearrange("e p w -> p e w").bitcast(I32))
         nc.sync.dma_start(list1[:], offs)
-        load_scale_rows(w2_s_raw_first, w2t_scales[0 : E - 1])
+        load_scale_rows(w2_s_raw, w2t_scales)
         q_sb = late.tile([P, T], F32, name="q_sb", offset=0)
         g_sb = late.tile([P, T], F32, name="g_sb", offset=4 * T)
         a_rest = late.tile([P, PACK - 1, T], F32, name="a_rest", offset=8 * T)
         nc.sync.dma_start(a_rest[:, 0, :], a_planes[:, 1, :])
         nc.sync.dma_start(q_sb[:, 0:C], gate2[:, 0:C])
-        load_scale_rows(w2_s_raw_last, w2t_scales[E - 1 : E])
         nc.sync.dma_start(g_sb[:], gate1)
         for t in range(2, PACK):
             nc.sync.dma_start(a_rest[:, t - 1, :], a_planes[:, t, :])
@@ -93,11 +87,11 @@ def tile_moe_seb_silu_kernel(
         a_sb = [a_first[:, 0, :]] + [a_rest[:, t - 1, :] for t in range(1, PACK)]
 
         w2_w = {}
-        w2_s = {}
+        w2_s = [tile([P, PACK, P], U8, f"w2_s{e}") for e in range(E)]
 
-        def permute_scales(e, raw, engine, tag=None):
-            w2_s[e] = tile([P, PACK, P], U8, f"w2_s{e}", tag)
-            engine.tensor_copy(w2_s[e][:], raw.rearrange("p (m t) -> p t m", t=PACK))
+        def permute_scales(e, t0, t1):
+            planes = w2_s_raw[:, e, :].rearrange("p (m t) -> p t m", t=PACK)
+            nc.gpsimd.tensor_copy(w2_s[e][:, t0:t1, :], planes[:, t0:t1, :])
 
         def permute_words(e0, e1):
             planes = tile([P, e1 - e0, PACK, P], U16, f"w2_w{e0}")
@@ -114,8 +108,8 @@ def tile_moe_seb_silu_kernel(
             for e in range(e0, e1):
                 slot_w[e] = words[:, (e - e0) * C : (e - e0 + 1) * C]
 
-        def gather_scales(e0, e1, tag=None, offset=None):
-            scales = tile([P, (e1 - e0) * C], U8, f"slot_s{e0}", tag, offset)
+        def gather_scales(e0, e1):
+            scales = tile([P, (e1 - e0) * C], U8, f"slot_s{e0}")
             nc.vector.tensor_copy(scales[:], dy_s[:].indirect(entries(list2, e0 * C, e1 * C)))
             for e in range(e0, e1):
                 slot_s[e] = scales[:, (e - e0) * C : (e - e0 + 1) * C]
@@ -152,9 +146,9 @@ def tile_moe_seb_silu_kernel(
 
         times_g = tile([P, PACK, T], F32, "times_g")
 
-        def factor(t, tag=None, offset=None):
+        def factor(t, tag=None, tag_less=None):
             silu = tile([P, T], F32, f"silu{t}", tag)
-            one_less = tile([P, T], F32, f"one_less{t}", offset=offset)
+            one_less = tile([P, T], F32, f"one_less{t}", tag_less)
             nc.scalar.activation(silu[:], a_sb[t], ACT.Silu, scale=-1.0)
             nc.gpsimd.tensor_scalar(one_less[:], silu[:], -1.0, 1.0, MULT, ADD)
             nc.gpsimd.tensor_tensor(times_g[:, t, :], one_less[:], g_sb[:], MULT)
@@ -162,19 +156,20 @@ def tile_moe_seb_silu_kernel(
         gather_words(0, 1)
         gather_scales(0, 1)
         permute_words(0, 1)
-        for e in range(E - 1):
-            permute_scales(e, w2_s_raw_first[:, e, :], nc.vector)
-        factor(0, offset=C)
-        permute_scales(E - 1, w2_s_raw_last[:, 0, :], nc.gpsimd, "silu0")
+        permute_scales(0, 0, 2)
+        permute_scales(0, 2, PACK)
+        for e in range(1, E):
+            permute_scales(e, 0, PACK)
+        factor(0, None, "w2_s_raw")
         gather_words(1, E)
-        gather_scales(1, 2, offset=0)
+        gather_scales(1, 2)
+        gather_scales(2, E)
         permute_words(1, E)
         first = [tile([P, 1, C], F32, f"gated_first{t}") for t in range(2)]
         for t in range(2):
             second_layer(0, t, t + 1, first[t][:])
         first_high = tile([P, 2, C], F32, "gated_first_high")
         second_layer(0, 2, PACK, first_high[:])
-        gather_scales(2, E, "w2_w0")
         half = C // 2
         for t in range(2):
             scatter_dc("scalar", t, 0, C, first[t][:, 0, :])

@@ -95,7 +95,10 @@ def tile_moe_seb_silu_kernel(
 
         def permute_words(e0, e1):
             planes = tile([P, e1 - e0, PACK, P], U16, f"w2_w{e0}")
-            nc.scalar.copy(planes[:], w2_w_raw[:, e0:e1].bitcast(U16).rearrange("p e (m t) -> p e t m", t=PACK))
+            nc.scalar.copy(
+                planes[:].rearrange("p e t (c i) -> p e c t i", i=4),
+                w2_w_raw[:, e0:e1].bitcast(U16).rearrange("p e (c i t) -> p e c t i", i=4, t=PACK),
+            )
             for e in range(e0, e1):
                 w2_w[e] = planes[:, e - e0]
 
@@ -177,9 +180,11 @@ def tile_moe_seb_silu_kernel(
         scatter_dc("vector", 3, 0, C, first_high[:, 1, :])
         scatter_dc("scalar", 2, half, C, first_high[:, 0, half:C])
         factor(1)
-        rest = [tile([P, 2, (E - 1) * C], F32, f"gated_rest{h}") for h in range(2)]
-        for e, h in ((1, 0), (1, 1), (2, 1), (2, 0)):
-            second_layer(e, 2 * h, 2 * h + 2, rest[h][:, :, (e - 1) * C : e * C])
+        rest = {}
+        for h in range(2):
+            for e in range(1, E):
+                rest[e, h] = tile([P, 2, C], F32, f"gated{e}_{h}")
+                second_layer(e, 2 * h, 2 * h + 2, rest[e, h][:])
         w1_w = tile([P, E, W], I32, "w1_w", "dy_w")
         w1_s = tile([P, E, W], U8, "w1_s", "dy_s")
         nc.sync.dma_start(w1_w[:], w1t_words[:, 0].rearrange("e p k d -> p e (k d)").bitcast(I32))
@@ -188,9 +193,9 @@ def tile_moe_seb_silu_kernel(
         factor(3, "gated_first1")
         for e in range(1, E):
             for t in range(PACK):
-                scatter_dc(["scalar", "vector"][t // 2], t, e * C, (e + 1) * C, rest[t // 2][:, t % 2, (e - 1) * C : e * C])
+                scatter_dc(["scalar", "vector"][t // 2], t, e * C, (e + 1) * C, rest[e, t // 2][:, t % 2, :])
 
-        sig = tile([P, T // 4, PACK, 4], F32, "sig", "gated_rest0")
+        sig = tile([P, T // 4, PACK, 4], F32, "sig", "gated1_0")
         picked = {}
         da_w = [tile([P, C], U32, f"da_w{e}") for e in range(E)]
         da_s = [tile([P, C], U8, f"da_s{e}") for e in range(E)]

@@ -169,11 +169,12 @@ def tile_moe_seb_silu_kernel(
         gather_scales(2, E)
         permute_words(1, E)
         first = [tile([P, 1, C], F32, f"gated_first{t}") for t in range(2)]
-        for t in range(2):
-            second_layer(0, t, t + 1, first[t][:])
         first_high = tile([P, 2, C], F32, "gated_first_high")
+        second_layer(0, 0, 1, first[0][:])
         second_layer(0, 2, PACK, first_high[:])
+        second_layer(0, 1, 2, first[1][:])
         half = C // 2
+        halves = [(0, half), (half, C)]
         for t in range(2):
             scatter_dc("scalar", t, 0, C, first[t][:, 0, :])
         scatter_dc("vector", 2, 0, half, first_high[:, 0, 0:half])
@@ -197,6 +198,8 @@ def tile_moe_seb_silu_kernel(
 
         sig = tile([P, T // 4, PACK, 4], F32, "sig", "gated1_0")
         picked = {}
+        rounded = {}
+        dx = {}
         da_w = [tile([P, C], U32, f"da_w{e}") for e in range(E)]
         da_s = [tile([P, C], U8, f"da_s{e}") for e in range(E)]
         out_sb = [tile([P, T], F32, f"out_sb{k}") for k in range(PACK)]
@@ -208,37 +211,41 @@ def tile_moe_seb_silu_kernel(
                 ACT.Sigmoid,
             )
 
-        def gather_dc(e0, e1, tag=None):
-            both = tile([P, PACK, (e1 - e0) * C], F32, f"picked{e0}", tag)
+        def gather_dc(e, parts, tag=None):
+            picked[e] = tile([P, PACK, C], F32, f"picked{e}", tag)
             for t in range(PACK):
-                nc.vector.tensor_tensor(
-                    both[:, t, :], dc[t][:].indirect(entries(list1, e0 * C, e1 * C)), times_g[:, t, e0 * C : e1 * C], MULT
-                )
-            for e in range(e0, e1):
-                picked[e] = both[:, :, (e - e0) * C : (e - e0 + 1) * C]
+                for s0, s1 in parts:
+                    slots = slice(e * C + s0, e * C + s1)
+                    nc.vector.tensor_tensor(
+                        picked[e][:, t, s0:s1],
+                        dc[t][:].indirect(entries(list1, slots.start, slots.stop)),
+                        times_g[:, t, slots],
+                        MULT,
+                    )
 
-        def quantise(parts):
-            rounded = [tile([P, s1 - s0, PACK], BF16, f"da_bf{e}_{s0}") for e, s0, s1 in parts]
-            for n, (e, s0, s1) in enumerate(parts):
-                nc.vector.tensor_tensor(
-                    rounded[n][:].rearrange("p (c i) t -> p c t i", i=4),
-                    picked[e][:, :, s0:s1].rearrange("p t (c i) -> p c t i", i=4),
-                    sig[:, (e * C + s0) // 4 : (e * C + s1) // 4],
-                    MULT,
-                )
-            for n, (e, s0, s1) in enumerate(parts):
-                nc.vector.quantize_mx(
-                    out=da_w[e][:, s0:s1].bitcast(FP8X4),
-                    scales=da_s[e][:, s0:s1],
-                    in_=rounded[n][:].rearrange("p n t -> p (n t)"),
-                )
+        def round_da(e, s0, s1):
+            rounded[e, s0] = tile([P, s1 - s0, PACK], BF16, f"da_bf{e}_{s0}")
+            nc.vector.tensor_tensor(
+                rounded[e, s0][:].rearrange("p (c i) t -> p c t i", i=4),
+                picked[e][:, :, s0:s1].rearrange("p t (c i) -> p c t i", i=4),
+                sig[:, (e * C + s0) // 4 : (e * C + s1) // 4],
+                MULT,
+            )
 
-        def first_layer(e, k0, k1, s0, s1, copy, into):
-            bank = psum.tile([P, k1 - k0, s1 - s0], F32, name="bank", tag="bank")
-            for k in range(k0, k1):
+        def quantise(e, s0, s1):
+            nc.vector.quantize_mx(
+                out=da_w[e][:, s0:s1].bitcast(FP8X4),
+                scales=da_s[e][:, s0:s1],
+                in_=rounded[e, s0][:].rearrange("p n t -> p (n t)"),
+            )
+
+        def first_layer(blocks, s0, s1, copy):
+            bank = psum.tile([P, len(blocks), s1 - s0], F32, name="bank", tag="bank")
+            sums = tile([P, len(blocks), s1 - s0], F32, f"dx{blocks[0][0]}_{blocks[0][1]}_{s0}")
+            for n, (e, k) in enumerate(blocks):
                 rows = slice(k * P, (k + 1) * P)
                 nc.tensor.matmul_mx(
-                    out=bank[:, k - k0, :],
+                    out=bank[:, n, :],
                     lhsT=w1_w[:, e, rows].bitcast(FP8X4),
                     lhsT_scale=w1_s[:, e, rows],
                     rhs=da_w[e][:, s0:s1].bitcast(FP8X4),
@@ -246,10 +253,11 @@ def tile_moe_seb_silu_kernel(
                     start=True,
                     stop=True,
                 )
-            copy(into, bank[:])
+                dx[e, k, s0] = sums[:, n, :]
+            copy(sums[:], bank[:])
 
-        def scatter_out(engine, e, k, values, s0=0, s1=C):
-            scatter(engine, out_sb[k][:].indirect(entries(list1, e * C + s0, e * C + s1)), values)
+        def scatter_out(engine, e, k, s0=0, s1=C):
+            scatter(engine, out_sb[k][:].indirect(entries(list1, e * C + s0, e * C + s1)), dx[e, k, s0])
 
         def store(queue, k):
             queue.dma_start(out[k * P : (k + 1) * P, :], out_sb[k][:])
@@ -259,31 +267,35 @@ def tile_moe_seb_silu_kernel(
         sigmoid_of(a_rest, 1, PACK, half, C)
         sigmoid_of(a_first, 0, 1, C, T)
         sigmoid_of(a_rest, 1, PACK, C, T)
-        gather_dc(0, 1)
-        quantise([(0, 0, half), (0, half, C)])
-        dx_first = tile([P, PACK, C], F32, "dx_first")
-        first_layer(0, 0, PACK, 0, half, nc.scalar.copy, dx_first[:, :, 0:half])
-        scatter_out("scalar", 0, 2, dx_first[:, 2, 0:half], 0, half)
-        first_layer(0, 0, PACK, half, C, nc.scalar.copy, dx_first[:, :, half:C])
-        gather_dc(1, 2, "da_bf0_0")
-        scatter_out("scalar", 0, 3, dx_first[:, 3, :])
-        scatter_out("scalar", 0, 2, dx_first[:, 2, half:C], half, C)
-        scatter_out("scalar", 0, 0, dx_first[:, 0, :])
-        scatter_out("scalar", 0, 1, dx_first[:, 1, :])
-        quantise([(1, 0, C)])
-        gather_dc(2, E, "da_bf0_0")
-        quantise([(2, 0, C)])
-        dx = {}
-        for e, k0, copy, tag in (
-            (1, 0, nc.scalar.copy, None),
-            (1, 2, nc.vector.tensor_copy, "da_bf0_0"),
-            (2, 2, nc.vector.tensor_copy, None),
-            (2, 0, nc.scalar.copy, None),
-        ):
-            dx[e, k0] = tile([P, 2, C], F32, f"dx{e}_{k0}", tag)
-            first_layer(e, k0, k0 + 2, 0, C, copy, dx[e, k0][:])
-        for e in range(1, E):
-            for k in range(PACK):
-                scatter_out(["scalar", "vector"][k // 2], e, k, dx[e, k - k % 2][:, k % 2, :])
-                if e == E - 1:
-                    store([nc.scalar, nc.sync][k // 2], k)
+        gather_dc(0, halves)
+        for s0, s1 in halves:
+            round_da(0, s0, s1)
+        quantise(0, 0, half)
+        first_layer([(0, 2), (0, 3)], 0, half, nc.scalar.copy)
+        first_layer([(0, 0), (0, 1)], 0, half, nc.scalar.copy)
+        for k in (2, 3, 0, 1):
+            scatter_out("scalar", 0, k, 0, half)
+        gather_dc(1, [(0, C)], "picked0")
+        quantise(0, half, C)
+        first_layer([(0, k) for k in (2, 3, 0, 1)], half, C, nc.scalar.copy)
+        for k in (2, 3, 0, 1):
+            scatter_out("scalar", 0, k, half, C)
+        round_da(1, 0, C)
+        gather_dc(2, [(0, C)], f"da_bf0_{half}")
+        quantise(1, 0, C)
+        round_da(2, 0, C)
+        first_layer([(1, 2)], 0, C, nc.vector.tensor_copy)
+        for k in range(2):
+            first_layer([(1, k)], 0, C, nc.scalar.copy)
+        quantise(2, 0, C)
+        scatter_out("vector", 1, 2)
+        first_layer([(1, 3), (2, 2)], 0, C, nc.vector.tensor_copy)
+        first_layer([(2, 3)], 0, C, nc.vector.tensor_copy)
+        for k in range(2):
+            scatter_out("scalar", 1, k)
+        for k in range(2):
+            first_layer([(2, k)], 0, C, nc.scalar.copy)
+        scatter_out("vector", 1, 3)
+        for k in range(PACK):
+            scatter_out(["scalar", "vector"][k // 2], 2, k)
+            store([nc.scalar, nc.sync][k // 2], k)

@@ -68,9 +68,9 @@ def tile_moe_seb_silu_kernel(
         nc.vector.tensor_copy(
             w2_s_raw[:].rearrange("p e w -> p (e w)").bitcast(I32), zero[:, 0:1].to_broadcast([P, E * W // 4])
         )
-        load_scale_rows_repeated(dy_s, dy_scales[0])
+        nc.scalar.dma_start(dy_w[:], dy_words[0].rearrange("p t d -> p (t d)").bitcast(I32))
         nc.sync.dma_start(list2[:], offs2)
-        nc.sync.dma_start(dy_w[:], dy_words[0].rearrange("p t d -> p (t d)").bitcast(I32))
+        load_scale_rows_repeated(dy_s, dy_scales[0])
         nc.sync.dma_start(a_first[:], a_planes[:, 0:1, :])
         nc.sync.dma_start(w2_w_raw[:].bitcast(I32), w2t_words[:, 0].rearrange("e p w -> p e w").bitcast(I32))
         nc.sync.dma_start(list1[:], offs)
@@ -87,11 +87,11 @@ def tile_moe_seb_silu_kernel(
         a_sb = [a_first[:, 0, :]] + [a_rest[:, t - 1, :] for t in range(1, PACK)]
 
         w2_w = {}
-        w2_s = [tile([P, PACK, P], U8, f"w2_s{e}") for e in range(E)]
+        w2_s = tile([P, E, PACK, P], U8, "w2_s")
 
-        def permute_scales(e, t0, t1):
-            planes = w2_s_raw[:, e, :].rearrange("p (m t) -> p t m", t=PACK)
-            nc.gpsimd.tensor_copy(w2_s[e][:, t0:t1, :], planes[:, t0:t1, :])
+        def permute_scales(e0, e1, t0, t1):
+            planes = w2_s_raw[:].rearrange("p e (m t) -> p e t m", t=PACK)
+            nc.gpsimd.tensor_copy(w2_s[:, e0:e1, t0:t1, :], planes[:, e0:e1, t0:t1, :])
 
         def permute_words(e0, e1):
             planes = tile([P, e1 - e0, PACK, P], U16, f"w2_w{e0}")
@@ -125,7 +125,7 @@ def tile_moe_seb_silu_kernel(
                 nc.tensor.matmul_mx(
                     out=bank[:, t - t0, :],
                     lhsT=w2_w[e][:, t, :].bitcast(U8).bitcast(FP4X4),
-                    lhsT_scale=w2_s[e][:, t, :],
+                    lhsT_scale=w2_s[:, e, t, :],
                     rhs=slot_w[e].bitcast(FP8X4),
                     rhs_scale=slot_s[e],
                     start=True,
@@ -149,21 +149,28 @@ def tile_moe_seb_silu_kernel(
 
         times_g = tile([P, PACK, T], F32, "times_g")
 
-        def factor(t, tag=None, tag_less=None):
-            silu = tile([P, T], F32, f"silu{t}", tag)
-            one_less = tile([P, T], F32, f"one_less{t}", tag_less)
-            nc.scalar.activation(silu[:], a_sb[t], ACT.Silu, scale=-1.0)
-            nc.gpsimd.tensor_scalar(one_less[:], silu[:], -1.0, 1.0, MULT, ADD)
-            nc.gpsimd.tensor_tensor(times_g[:, t, :], one_less[:], g_sb[:], MULT)
+        def silu_of(t, into):
+            nc.scalar.activation(into[:, 0, :], a_sb[t], ACT.Silu, scale=-1.0)
+
+        one_less = {}
+
+        def one_less_silu(t0, t1, silu, tag):
+            one_less[t0] = tile([P, t1 - t0, T], F32, f"one_less{t0}", tag)
+            nc.gpsimd.tensor_scalar(one_less[t0][:], silu, -1.0, 1.0, MULT, ADD)
+
+        def times_gate1(t0, t1):
+            nc.gpsimd.tensor_tensor(
+                times_g[:, t0:t1, :], one_less[t0][:], g_sb[:].unsqueeze(1).to_broadcast([P, t1 - t0, T]), MULT
+            )
 
         gather_words(0, 1)
         gather_scales(0, 1)
         permute_words(0, 1)
-        permute_scales(0, 0, 2)
-        permute_scales(0, 2, PACK)
-        for e in range(1, E):
-            permute_scales(e, 0, PACK)
-        factor(0, None, "w2_s_raw")
+        permute_scales(0, 1, 0, 2)
+        permute_scales(0, 1, 2, PACK)
+        permute_scales(1, E, 0, PACK)
+        silu_low = tile([P, 2, T], F32, "silu_low")
+        silu_of(0, silu_low[:, 0:1, :])
         gather_words(1, E)
         gather_scales(1, 2)
         gather_scales(2, E)
@@ -180,7 +187,9 @@ def tile_moe_seb_silu_kernel(
         scatter_dc("vector", 2, 0, half, first_high[:, 0, 0:half])
         scatter_dc("vector", 3, 0, C, first_high[:, 1, :])
         scatter_dc("scalar", 2, half, C, first_high[:, 0, half:C])
-        factor(1)
+        silu_of(1, silu_low[:, 1:2, :])
+        one_less_silu(0, 2, silu_low[:], "w2_s_raw")
+        times_gate1(0, 2)
         rest = {}
         for h in range(2):
             for e in range(1, E):
@@ -190,8 +199,12 @@ def tile_moe_seb_silu_kernel(
         w1_s = tile([P, E, W], U8, "w1_s", "dy_s")
         nc.sync.dma_start(w1_w[:], w1t_words[:, 0].rearrange("e p k d -> p e (k d)").bitcast(I32))
         load_scale_rows(w1_s, w1t_scales)
-        factor(2, "gated_first0")
-        factor(3, "gated_first1")
+        for t in range(2, PACK):
+            silu = tile([P, 1, T], F32, f"silu{t}", f"gated_first{t - 2}")
+            silu_of(t, silu[:])
+            one_less_silu(t, t + 1, silu[:], "w2_s_raw" if t == 2 else "gated_first0")
+        for t in range(2, PACK):
+            times_gate1(t, t + 1)
         for e in range(1, E):
             for t in range(PACK):
                 scatter_dc(["scalar", "vector"][t // 2], t, e * C, (e + 1) * C, rest[e, t // 2][:, t % 2, :])

@@ -166,8 +166,8 @@ def tile_moe_seb_silu_kernel(
         gather_words(0, 1)
         gather_scales(0, 1)
         permute_words(0, 1)
-        permute_scales(0, 1, 0, 2)
-        permute_scales(0, 1, 2, PACK)
+        for t0, t1 in ((0, 1), (2, PACK), (1, 2)):
+            permute_scales(0, 1, t0, t1)
         permute_scales(1, E, 0, PACK)
         silu_low = tile([P, 2, T], F32, "silu_low")
         silu_of(0, silu_low[:, 0:1, :])
@@ -225,12 +225,13 @@ def tile_moe_seb_silu_kernel(
             )
 
         def gather_dc(e, parts, tag=None):
-            picked[e] = tile([P, PACK, C], F32, f"picked{e}", tag)
+            for s0, s1 in parts:
+                picked[e, s0] = tile([P, PACK, s1 - s0], F32, f"picked{e}_{s0}", tag)
             for t in range(PACK):
                 for s0, s1 in parts:
                     slots = slice(e * C + s0, e * C + s1)
                     nc.vector.tensor_tensor(
-                        picked[e][:, t, s0:s1],
+                        picked[e, s0][:, t, :],
                         dc[t][:].indirect(entries(list1, slots.start, slots.stop)),
                         times_g[:, t, slots],
                         MULT,
@@ -240,7 +241,7 @@ def tile_moe_seb_silu_kernel(
             rounded[e, s0] = tile([P, s1 - s0, PACK], BF16, f"da_bf{e}_{s0}")
             nc.vector.tensor_tensor(
                 rounded[e, s0][:].rearrange("p (c i) t -> p c t i", i=4),
-                picked[e][:, :, s0:s1].rearrange("p t (c i) -> p c t i", i=4),
+                picked[e, s0][:].rearrange("p t (c i) -> p c t i", i=4),
                 sig[:, (e * C + s0) // 4 : (e * C + s1) // 4],
                 MULT,
             )
@@ -288,7 +289,7 @@ def tile_moe_seb_silu_kernel(
         first_layer([(0, 0), (0, 1)], 0, half, nc.scalar.copy)
         for k in (2, 3, 0, 1):
             scatter_out("scalar", 0, k, 0, half)
-        gather_dc(1, [(0, C)], "picked0")
+        gather_dc(1, [(0, C)], "picked0_0")
         quantise(0, half, C)
         first_layer([(0, k) for k in (2, 3, 0, 1)], half, C, nc.scalar.copy)
         for k in (2, 3, 0, 1):

@@ -21,6 +21,7 @@ E = 3
 C = 256
 W = 512
 PER_COLUMN = 16
+RUN = 8
 FLOPS = 2 * 2 * W * W * T
 
 
@@ -209,7 +210,7 @@ def tile_moe_seb_silu_kernel(
             for t in range(PACK):
                 scatter_dc(["scalar", "vector"][t // 2], t, e * C, (e + 1) * C, rest[e, t // 2][:, t % 2, :])
 
-        sig = tile([P, T // 4, PACK, 4], F32, "sig", "gated1_0")
+        sig = tile([P, T // RUN, PACK, RUN], F32, "sig", "gated1_0")
         picked = {}
         rounded = {}
         dx = {}
@@ -219,8 +220,8 @@ def tile_moe_seb_silu_kernel(
 
         def sigmoid_of(planes, t0, t1, s0, s1):
             nc.scalar.activation(
-                sig[:, s0 // 4 : s1 // 4, t0:t1, :],
-                planes[:, :, s0:s1].rearrange("p t (c i) -> p c t i", i=4),
+                sig[:, s0 // RUN : s1 // RUN, t0:t1, :],
+                planes[:, :, s0:s1].rearrange("p t (c i) -> p c t i", i=RUN),
                 ACT.Sigmoid,
             )
 
@@ -240,9 +241,9 @@ def tile_moe_seb_silu_kernel(
         def round_da(e, s0, s1):
             rounded[e, s0] = tile([P, s1 - s0, PACK], BF16, f"da_bf{e}_{s0}")
             nc.vector.tensor_tensor(
-                rounded[e, s0][:].rearrange("p (c i) t -> p c t i", i=4),
-                picked[e, s0][:].rearrange("p t (c i) -> p c t i", i=4),
-                sig[:, (e * C + s0) // 4 : (e * C + s1) // 4],
+                rounded[e, s0][:].rearrange("p (c i) t -> p c t i", i=RUN),
+                picked[e, s0][:].rearrange("p t (c i) -> p c t i", i=RUN),
+                sig[:, (e * C + s0) // RUN : (e * C + s1) // RUN],
                 MULT,
             )
 

@@ -22,6 +22,7 @@ C = 256
 W = 512
 PER_COLUMN = 16
 RUN = 8
+FAR = (16 * 1024, 88 * 1024)
 FLOPS = 2 * 2 * W * W * T
 
 
@@ -32,6 +33,7 @@ def tile_moe_seb_silu_kernel(
     with ExitStack() as ctx:
         keep = ctx.enter_context(tc.tile_pool(name="keep", bufs=1))
         late = ctx.enter_context(tc.tile_pool(name="late", bufs=1))
+        far = ctx.enter_context(tc.tile_pool(name="far", bufs=1))
         psum = ctx.enter_context(tc.psum_pool(name="psum", bufs=8))
 
         def tile(shape, dtype, name, tag=None):
@@ -42,6 +44,11 @@ def tile_moe_seb_silu_kernel(
 
         list1 = keep.tile([P, T // PER_COLUMN], U16, name="list1")
         list2 = keep.tile([P, T // PER_COLUMN], U16, name="list2")
+        dc = {t: tile([P, T], F32, f"dc{t}") for t in (2, 3)}
+        out_sb = {k: tile([P, T], F32, f"out_sb{k}") for k in (2, 3)}
+        for n in range(2):
+            dc[n] = far.tile([P, T], F32, name=f"dc{n}", offset=FAR[0] + 4 * T * n)
+            out_sb[n] = far.tile([P, T], F32, name=f"out_sb{n}", offset=FAR[1] + 4 * T * n)
         dy_w = tile([P, T], I32, "dy_w")
         dy_s = tile([P, T], U8, "dy_s")
         w2_w_raw = tile([P, E, 2 * W], U8, "w2_w_raw")
@@ -118,7 +125,6 @@ def tile_moe_seb_silu_kernel(
             for e in range(e0, e1):
                 slot_s[e] = scales[:, (e - e0) * C : (e - e0 + 1) * C]
 
-        dc = [tile([P, T], F32, f"dc{t}") for t in range(PACK)]
 
         def second_layer(e, t0, t1, into):
             bank = psum.tile([P, 2, C], F32, name="bank", tag="bank")
@@ -216,7 +222,6 @@ def tile_moe_seb_silu_kernel(
         dx = {}
         da_w = [tile([P, C], U32, f"da_w{e}") for e in range(E)]
         da_s = [tile([P, C], U8, f"da_s{e}") for e in range(E)]
-        out_sb = [tile([P, T], F32, f"out_sb{k}") for k in range(PACK)]
 
         def sigmoid_of(planes, t0, t1, s0, s1):
             nc.scalar.activation(

from contextlib import ExitStack

import concourse.mybir as mybir

F32 = mybir.dt.float32
BF16 = mybir.dt.bfloat16
I32 = mybir.dt.int32
U32 = mybir.dt.uint32
U16 = mybir.dt.uint16
U8 = mybir.dt.uint8
FP8X4 = mybir.dt.float8_e4m3fn_x4
FP4X4 = mybir.dt.float4_e2m1fn_x4
ACT = mybir.ActivationFunctionType
MULT = mybir.AluOpType.mult
ADD = mybir.AluOpType.add

P = 128
PACK = 4
T = 768
E = 3
C = 256
W = 512
PER_COLUMN = 16
RUN = 8
FAR = (16 * 1024, 88 * 1024)
FLOPS = 2 * 2 * W * W * T


def tile_moe_seb_silu_kernel(
    tc, dy_words, dy_scales, w2t_words, w2t_scales, w1t_words, w1t_scales, a, gate1, gate2, offs, offs2, out
):
    nc = tc.nc
    with ExitStack() as ctx:
        keep = ctx.enter_context(tc.tile_pool(name="keep", bufs=1))
        late = ctx.enter_context(tc.tile_pool(name="late", bufs=1))
        far = ctx.enter_context(tc.tile_pool(name="far", bufs=1))
        psum = ctx.enter_context(tc.psum_pool(name="psum", bufs=8))

        def tile(shape, dtype, name, tag=None):
            return keep.tile(shape, dtype, name=name, tag=tag or name, align_bytes=64)

        def entries(listed, s0, s1):
            return listed[:, s0 // PER_COLUMN : s1 // PER_COLUMN]

        list1 = keep.tile([P, T // PER_COLUMN], U16, name="list1")
        list2 = keep.tile([P, T // PER_COLUMN], U16, name="list2")
        dc = {t: tile([P, T], F32, f"dc{t}") for t in (2, 3)}
        out_sb = {k: tile([P, T], F32, f"out_sb{k}") for k in (2, 3)}
        for n in range(2):
            dc[n] = far.tile([P, T], F32, name=f"dc{n}", offset=FAR[0] + 4 * T * n)
            out_sb[n] = far.tile([P, T], F32, name=f"out_sb{n}", offset=FAR[1] + 4 * T * n)
        dy_w = tile([P, T], I32, "dy_w")
        dy_s = tile([P, T], U8, "dy_s")
        w2_w_raw = tile([P, E, 2 * W], U8, "w2_w_raw")
        a_first = tile([P, 1, T], F32, "a_first")
        w2_s_raw = tile([P, E, W], U8, "w2_s_raw")
        zero = late.tile([P, (PACK + 1) * T], I32, name="zero", offset=0)
        a_planes = a.rearrange("(p t) w -> p t w", t=PACK)

        def load_scale_rows(into, scales):
            for quad in range(4):
                nc.sync.dma_start(
                    into[32 * quad : 32 * quad + 4].bitcast(I32),
                    scales[:, 0, 4 * quad : 4 * quad + 4, :].rearrange("e r w -> r e w").bitcast(I32),
                )

        def load_scale_rows_repeated(into, rows):
            words = rows.shape[1] // 4
            for quad in range(4):
                nc.sync.dma_start(
                    into[32 * quad : 32 * quad + 32].bitcast(I32),
                    rows[4 * quad : 4 * quad + 4, :].bitcast(I32).unsqueeze(0).to_broadcast([8, 4, words]),
                )

        nc.gpsimd.memset(zero[:, 0:1], 0)
        nc.vector.tensor_copy(
            w2_s_raw[:].rearrange("p e w -> p (e w)").bitcast(I32), zero[:, 0:1].to_broadcast([P, E * W // 4])
        )
        nc.scalar.dma_start(dy_w[:], dy_words[0].rearrange("p t d -> p (t d)").bitcast(I32))
        nc.sync.dma_start(list2[:], offs2)
        load_scale_rows_repeated(dy_s, dy_scales[0])
        nc.sync.dma_start(a_first[:], a_planes[:, 0:1, :])
        nc.sync.dma_start(w2_w_raw[:].bitcast(I32), w2t_words[:, 0].rearrange("e p w -> p e w").bitcast(I32))
        nc.sync.dma_start(list1[:], offs)
        load_scale_rows(w2_s_raw, w2t_scales)
        q_sb = late.tile([P, T], F32, name="q_sb", offset=0)
        g_sb = late.tile([P, T], F32, name="g_sb", offset=4 * T)
        a_rest = late.tile([P, PACK - 1, T], F32, name="a_rest", offset=8 * T)
        nc.sync.dma_start(a_rest[:, 0, :], a_planes[:, 1, :])
        nc.sync.dma_start(q_sb[:, 0:C], gate2[:, 0:C])
        nc.sync.dma_start(g_sb[:], gate1)
        for t in range(2, PACK):
            nc.sync.dma_start(a_rest[:, t - 1, :], a_planes[:, t, :])
        nc.sync.dma_start(q_sb[:, C:T], gate2[:, C:T])
        a_sb = [a_first[:, 0, :]] + [a_rest[:, t - 1, :] for t in range(1, PACK)]

        w2_w = {}
        w2_s = tile([P, E, PACK, P], U8, "w2_s")

        def permute_scales(e0, e1, t0, t1):
            planes = w2_s_raw[:].rearrange("p e (m t) -> p e t m", t=PACK)
            nc.gpsimd.tensor_copy(w2_s[:, e0:e1, t0:t1, :], planes[:, e0:e1, t0:t1, :])

        def permute_words(e0, e1):
            planes = tile([P, e1 - e0, PACK, P], U16, f"w2_w{e0}")
            nc.scalar.copy(
                planes[:].rearrange("p e t (c i) -> p e c t i", i=4),
                w2_w_raw[:, e0:e1].bitcast(U16).rearrange("p e (c i t) -> p e c t i", i=4, t=PACK),
            )
            for e in range(e0, e1):
                w2_w[e] = planes[:, e - e0]

        slot_w = {}
        slot_s = {}

        def gather_words(e0, e1):
            words = tile([P, (e1 - e0) * C], U32, f"slot_w{e0}")
            nc.vector.tensor_copy(words[:], dy_w[:].bitcast(U32).indirect(entries(list2, e0 * C, e1 * C)))
            for e in range(e0, e1):
                slot_w[e] = words[:, (e - e0) * C : (e - e0 + 1) * C]

        def gather_scales(e0, e1):
            scales = tile([P, (e1 - e0) * C], U8, f"slot_s{e0}")
            nc.vector.tensor_copy(scales[:], dy_s[:].indirect(entries(list2, e0 * C, e1 * C)))
            for e in range(e0, e1):
                slot_s[e] = scales[:, (e - e0) * C : (e - e0 + 1) * C]


        def second_layer(e, t0, t1, into):
            bank = psum.tile([P, 2, C], F32, name="bank", tag="bank")
            for t in range(t0, t1):
                nc.tensor.matmul_mx(
                    out=bank[:, t - t0, :],
                    lhsT=w2_w[e][:, t, :].bitcast(U8).bitcast(FP4X4),
                    lhsT_scale=w2_s[:, e, t, :],
                    rhs=slot_w[e].bitcast(FP8X4),
                    rhs_scale=slot_s[e],
                    start=True,
                    stop=True,
                )
            nc.vector.tensor_tensor(
                into,
                bank[:, 0 : t1 - t0, :],
                q_sb[:, e * C : (e + 1) * C].unsqueeze(1).to_broadcast([P, t1 - t0, C]),
                MULT,
            )

        def scatter(engine, window, values):
            if engine == "vector":
                nc.vector.tensor_copy(window, values)
            else:
                nc.scalar.activation(window, values, ACT.Copy)

        def scatter_dc(engine, t, s0, s1, values):
            scatter(engine, dc[t][:].indirect(entries(list2, s0, s1)), values)

        times_g = tile([P, PACK, T], F32, "times_g")

        def silu_of(t, into):
            nc.scalar.activation(into[:, 0, :], a_sb[t], ACT.Silu, scale=-1.0)

        one_less = {}

        def one_less_silu(t0, t1, silu, tag):
            one_less[t0] = tile([P, t1 - t0, T], F32, f"one_less{t0}", tag)
            nc.gpsimd.tensor_scalar(one_less[t0][:], silu, -1.0, 1.0, MULT, ADD)

        def times_gate1(t0, t1):
            nc.gpsimd.tensor_tensor(
                times_g[:, t0:t1, :], one_less[t0][:], g_sb[:].unsqueeze(1).to_broadcast([P, t1 - t0, T]), MULT
            )

        gather_words(0, 1)
        gather_scales(0, 1)
        permute_words(0, 1)
        for t0, t1 in ((0, 1), (2, PACK), (1, 2)):
            permute_scales(0, 1, t0, t1)
        permute_scales(1, E, 0, PACK)
        silu_low = tile([P, 2, T], F32, "silu_low")
        silu_of(0, silu_low[:, 0:1, :])
        gather_words(1, E)
        gather_scales(1, 2)
        gather_scales(2, E)
        permute_words(1, E)
        first = [tile([P, 1, C], F32, f"gated_first{t}") for t in range(2)]
        first_high = tile([P, 2, C], F32, "gated_first_high")
        second_layer(0, 0, 1, first[0][:])
        second_layer(0, 2, PACK, first_high[:])
        second_layer(0, 1, 2, first[1][:])
        half = C // 2
        halves = [(0, half), (half, C)]
        for t in range(2):
            scatter_dc("scalar", t, 0, C, first[t][:, 0, :])
        scatter_dc("vector", 2, 0, half, first_high[:, 0, 0:half])
        scatter_dc("vector", 3, 0, C, first_high[:, 1, :])
        scatter_dc("scalar", 2, half, C, first_high[:, 0, half:C])
        silu_of(1, silu_low[:, 1:2, :])
        one_less_silu(0, 2, silu_low[:], "w2_s_raw")
        times_gate1(0, 2)
        rest = {}
        for h in range(2):
            for e in range(1, E):
                rest[e, h] = tile([P, 2, C], F32, f"gated{e}_{h}")
                second_layer(e, 2 * h, 2 * h + 2, rest[e, h][:])
        w1_w = tile([P, E, W], I32, "w1_w", "dy_w")
        w1_s = tile([P, E, W], U8, "w1_s", "dy_s")
        nc.sync.dma_start(w1_w[:], w1t_words[:, 0].rearrange("e p k d -> p e (k d)").bitcast(I32))
        load_scale_rows(w1_s, w1t_scales)
        for t in range(2, PACK):
            silu = tile([P, 1, T], F32, f"silu{t}", f"gated_first{t - 2}")
            silu_of(t, silu[:])
            one_less_silu(t, t + 1, silu[:], "w2_s_raw" if t == 2 else "gated_first0")
        for t in range(2, PACK):
            times_gate1(t, t + 1)
        for e in range(1, E):
            for t in range(PACK):
                scatter_dc(["scalar", "vector"][t // 2], t, e * C, (e + 1) * C, rest[e, t // 2][:, t % 2, :])

        sig = tile([P, T // RUN, PACK, RUN], F32, "sig", "gated1_0")
        picked = {}
        rounded = {}
        dx = {}
        da_w = [tile([P, C], U32, f"da_w{e}") for e in range(E)]
        da_s = [tile([P, C], U8, f"da_s{e}") for e in range(E)]

        def sigmoid_of(planes, t0, t1, s0, s1):
            nc.scalar.activation(
                sig[:, s0 // RUN : s1 // RUN, t0:t1, :],
                planes[:, :, s0:s1].rearrange("p t (c i) -> p c t i", i=RUN),
                ACT.Sigmoid,
            )

        def gather_dc(e, parts, tag=None):
            for s0, s1 in parts:
                picked[e, s0] = tile([P, PACK, s1 - s0], F32, f"picked{e}_{s0}", tag)
            for t in range(PACK):
                for s0, s1 in parts:
                    slots = slice(e * C + s0, e * C + s1)
                    nc.vector.tensor_tensor(
                        picked[e, s0][:, t, :],
                        dc[t][:].indirect(entries(list1, slots.start, slots.stop)),
                        times_g[:, t, slots],
                        MULT,
                    )

        def round_da(e, s0, s1):
            rounded[e, s0] = tile([P, s1 - s0, PACK], BF16, f"da_bf{e}_{s0}")
            nc.vector.tensor_tensor(
                rounded[e, s0][:].rearrange("p (c i) t -> p c t i", i=RUN),
                picked[e, s0][:].rearrange("p t (c i) -> p c t i", i=RUN),
                sig[:, (e * C + s0) // RUN : (e * C + s1) // RUN],
                MULT,
            )

        def quantise(e, s0, s1):
            nc.vector.quantize_mx(
                out=da_w[e][:, s0:s1].bitcast(FP8X4),
                scales=da_s[e][:, s0:s1],
                in_=rounded[e, s0][:].rearrange("p n t -> p (n t)"),
            )

        def first_layer(blocks, s0, s1, copy):
            bank = psum.tile([P, len(blocks), s1 - s0], F32, name="bank", tag="bank")
            sums = tile([P, len(blocks), s1 - s0], F32, f"dx{blocks[0][0]}_{blocks[0][1]}_{s0}")
            for n, (e, k) in enumerate(blocks):
                rows = slice(k * P, (k + 1) * P)
                nc.tensor.matmul_mx(
                    out=bank[:, n, :],
                    lhsT=w1_w[:, e, rows].bitcast(FP8X4),
                    lhsT_scale=w1_s[:, e, rows],
                    rhs=da_w[e][:, s0:s1].bitcast(FP8X4),
                    rhs_scale=da_s[e][:, s0:s1],
                    start=True,
                    stop=True,
                )
                dx[e, k, s0] = sums[:, n, :]
            copy(sums[:], bank[:])

        def scatter_out(engine, e, k, s0=0, s1=C):
            scatter(engine, out_sb[k][:].indirect(entries(list1, e * C + s0, e * C + s1)), dx[e, k, s0])

        def store(queue, k):
            queue.dma_start(out[k * P : (k + 1) * P, :], out_sb[k][:])

        sigmoid_of(a_first, 0, 1, 0, C)
        sigmoid_of(a_rest, 1, PACK, 0, half)
        sigmoid_of(a_rest, 1, PACK, half, C)
        sigmoid_of(a_first, 0, 1, C, T)
        sigmoid_of(a_rest, 1, PACK, C, T)
        gather_dc(0, halves)
        for s0, s1 in halves:
            round_da(0, s0, s1)
        quantise(0, 0, half)
        first_layer([(0, 2), (0, 3)], 0, half, nc.scalar.copy)
        first_layer([(0, 0), (0, 1)], 0, half, nc.scalar.copy)
        for k in (2, 3, 0, 1):
            scatter_out("scalar", 0, k, 0, half)
        gather_dc(1, [(0, C)], "picked0_0")
        quantise(0, half, C)
        first_layer([(0, k) for k in (2, 3, 0, 1)], half, C, nc.scalar.copy)
        for k in (2, 3, 0, 1):
            scatter_out("scalar", 0, k, half, C)
        round_da(1, 0, C)
        gather_dc(2, [(0, C)], f"da_bf0_{half}")
        quantise(1, 0, C)
        round_da(2, 0, C)
        first_layer([(1, 2)], 0, C, nc.vector.tensor_copy)
        for k in range(2):
            first_layer([(1, k)], 0, C, nc.scalar.copy)
        quantise(2, 0, C)
        scatter_out("vector", 1, 2)
        first_layer([(1, 3), (2, 2)], 0, C, nc.vector.tensor_copy)
        first_layer([(2, 3)], 0, C, nc.vector.tensor_copy)
        for k in range(2):
            scatter_out("scalar", 1, k)
        for k in range(2):
            first_layer([(2, k)], 0, C, nc.scalar.copy)
        scatter_out("vector", 1, 3)
        for k in range(PACK):
            scatter_out(["scalar", "vector"][k // 2], 2, k)
            store([nc.scalar, nc.sync][k // 2], k)
